import numpy as np
import ml_dtypes


def mxq(x, axis, fmt="e4m3"):
    dtype, down = {"e4m3": (ml_dtypes.float8_e4m3fn, 7), "e5m2": (ml_dtypes.float8_e5m2, 14)}[fmt]
    v = np.moveaxis(np.asarray(x, np.float32).astype(ml_dtypes.bfloat16).astype(np.float64), axis, -1)
    blocks = v.reshape(v.shape[:-1] + (-1, 32))
    amax = np.abs(blocks).max(-1, keepdims=True)
    byte = np.maximum(np.where(amax > 0, np.frexp(amax)[1] - 1 + 127, 0) - down, 1)
    scale = np.exp2(byte - 127.0)
    codes = (blocks / scale).astype(np.float32).astype(dtype).astype(np.float64)
    return np.moveaxis((codes * scale).reshape(v.shape), -1, axis)


WIDE = False


def mx_kscale(k):
    if not WIDE:
        return np.ones(k)
    levels = np.array([24, -24, 12, -12, 0])
    if k % 512:
        return np.exp2(np.random.permutation(np.resize(levels, k // 32))).repeat(32)
    a = np.empty((k // 512, 16))
    for p in range(k // 512):
        a[p, :8] = np.random.permutation(np.resize(levels, 8))
        for g in range(8):
            far = levels[np.abs(levels - a[p, g]) >= 10]
            a[p, g + 8] = far[np.random.randint(len(far))]
    return np.exp2(a.ravel()).repeat(32)


def f64(x):
    return np.asarray(x).astype(np.float64)


def striped(idx):
    return np.tile(idx.reshape(-1, 16).T, (8, 1)).astype(np.uint16)


def unstriped(offs):
    return offs[:16].T.reshape(-1).astype(np.int64)


E2M1 = np.array([0.0, 0.5, 1.0, 1.5, 2.0, 3.0, 4.0, 6.0, -0.0, -0.5, -1.0, -1.5, -2.0, -3.0, -4.0, -6.0])


def pack_weight(w, fmt):
    k, n = w.shape
    w = f64(np.asarray(w, np.float32).astype(ml_dtypes.bfloat16)).reshape(k // 32, 32, n)
    amax = np.abs(w).max(1)
    if fmt == "e4m3":
        byte = np.frexp(amax)[1] - 1 + 127 - 7
    else:
        mant, ex = np.frexp(amax / 6.0)
        byte = np.where(mant > 0.5, ex, ex - 1) + 127
    byte = np.clip(np.where(amax > 0, byte, 1), 1, 254)
    scaled = (w * np.exp2(127.0 - byte)[:, None, :]).reshape(k, n).astype(np.float32)
    by_word = np.ascontiguousarray(scaled.reshape(k // 512, 128, 4, n).transpose(0, 1, 3, 2))
    if fmt == "e4m3":
        words = by_word.astype(ml_dtypes.float8_e4m3fn).view(np.uint8)
    else:
        c = by_word.astype(ml_dtypes.float4_e2m1fn).view(np.uint8) & 0xF
        words = (c[..., 0::2] | (c[..., 1::2] << 4)).reshape(k // 512, 128, 2 * n)
    return np.ascontiguousarray(words), np.ascontiguousarray(byte.astype(np.uint8).reshape(k // 512, 16, n))


def unpack_weight(words, scales, fmt):
    g, _, n = scales.shape
    words = np.ascontiguousarray(words).reshape(g, 128, n, -1)
    if fmt == "e4m3":
        vals = words.view(ml_dtypes.float8_e4m3fn).astype(np.float64)
    else:
        nib = np.empty((g, 128, n, 4), np.uint8)
        nib[..., 0::2] = words & 0xF
        nib[..., 1::2] = words >> 4
        vals = E2M1[nib]
    vals = vals * np.repeat(np.exp2(scales.astype(np.float64) - 127.0), 8, axis=1)[..., None]
    return vals.transpose(0, 1, 3, 2).reshape(g * 512, n)


def planes(y):
    n, m = y.shape
    v = y.astype(np.float32).astype(ml_dtypes.bfloat16).astype(np.float64).reshape(n // 32, 32, m)
    top = np.abs(v).max(1)
    byte = np.clip(np.where(top > 0, np.frexp(top)[1] - 1 + 127 - 7, 1), 1, 254)
    codes = (v * np.exp2(127.0 - byte)[:, None, :]).reshape(n, m).astype(np.float32).astype(ml_dtypes.float8_e4m3fn).view(np.uint8)
    words = codes.reshape(n // 512, 128, 4, m).transpose(0, 1, 3, 2)
    return np.ascontiguousarray(words), np.ascontiguousarray(byte.astype(np.uint8).reshape(n // 512, 16, m))


K, R, N, T, J = 512, 1024, 512, 2048, 1024


def setup_inputs():
    n = np.random.standard_normal
    s = mx_kscale(K)[:, None]
    u = mx_kscale(R)[:, None]
    wd = n((R, N)) / np.sqrt(R) / u
    wd4 = pack_weight(wd, "e2m1")
    wdrest = wd - unpack_weight(*wd4, "e2m1")
    p_tab = pack_weight(n((K, T)) * s, "e4m3")
    p_wu = pack_weight(n((K, R)) / np.sqrt(K) / s, "e4m3")
    p_wd8 = pack_weight(wdrest, "e4m3")
    return {
        "tab_words": p_tab[0],
        "tab_scales": p_tab[1],
        "wu_words": p_wu[0],
        "wu_scales": p_wu[1],
        "sm": (np.random.uniform(0.5, 2.0, R) * u[:, 0]).astype(np.float32),
        "wd4_words": wd4[0],
        "wd4_scales": wd4[1],
        "wd8_words": p_wd8[0],
        "wd8_scales": p_wd8[1],
        "wgo": np.tile(np.random.uniform(0.5, 2.0, J), (128, 1)).astype(np.float32),
        "offs": striped(np.random.permutation(T)[:J]),
    }


def reference(tab_words, tab_scales, wu_words, wu_scales, sm, wd4_words, wd4_scales, wd8_words, wd8_scales, wgo, offs):
    idx = unstriped(offs)
    tab_ = unpack_weight(tab_words, tab_scales, "e4m3")[:, idx]
    wu_ = unpack_weight(wu_words, wu_scales, "e4m3")
    a = wu_.T @ tab_
    h = f64(sm)[:, None] * (np.maximum(a, 0.0)) ** 2
    h_ = mxq(h, 0, "e4m3")
    wd4_ = unpack_weight(wd4_words, wd4_scales, "e2m1")
    wd8_ = unpack_weight(wd8_words, wd8_scales, "e4m3")
    y = wd4_.T @ h_ + wd8_.T @ h_
    out = np.zeros((N, T))
    out[:, idx] = f64(wgo)[0] * (y)
    return (out,) + planes(out)

@@ -1,0 +1,245 @@
+from contextlib import ExitStack
+
+import concourse.mybir as mybir
+
+K, R, N, T, J = 512, 1024, 512, 2048, 1024
+FLOPS = 2 * K * R * J + 2 * 2 * R * N * J
+
+F32 = mybir.dt.float32
+BF16 = mybir.dt.bfloat16
+I32 = mybir.dt.int32
+U32 = mybir.dt.uint32
+U16 = mybir.dt.uint16
+U8 = mybir.dt.uint8
+FP8X4 = mybir.dt.float8_e4m3fn_x4
+FP4X4 = mybir.dt.float4_e2m1fn_x4
+ALU = mybir.AluOpType
+ACT = mybir.ActivationFunctionType
+
+P = 128
+PACK = 4
+PASS = P * PACK
+HB = R // PASS
+CHUNKS = (256, 256, 512)
+TAIL = (256, 512, 512, 512, 256)
+TINY = 2.0 ** -100
+
+
+def tile_list_modp_relu2_res_noneP_kernel(
+    tc, tab_words, tab_scales, wu_words, wu_scales, sm, wd4_words, wd4_scales, wd8_words, wd8_scales, wgo, offs,
+    out_0, out_1, out_2,
+):
+    nc = tc.nc
+    with ExitStack() as ctx:
+        keep = ctx.enter_context(tc.tile_pool(name="keep", bufs=1))
+        ring = ctx.enter_context(tc.tile_pool(name="ring", bufs=2))
+        psum = ctx.enter_context(tc.psum_pool(name="psum", bufs=4))
+
+        offsets = keep.tile([P, J // 16], U16, name="offsets")
+        tab_w = keep.tile([P, T], I32, name="tab_w", align_bytes=64)
+        tab_s = keep.tile([P, T], U8, name="tab_s", align_bytes=64)
+        wu_raw = keep.tile([P, R], I32, name="wu_raw", align_bytes=64)
+        wus_raw = keep.tile([P, PASS], U8, name="wus_raw", align_bytes=64)
+        wd8_raw = keep.tile([P, HB * N], I32, name="wd8_raw", align_bytes=64)
+        wd4_raw = keep.tile([P, HB * N * 2], U8, name="wd4_raw", align_bytes=64)
+        wds_raw = keep.tile([P, HB * N], U8, name="wds_raw", align_bytes=64)
+        sm_t = keep.tile([P, HB * PACK], F32, name="sm_t")
+        wgo_t = keep.tile([P, J], F32, name="wgo_t")
+
+        nc.vector.memset(wus_raw[:].bitcast(I32), 0)
+        nc.vector.memset(tab_s[:].bitcast(I32), 0)
+        nc.vector.memset(wds_raw[:].bitcast(I32), 0)
+
+        nc.sync.dma_start(offsets[:], offs)
+        nc.sync.dma_start(sm_t[:].rearrange("p (b t) -> p b t", t=PACK), sm.rearrange("(b p t) -> p b t", p=P, t=PACK))
+        nc.sync.dma_start(wu_raw[:], wu_words[0].rearrange("p r i -> p (r i)").bitcast(I32))
+        nc.sync.dma_start(tab_w[:], tab_words[0].rearrange("p t i -> p (t i)").bitcast(I32))
+        for q in range(4):
+            nc.sync.dma_start(tab_s[32 * q : 32 * q + 4, :].bitcast(I32), tab_scales[0, 4 * q : 4 * q + 4, :].bitcast(I32))
+        for q in range(4):
+            nc.sync.dma_start(
+                wus_raw[32 * q : 32 * q + 4 * HB, :].bitcast(I32),
+                wu_scales[0, 4 * q : 4 * q + 4, :].bitcast(I32).rearrange("r (b n) -> b r n", b=HB),
+            )
+        nc.sync.dma_start(
+            wd8_raw[:].rearrange("p (a n) -> p a n", a=HB), wd8_words.rearrange("a p n i -> p a (n i)").bitcast(I32)
+        )
+        nc.sync.dma_start(
+            wd4_raw[:].bitcast(I32).rearrange("p (a n) -> p a n", a=HB), wd4_words.rearrange("a p n -> p a n").bitcast(I32)
+        )
+        for first, planes in ((0, wd4_scales), (4, wd8_scales)):
+            for q in range(4):
+                nc.sync.dma_start(
+                    wds_raw[32 * q + first : 32 * q + first + 4, :].bitcast(I32).rearrange("r (a n) -> r a n", a=HB),
+                    planes[:, 4 * q : 4 * q + 4, :].bitcast(I32).rearrange("a r n -> r a n"),
+                )
+        nc.sync.dma_start(wgo_t[:], wgo)
+
+        windows = [keep.tile([P, T], F32, name="window%d" % t) for t in range(PACK)]
+        for t in range(PACK):
+            nc.vector.memset(windows[t][:], 0.0)
+
+        mag = keep.tile([P, HB * PACK], F32, name="mag")
+        magc = keep.tile([P, HB * PACK], F32, name="magc")
+        root0 = keep.tile([P, HB * PACK], F32, name="root0")
+        rinv = keep.tile([P, HB * PACK], F32, name="rinv")
+        quot = keep.tile([P, HB * PACK], F32, name="quot")
+        root2 = keep.tile([P, HB * PACK], F32, name="root2")
+        nc.vector.scalar_tensor_tensor(mag[:], sm_t[:], -1.0, sm_t[:], ALU.mult, ALU.max)
+        nc.vector.tensor_scalar(magc[:], mag[:], TINY, None, ALU.max)
+        nc.scalar.activation(root0[:], magc[:], ACT.Sqrt)
+        nc.vector.reciprocal(rinv[:], root0[:])
+        nc.vector.tensor_tensor(quot[:], magc[:], rinv[:], ALU.mult)
+        nc.vector.tensor_tensor(root2[:], quot[:], root0[:], ALU.add)
+        wide = max(CHUNKS)
+        signs = []
+        for b in range(HB):
+            sign_b = keep.tile([P, wide, PACK], BF16, name="sign%d" % b, align_bytes=64)
+            nc.scalar.activation(
+                sign_b[:], sm_t[:, b * PACK : (b + 1) * PACK].unsqueeze(1).to_broadcast([P, wide, PACK]), ACT.Sign
+            )
+            signs.append(sign_b)
+
+        wu_w = keep.tile([P, R], I32, name="wu_w", align_bytes=64)
+        wu_s = keep.tile([P, PASS], U8, name="wu_s", align_bytes=64)
+        nc.vector.tensor_copy(
+            wu_w[:].rearrange("p (b t m) -> p b m t", b=HB, t=PACK), wu_raw[:].rearrange("p (b m t) -> p b m t", b=HB, t=PACK)
+        )
+        nc.vector.tensor_copy(
+            wu_s[:].rearrange("p (t m) -> p m t", t=PACK), wus_raw[:].rearrange("p (m t) -> p m t", t=PACK)
+        )
+
+        starts = [sum(CHUNKS[:c]) for c in range(len(CHUNKS))]
+        picked = []
+        for c, width in enumerate(CHUNKS):
+            cols = offsets[:, starts[c] // 16 : (starts[c] + width) // 16]
+            g_w = keep.tile([P, width], I32, name="g_w%d" % c, align_bytes=64)
+            g_s = keep.tile([P, width], U8, name="g_s%d" % c, align_bytes=64)
+            nc.vector.tensor_copy(g_w[:].bitcast(U32), tab_w[:].bitcast(U32).indirect(cols))
+            nc.vector.tensor_copy(g_s[:], tab_s[:].indirect(cols))
+            picked.append((g_w, g_s))
+
+        wd8_w = keep.tile([P, HB * N], I32, name="wd8_w", align_bytes=64)
+        wd4_w = keep.tile([P, HB * N * 2], U8, name="wd4_w", align_bytes=64)
+        wd_s = keep.tile([P, HB * N], U8, name="wd_s", align_bytes=64)
+        nc.vector.tensor_copy(
+            wd8_w[:].rearrange("p (a t m) -> p a m t", a=HB, t=PACK), wd8_raw[:].rearrange("p (a m t) -> p a m t", a=HB, t=PACK)
+        )
+        nc.vector.tensor_copy(
+            wd4_w[:].rearrange("p (a t m e) -> p a m t e", a=HB, t=PACK, e=2),
+            wd4_raw[:].rearrange("p (a m t e) -> p a m t e", a=HB, t=PACK, e=2),
+        )
+        nc.vector.tensor_copy(
+            wd_s[:].rearrange("p (a t m) -> p a m t", a=HB, t=PACK), wds_raw[:].rearrange("p (a m t) -> p a m t", a=HB, t=PACK)
+        )
+
+        hidden = {}
+
+        def make_hidden(c, b):
+            width = CHUNKS[c]
+            g_w, g_s = picked[c]
+            relu = ring.tile([P, PACK, width], F32, name="relu", tag="relu")
+            for t in range(PACK):
+                acc = psum.tile([P, width], F32, name="acc_a", tag="acc_a")
+                col = b * PASS + t * P
+                nc.tensor.matmul_mx(
+                    out=acc[:],
+                    lhsT=wu_w[:, col : col + P].bitcast(FP8X4),
+                    lhsT_scale=wu_s[4 * b :, t * P : (t + 1) * P],
+                    rhs=g_w[:].bitcast(FP8X4),
+                    rhs_scale=g_s[:],
+                    start=True,
+                    stop=True,
+                )
+                nc.scalar.activation(relu[:, t, :], acc[:], ACT.Relu, scale=root2[:, b * PACK + t : b * PACK + t + 1])
+            square = ring.tile([P, width * PACK], BF16, name="square", tag="square", align_bytes=64)
+            nc.scalar.activation(
+                square[:].rearrange("p (c i t) -> p c t i", i=4, t=PACK),
+                relu[:].rearrange("p t (c i) -> p c t i", i=4),
+                ACT.Square,
+                scale=0.5,
+            )
+            signed = ring.tile([P, width * PACK], BF16, name="signed", tag="signed", align_bytes=64)
+            nc.vector.tensor_tensor(
+                signed[:], square[:], signs[b][:].rearrange("p c t -> p (c t)")[:, : width * PACK], ALU.mult
+            )
+            h_w = keep.tile([P, width], U32, name="h_w%d_%d" % (c, b), align_bytes=64)
+            h_s = keep.tile([P, width], U8, name="h_s%d_%d" % (c, b), align_bytes=64)
+            nc.vector.quantize_mx(out=h_w[:].bitcast(FP8X4), scales=h_s[:], in_=signed[:])
+            hidden[(c, b)] = (h_w, h_s)
+
+        def put_result(c, t):
+            width = CHUNKS[c]
+            acc = psum.tile([P, width], F32, name="acc_y", tag="acc_y")
+            narrow = width if width == 512 else P
+            for b in range(HB):
+                h_w, h_s = hidden[(c, b)]
+                col = b * N + t * P
+                nc.tensor.matmul_mx(
+                    out=acc[:],
+                    lhsT=wd8_w[:, col : col + P].bitcast(FP8X4),
+                    lhsT_scale=wd_s[4:, col : col + P],
+                    rhs=h_w[:].bitcast(FP8X4),
+                    rhs_scale=h_s[:],
+                    start=(b == 0),
+                    stop=False,
+                )
+                for j0 in range(0, width, narrow):
+                    nc.tensor.matmul_mx(
+                        out=acc[:, j0 : j0 + narrow],
+                        lhsT=wd4_w[:, 2 * col : 2 * (col + P)].bitcast(FP4X4),
+                        lhsT_scale=wd_s[:, col : col + P],
+                        rhs=h_w[:, j0 : j0 + narrow].bitcast(FP8X4),
+                        rhs_scale=h_s[:, j0 : j0 + narrow],
+                        start=False,
+                        stop=(b == HB - 1 and j0 + narrow == width),
+                    )
+            y = keep.tile([P, width], F32, name="y%d_%d" % (c, t))
+            nc.scalar.copy(y[:], acc[:])
+            cols = offsets[:, starts[c] // 16 : (starts[c] + width) // 16]
+            nc.vector.tensor_tensor(windows[t][:].indirect(cols), y[:], wgo_t[:, starts[c] : starts[c] + width], ALU.mult)
+
+        make_hidden(0, 0)
+        make_hidden(0, 1)
+        for c in range(len(CHUNKS) - 1):
+            put_result(c, 0)
+            put_result(c, 1)
+            make_hidden(c + 1, 0)
+            put_result(c, 2)
+            make_hidden(c + 1, 1)
+            put_result(c, 3)
+
+        rows = out_0.rearrange("(p t) c -> p t c", t=PACK)
+        edges = [sum(TAIL[:i]) for i in range(len(TAIL))]
+        pairs = [keep.tile([P, 2, w, 2], BF16, name="pairs%d" % i, align_bytes=64) for i, w in enumerate(TAIL)]
+        for t in range(PACK):
+            put_result(len(CHUNKS) - 1, t)
+        for t in range(PACK):
+            nc.sync.dma_start(rows[:, t, :], windows[t][:])
+            for i, w in enumerate(TAIL):
+                nc.scalar.copy(pairs[i][:, t // 2, :, t % 2], windows[t][:, edges[i] : edges[i] + w])
+
+        out_s = keep.tile([P, T], U8, name="out_s", align_bytes=64)
+        words_out = out_1[0].rearrange("p t i -> p (t i)").bitcast(I32)
+        grouped = [keep.tile([P, w * PACK], BF16, name="grouped%d" % i, align_bytes=64) for i, w in enumerate(TAIL)]
+
+        def group(i):
+            nc.vector.tensor_copy(
+                grouped[i][:].bitcast(I32).rearrange("p (c u) -> p c u", u=2),
+                pairs[i][:].rearrange("p u c e -> p u (c e)").bitcast(I32).rearrange("p u c -> p c u"),
+            )
+
+        def finish(i):
+            w = TAIL[i]
+            out_w = keep.tile([P, w], I32, name="out_w%d" % i, align_bytes=64)
+            nc.vector.quantize_mx(out=out_w[:].bitcast(FP8X4), scales=out_s[:, edges[i] : edges[i] + w], in_=grouped[i][:])
+            nc.sync.dma_start(words_out[:, edges[i] : edges[i] + w], out_w[:])
+
+        group(0)
+        for i in range(1, len(TAIL)):
+            group(i)
+            finish(i - 1)
+        finish(len(TAIL) - 1)
+        for q in range(4):
+            queue = nc.sync if q % 2 == 0 else nc.scalar
+            queue.dma_start(out_2[0, 4 * q : 4 * q + 4, :].bitcast(I32), out_s[32 * q : 32 * q + 4, :].bitcast(I32))

@@ -21,8 +21,7 @@ PACK = 4
 PASS = P * PACK
 HB = R // PASS
 CHUNKS = (256, 256, 512)
-TAIL = (256, 512, 512, 512, 256)
-TINY = 2.0 ** -100
+TAIL = ((256, False), (256, False), (512, True), (512, True), (256, True), (256, False))
 
 
 def tile_list_modp_relu2_res_noneP_kernel(
@@ -39,59 +38,39 @@ def tile_list_modp_relu2_res_noneP_kernel(
         tab_w = keep.tile([P, T], I32, name="tab_w", align_bytes=64)
         tab_s = keep.tile([P, T], U8, name="tab_s", align_bytes=64)
         wu_raw = keep.tile([P, R], I32, name="wu_raw", align_bytes=64)
-        wus_raw = keep.tile([P, PASS], U8, name="wus_raw", align_bytes=64)
-        wd8_raw = keep.tile([P, HB * N], I32, name="wd8_raw", align_bytes=64)
-        wd4_raw = keep.tile([P, HB * N * 2], U8, name="wd4_raw", align_bytes=64)
-        wds_raw = keep.tile([P, HB * N], U8, name="wds_raw", align_bytes=64)
+        wus_raw = keep.tile([P, R], U8, name="wus_raw", align_bytes=64)
         sm_t = keep.tile([P, HB * PACK], F32, name="sm_t")
-        wgo_t = keep.tile([P, J], F32, name="wgo_t")
 
-        nc.vector.memset(wus_raw[:].bitcast(I32), 0)
-        nc.vector.memset(tab_s[:].bitcast(I32), 0)
-        nc.vector.memset(wds_raw[:].bitcast(I32), 0)
+        wds_raw = keep.tile([P, HB * N], U8, name="wds_raw", align_bytes=64)
+        nc.gpsimd.memset(tab_s[:].bitcast(I32), 0)
+        nc.gpsimd.memset(wds_raw[:].bitcast(I32), 0)
 
         nc.sync.dma_start(offsets[:], offs)
         nc.sync.dma_start(sm_t[:].rearrange("p (b t) -> p b t", t=PACK), sm.rearrange("(b p t) -> p b t", p=P, t=PACK))
-        nc.sync.dma_start(wu_raw[:], wu_words[0].rearrange("p r i -> p (r i)").bitcast(I32))
-        nc.sync.dma_start(tab_w[:], tab_words[0].rearrange("p t i -> p (t i)").bitcast(I32))
-        for q in range(4):
-            nc.sync.dma_start(tab_s[32 * q : 32 * q + 4, :].bitcast(I32), tab_scales[0, 4 * q : 4 * q + 4, :].bitcast(I32))
         for q in range(4):
             nc.sync.dma_start(
-                wus_raw[32 * q : 32 * q + 4 * HB, :].bitcast(I32),
-                wu_scales[0, 4 * q : 4 * q + 4, :].bitcast(I32).rearrange("r (b n) -> b r n", b=HB),
+                wus_raw[32 * q : 32 * q + 32, :].bitcast(I32),
+                wu_scales[0, 4 * q : 4 * q + 4, :].bitcast(I32).unsqueeze(0).to_broadcast([8, 4, R // 4]),
             )
-        nc.sync.dma_start(
-            wd8_raw[:].rearrange("p (a n) -> p a n", a=HB), wd8_words.rearrange("a p n i -> p a (n i)").bitcast(I32)
-        )
-        nc.sync.dma_start(
-            wd4_raw[:].bitcast(I32).rearrange("p (a n) -> p a n", a=HB), wd4_words.rearrange("a p n -> p a n").bitcast(I32)
-        )
-        for first, planes in ((0, wd4_scales), (4, wd8_scales)):
-            for q in range(4):
-                nc.sync.dma_start(
-                    wds_raw[32 * q + first : 32 * q + first + 4, :].bitcast(I32).rearrange("r (a n) -> r a n", a=HB),
-                    planes[:, 4 * q : 4 * q + 4, :].bitcast(I32).rearrange("a r n -> r a n"),
-                )
-        nc.sync.dma_start(wgo_t[:], wgo)
+        nc.sync.dma_start(tab_w[:], tab_words[0].rearrange("p t i -> p (t i)").bitcast(I32))
+        nc.sync.dma_start(wu_raw[:], wu_words[0].rearrange("p r i -> p (r i)").bitcast(I32))
+        for q in range(4):
+            nc.sync.dma_start(tab_s[32 * q : 32 * q + 4, :].bitcast(I32), tab_scales[0, 4 * q : 4 * q + 4, :].bitcast(I32))
 
         windows = [keep.tile([P, T], F32, name="window%d" % t) for t in range(PACK)]
-        for t in range(PACK):
+        for t in range(2):
             nc.vector.memset(windows[t][:], 0.0)
+        for t in range(2, PACK):
+            for c0 in range(0, T, 512):
+                nc.gpsimd.memset(windows[t][:, c0 : c0 + 512], 0.0)
 
         mag = keep.tile([P, HB * PACK], F32, name="mag")
-        magc = keep.tile([P, HB * PACK], F32, name="magc")
-        root0 = keep.tile([P, HB * PACK], F32, name="root0")
-        rinv = keep.tile([P, HB * PACK], F32, name="rinv")
-        quot = keep.tile([P, HB * PACK], F32, name="quot")
-        root2 = keep.tile([P, HB * PACK], F32, name="root2")
-        nc.vector.scalar_tensor_tensor(mag[:], sm_t[:], -1.0, sm_t[:], ALU.mult, ALU.max)
-        nc.vector.tensor_scalar(magc[:], mag[:], TINY, None, ALU.max)
-        nc.scalar.activation(root0[:], magc[:], ACT.Sqrt)
-        nc.vector.reciprocal(rinv[:], root0[:])
-        nc.vector.tensor_tensor(quot[:], magc[:], rinv[:], ALU.mult)
-        nc.vector.tensor_tensor(root2[:], quot[:], root0[:], ALU.add)
-        wide = max(CHUNKS)
+        half = keep.tile([P, HB * PACK], F32, name="half")
+        root = keep.tile([P, HB * PACK], F32, name="root")
+        nc.gpsimd.memset(half[:], 0.5)
+        nc.scalar.activation(mag[:], sm_t[:], ACT.Abs)
+        nc.gpsimd.tensor_tensor(root[:], mag[:], half[:], ALU.pow)
+        wide = min(CHUNKS)
         signs = []
         for b in range(HB):
             sign_b = keep.tile([P, wide, PACK], BF16, name="sign%d" % b, align_bytes=64)
@@ -101,33 +80,58 @@ def tile_list_modp_relu2_res_noneP_kernel(
             signs.append(sign_b)
 
         wu_w = keep.tile([P, R], I32, name="wu_w", align_bytes=64)
-        wu_s = keep.tile([P, PASS], U8, name="wu_s", align_bytes=64)
+        wu_s = keep.tile([P, R], U8, name="wu_s", align_bytes=64)
+        for b in range(HB):
+            part = slice(b * PASS, (b + 1) * PASS)
+            nc.vector.tensor_copy(
+                wu_w[:, part].rearrange("p (t m) -> p m t", t=PACK), wu_raw[:, part].rearrange("p (m t) -> p m t", t=PACK)
+            )
         nc.vector.tensor_copy(
-            wu_w[:].rearrange("p (b t m) -> p b m t", b=HB, t=PACK), wu_raw[:].rearrange("p (b m t) -> p b m t", b=HB, t=PACK)
+            wu_s[:].rearrange("p (b t m) -> p b m t", b=HB, t=PACK), wus_raw[:].rearrange("p (b m t) -> p b m t", b=HB, t=PACK)
         )
-        nc.vector.tensor_copy(
-            wu_s[:].rearrange("p (t m) -> p m t", t=PACK), wus_raw[:].rearrange("p (m t) -> p m t", t=PACK)
+
+        wd_raw = keep.tile([P, HB * N + HB * N // 2], I32, name="wd_raw", align_bytes=64)
+        wd8_raw = wd_raw[:, : HB * N]
+        wd4_raw = wd_raw[:, HB * N :].bitcast(U8)
+        wgo_t = keep.tile([P, J], F32, name="wgo_t")
+        nc.sync.dma_start(
+            wd8_raw.rearrange("p (a n) -> p a n", a=HB), wd8_words.rearrange("a p n i -> p a (n i)").bitcast(I32)
         )
+        nc.sync.dma_start(
+            wd_raw[:, HB * N :].rearrange("p (a n) -> p a n", a=HB), wd4_words.rearrange("a p n -> p a n").bitcast(I32)
+        )
+        for first, planes in ((0, wd4_scales), (4, wd8_scales)):
+            for q in range(4):
+                nc.sync.dma_start(
+                    wds_raw[32 * q + first : 32 * q + first + 4, :].bitcast(I32).rearrange("r (a n) -> r a n", a=HB),
+                    planes[:, 4 * q : 4 * q + 4, :].bitcast(I32).rearrange("a r n -> r a n"),
+                )
+        nc.sync.dma_start(wgo_t[:], wgo)
 
         starts = [sum(CHUNKS[:c]) for c in range(len(CHUNKS))]
         picked = []
-        for c, width in enumerate(CHUNKS):
+
+        def pick(c, tag_w, tag_s):
+            width = CHUNKS[c]
             cols = offsets[:, starts[c] // 16 : (starts[c] + width) // 16]
-            g_w = keep.tile([P, width], I32, name="g_w%d" % c, align_bytes=64)
-            g_s = keep.tile([P, width], U8, name="g_s%d" % c, align_bytes=64)
+            g_w = keep.tile([P, width], I32, name="g_w%d" % c, tag=tag_w, align_bytes=64)
+            g_s = keep.tile([P, width], U8, name="g_s%d" % c, tag=tag_s, align_bytes=64)
             nc.vector.tensor_copy(g_w[:].bitcast(U32), tab_w[:].bitcast(U32).indirect(cols))
             nc.vector.tensor_copy(g_s[:], tab_s[:].indirect(cols))
             picked.append((g_w, g_s))
+
+        pick(0, "g_w0", "g_s0")
+        pick(1, "g_w1", "g_s1")
 
         wd8_w = keep.tile([P, HB * N], I32, name="wd8_w", align_bytes=64)
         wd4_w = keep.tile([P, HB * N * 2], U8, name="wd4_w", align_bytes=64)
         wd_s = keep.tile([P, HB * N], U8, name="wd_s", align_bytes=64)
         nc.vector.tensor_copy(
-            wd8_w[:].rearrange("p (a t m) -> p a m t", a=HB, t=PACK), wd8_raw[:].rearrange("p (a m t) -> p a m t", a=HB, t=PACK)
+            wd8_w[:].rearrange("p (a t m) -> p a m t", a=HB, t=PACK), wd8_raw.rearrange("p (a m t) -> p a m t", a=HB, t=PACK)
         )
         nc.vector.tensor_copy(
-            wd4_w[:].rearrange("p (a t m e) -> p a m t e", a=HB, t=PACK, e=2),
-            wd4_raw[:].rearrange("p (a m t e) -> p a m t e", a=HB, t=PACK, e=2),
+            wd4_w[:].bitcast(U16).rearrange("p (a t m) -> p a m t", a=HB, t=PACK),
+            wd4_raw.bitcast(U16).rearrange("p (a m t) -> p a m t", a=HB, t=PACK),
         )
         nc.vector.tensor_copy(
             wd_s[:].rearrange("p (a t m) -> p a m t", a=HB, t=PACK), wds_raw[:].rearrange("p (a m t) -> p a m t", a=HB, t=PACK)
@@ -145,27 +149,31 @@ def tile_list_modp_relu2_res_noneP_kernel(
                 nc.tensor.matmul_mx(
                     out=acc[:],
                     lhsT=wu_w[:, col : col + P].bitcast(FP8X4),
-                    lhsT_scale=wu_s[4 * b :, t * P : (t + 1) * P],
+                    lhsT_scale=wu_s[:, col : col + P],
                     rhs=g_w[:].bitcast(FP8X4),
                     rhs_scale=g_s[:],
                     start=True,
                     stop=True,
                 )
-                nc.scalar.activation(relu[:, t, :], acc[:], ACT.Relu, scale=root2[:, b * PACK + t : b * PACK + t + 1])
-            square = ring.tile([P, width * PACK], BF16, name="square", tag="square", align_bytes=64)
+                factor = root[:, b * PACK + t : b * PACK + t + 1]
+                nc.scalar.activation(relu[:, t, :], acc[:], ACT.Relu, scale=factor)
+            square = keep.tile([P, width * PACK], BF16, name="square", tag="square%d_%d" % (c, b), align_bytes=64)
             nc.scalar.activation(
                 square[:].rearrange("p (c i t) -> p c t i", i=4, t=PACK),
                 relu[:].rearrange("p t (c i) -> p c t i", i=4),
                 ACT.Square,
-                scale=0.5,
             )
-            signed = ring.tile([P, width * PACK], BF16, name="signed", tag="signed", align_bytes=64)
-            nc.vector.tensor_tensor(
-                signed[:], square[:], signs[b][:].rearrange("p c t -> p (c t)")[:, : width * PACK], ALU.mult
-            )
+            signed = keep.tile([P, width * PACK], BF16, name="signed", tag="signed%d_%d" % (c, b), align_bytes=64)
             h_w = keep.tile([P, width], U32, name="h_w%d_%d" % (c, b), align_bytes=64)
             h_s = keep.tile([P, width], U8, name="h_s%d_%d" % (c, b), align_bytes=64)
-            nc.vector.quantize_mx(out=h_w[:].bitcast(FP8X4), scales=h_s[:], in_=signed[:])
+            for j0 in range(0, width, wide):
+                part = slice(j0 * PACK, (j0 + wide) * PACK)
+                nc.vector.tensor_tensor(signed[:, part], square[:, part], signs[b][:].rearrange("p c t -> p (c t)"), ALU.mult)
+            for j0 in range(0, width, wide):
+                part = slice(j0 * PACK, (j0 + wide) * PACK)
+                nc.vector.quantize_mx(
+                    out=h_w[:, j0 : j0 + wide].bitcast(FP8X4), scales=h_s[:, j0 : j0 + wide], in_=signed[:, part]
+                )
             hidden[(c, b)] = (h_w, h_s)
 
         def put_result(c, t):
@@ -194,13 +202,16 @@ def tile_list_modp_relu2_res_noneP_kernel(
                         start=False,
                         stop=(b == HB - 1 and j0 + narrow == width),
                     )
-            y = keep.tile([P, width], F32, name="y%d_%d" % (c, t))
+            held = t == PACK - 1 and c + 1 < len(CHUNKS)
+            tag = "square%d_%d" % (c + 1, HB - 1) if held else "y%d_%d" % (c, t)
+            y = keep.tile([P, width], F32, name="y", tag=tag, align_bytes=64)
             nc.scalar.copy(y[:], acc[:])
             cols = offsets[:, starts[c] // 16 : (starts[c] + width) // 16]
             nc.vector.tensor_tensor(windows[t][:].indirect(cols), y[:], wgo_t[:, starts[c] : starts[c] + width], ALU.mult)
 
         make_hidden(0, 0)
         make_hidden(0, 1)
+        pick(2, "signed0_0", "signed0_1")
         for c in range(len(CHUNKS) - 1):
             put_result(c, 0)
             put_result(c, 1)
@@ -210,27 +221,39 @@ def tile_list_modp_relu2_res_noneP_kernel(
             put_result(c, 3)
 
         rows = out_0.rearrange("(p t) c -> p t c", t=PACK)
-        edges = [sum(TAIL[:i]) for i in range(len(TAIL))]
-        pairs = [keep.tile([P, 2, w, 2], BF16, name="pairs%d" % i, align_bytes=64) for i, w in enumerate(TAIL)]
+        widths = [w for w, paired in TAIL]
+        edges = [sum(widths[:i]) for i in range(len(TAIL))]
+        rounded = [keep.tile([P, PACK * w], BF16, name="rounded%d" % i, align_bytes=64) for i, w in enumerate(widths)]
         for t in range(PACK):
             put_result(len(CHUNKS) - 1, t)
         for t in range(PACK):
             nc.sync.dma_start(rows[:, t, :], windows[t][:])
-            for i, w in enumerate(TAIL):
-                nc.scalar.copy(pairs[i][:, t // 2, :, t % 2], windows[t][:, edges[i] : edges[i] + w])
+            for i, (w, paired) in enumerate(TAIL):
+                if paired:
+                    place = rounded[i][:].rearrange("p (u c e) -> p u c e", u=2, e=2)[:, t // 2, :, t % 2]
+                else:
+                    place = rounded[i][:, t * w : (t + 1) * w]
+                nc.scalar.copy(place, windows[t][:, edges[i] : edges[i] + w])
 
         out_s = keep.tile([P, T], U8, name="out_s", align_bytes=64)
         words_out = out_1[0].rearrange("p t i -> p (t i)").bitcast(I32)
-        grouped = [keep.tile([P, w * PACK], BF16, name="grouped%d" % i, align_bytes=64) for i, w in enumerate(TAIL)]
+        grouped = [keep.tile([P, w * PACK], BF16, name="grouped%d" % i, align_bytes=64) for i, w in enumerate(widths)]
 
         def group(i):
-            nc.vector.tensor_copy(
-                grouped[i][:].bitcast(I32).rearrange("p (c u) -> p c u", u=2),
-                pairs[i][:].rearrange("p u c e -> p u (c e)").bitcast(I32).rearrange("p u c -> p c u"),
-            )
+            if TAIL[i][1]:
+                nc.vector.tensor_copy(
+                    grouped[i][:].bitcast(I32).rearrange("p (c u) -> p c u", u=2),
+                    rounded[i][:].bitcast(I32).rearrange("p (u c) -> p c u", u=2),
+                )
+            else:
+                copy = nc.scalar.copy if i == len(TAIL) - 1 else nc.vector.tensor_copy
+                copy(
+                    grouped[i][:].rearrange("p (c i t) -> p c t i", i=4, t=PACK),
+                    rounded[i][:].rearrange("p (t c i) -> p c t i", i=4, t=PACK),
+                )
 
         def finish(i):
-            w = TAIL[i]
+            w = widths[i]
             out_w = keep.tile([P, w], I32, name="out_w%d" % i, align_bytes=64)
             nc.vector.quantize_mx(out=out_w[:].bitcast(FP8X4), scales=out_s[:, edges[i] : edges[i] + w], in_=grouped[i][:])
             nc.sync.dma_start(words_out[:, edges[i] : edges[i] + w], out_w[:])

@@ -22,6 +22,7 @@ PASS = P * PACK
 HB = R // PASS
 CHUNKS = (256, 256, 512)
 TAIL = ((256, False), (256, False), (512, True), (512, True), (256, True), (256, False))
+TINY = 2.0 ** -100
 
 
 def tile_list_modp_relu2_res_noneP_kernel(
@@ -38,56 +39,63 @@ def tile_list_modp_relu2_res_noneP_kernel(
         tab_w = keep.tile([P, T], I32, name="tab_w", align_bytes=64)
         tab_s = keep.tile([P, T], U8, name="tab_s", align_bytes=64)
         wu_raw = keep.tile([P, R], I32, name="wu_raw", align_bytes=64)
-        wus_raw = keep.tile([P, R], U8, name="wus_raw", align_bytes=64)
+        wus_raw = keep.tile([P, PASS], U8, name="wus_raw", align_bytes=64)
         sm_t = keep.tile([P, HB * PACK], F32, name="sm_t")
 
         wds_raw = keep.tile([P, HB * N], U8, name="wds_raw", align_bytes=64)
         nc.gpsimd.memset(tab_s[:].bitcast(I32), 0)
+        nc.gpsimd.memset(wus_raw[:].bitcast(I32), 0)
         nc.gpsimd.memset(wds_raw[:].bitcast(I32), 0)
 
         nc.sync.dma_start(offsets[:], offs)
         nc.sync.dma_start(sm_t[:].rearrange("p (b t) -> p b t", t=PACK), sm.rearrange("(b p t) -> p b t", p=P, t=PACK))
         for q in range(4):
-            nc.sync.dma_start(
-                wus_raw[32 * q : 32 * q + 32, :].bitcast(I32),
-                wu_scales[0, 4 * q : 4 * q + 4, :].bitcast(I32).unsqueeze(0).to_broadcast([8, 4, R // 4]),
-            )
+            nc.sync.dma_start(tab_s[32 * q : 32 * q + 4, :].bitcast(I32), tab_scales[0, 4 * q : 4 * q + 4, :].bitcast(I32))
         nc.sync.dma_start(tab_w[:], tab_words[0].rearrange("p t i -> p (t i)").bitcast(I32))
         nc.sync.dma_start(wu_raw[:], wu_words[0].rearrange("p r i -> p (r i)").bitcast(I32))
         for q in range(4):
-            nc.sync.dma_start(tab_s[32 * q : 32 * q + 4, :].bitcast(I32), tab_scales[0, 4 * q : 4 * q + 4, :].bitcast(I32))
+            nc.sync.dma_start(
+                wus_raw[32 * q : 32 * q + 4 * HB, :].bitcast(I32),
+                wu_scales[0, 4 * q : 4 * q + 4, :].bitcast(I32).rearrange("r (b n) -> b r n", b=HB),
+            )
 
         windows = [keep.tile([P, T], F32, name="window%d" % t) for t in range(PACK)]
         for t in range(2):
-            nc.vector.memset(windows[t][:], 0.0)
+            nc.vector.memset(windows[t][:].bitcast(I32), 0)
         for t in range(2, PACK):
             for c0 in range(0, T, 512):
-                nc.gpsimd.memset(windows[t][:, c0 : c0 + 512], 0.0)
+                nc.gpsimd.memset(windows[t][:, c0 : c0 + 512].bitcast(I32), 0)
 
-        mag = keep.tile([P, HB * PACK], F32, name="mag")
-        half = keep.tile([P, HB * PACK], F32, name="half")
+        mag = keep.tile([P, HB * PACK], F32, name="mag", tag="sign0", align_bytes=64)
+        magc = keep.tile([P, HB * PACK], F32, name="magc")
+        root0 = keep.tile([P, HB * PACK], F32, name="root0", tag="sign1", align_bytes=64)
+        rinv = keep.tile([P, HB * PACK], F32, name="rinv")
+        quot = keep.tile([P, HB * PACK], F32, name="quot")
         root = keep.tile([P, HB * PACK], F32, name="root")
-        nc.gpsimd.memset(half[:], 0.5)
-        nc.scalar.activation(mag[:], sm_t[:], ACT.Abs)
-        nc.gpsimd.tensor_tensor(root[:], mag[:], half[:], ALU.pow)
+        nc.vector.scalar_tensor_tensor(mag[:], sm_t[:], -1.0, sm_t[:], ALU.mult, ALU.max)
+        nc.vector.tensor_scalar(magc[:], mag[:], TINY, None, ALU.max)
+        nc.scalar.activation(root0[:], magc[:], ACT.Sqrt)
+        nc.vector.reciprocal(rinv[:], root0[:])
+        nc.vector.tensor_tensor(quot[:], magc[:], rinv[:], ALU.mult)
+        nc.vector.tensor_tensor(root[:], quot[:], root0[:], ALU.add)
         wide = min(CHUNKS)
         signs = []
         for b in range(HB):
-            sign_b = keep.tile([P, wide, PACK], BF16, name="sign%d" % b, align_bytes=64)
+            sign_b = keep.tile([P, wide, PACK], BF16, name="sign", tag="sign%d" % b, align_bytes=64)
             nc.scalar.activation(
                 sign_b[:], sm_t[:, b * PACK : (b + 1) * PACK].unsqueeze(1).to_broadcast([P, wide, PACK]), ACT.Sign
             )
             signs.append(sign_b)
 
         wu_w = keep.tile([P, R], I32, name="wu_w", align_bytes=64)
-        wu_s = keep.tile([P, R], U8, name="wu_s", align_bytes=64)
+        wu_s = keep.tile([P, PASS], U8, name="wu_s", align_bytes=64)
         for b in range(HB):
             part = slice(b * PASS, (b + 1) * PASS)
             nc.vector.tensor_copy(
                 wu_w[:, part].rearrange("p (t m) -> p m t", t=PACK), wu_raw[:, part].rearrange("p (m t) -> p m t", t=PACK)
             )
         nc.vector.tensor_copy(
-            wu_s[:].rearrange("p (b t m) -> p b m t", b=HB, t=PACK), wus_raw[:].rearrange("p (b m t) -> p b m t", b=HB, t=PACK)
+            wu_s[:].rearrange("p (t m) -> p m t", t=PACK), wus_raw[:].rearrange("p (m t) -> p m t", t=PACK)
         )
 
         wd_raw = keep.tile([P, HB * N + HB * N // 2], I32, name="wd_raw", align_bytes=64)
@@ -149,7 +157,7 @@ def tile_list_modp_relu2_res_noneP_kernel(
                 nc.tensor.matmul_mx(
                     out=acc[:],
                     lhsT=wu_w[:, col : col + P].bitcast(FP8X4),
-                    lhsT_scale=wu_s[:, col : col + P],
+                    lhsT_scale=wu_s[4 * b :, t * P : (t + 1) * P],
                     rhs=g_w[:].bitcast(FP8X4),
                     rhs_scale=g_s[:],
                     start=True,
@@ -162,6 +170,7 @@ def tile_list_modp_relu2_res_noneP_kernel(
                 square[:].rearrange("p (c i t) -> p c t i", i=4, t=PACK),
                 relu[:].rearrange("p t (c i) -> p c t i", i=4),
                 ACT.Square,
+                scale=0.5,
             )
             signed = keep.tile([P, width * PACK], BF16, name="signed", tag="signed%d_%d" % (c, b), align_bytes=64)
             h_w = keep.tile([P, width], U32, name="h_w%d_%d" % (c, b), align_bytes=64)

@@ -43,28 +43,25 @@ def tile_list_modp_relu2_res_noneP_kernel(
         sm_t = keep.tile([P, HB * PACK], F32, name="sm_t")
 
         wds_raw = keep.tile([P, HB * N], U8, name="wds_raw", align_bytes=64)
-        nc.gpsimd.memset(tab_s[:].bitcast(I32), 0)
         nc.gpsimd.memset(wus_raw[:].bitcast(I32), 0)
+        nc.gpsimd.memset(tab_s[:].bitcast(I32), 0)
         nc.gpsimd.memset(wds_raw[:].bitcast(I32), 0)
 
         nc.sync.dma_start(offsets[:], offs)
         nc.sync.dma_start(sm_t[:].rearrange("p (b t) -> p b t", t=PACK), sm.rearrange("(b p t) -> p b t", p=P, t=PACK))
         for q in range(4):
-            nc.sync.dma_start(tab_s[32 * q : 32 * q + 4, :].bitcast(I32), tab_scales[0, 4 * q : 4 * q + 4, :].bitcast(I32))
-        nc.sync.dma_start(tab_w[:], tab_words[0].rearrange("p t i -> p (t i)").bitcast(I32))
-        nc.sync.dma_start(wu_raw[:], wu_words[0].rearrange("p r i -> p (r i)").bitcast(I32))
-        for q in range(4):
             nc.sync.dma_start(
                 wus_raw[32 * q : 32 * q + 4 * HB, :].bitcast(I32),
                 wu_scales[0, 4 * q : 4 * q + 4, :].bitcast(I32).rearrange("r (b n) -> b r n", b=HB),
             )
+        nc.sync.dma_start(tab_w[:], tab_words[0].rearrange("p t i -> p (t i)").bitcast(I32))
+        nc.sync.dma_start(wu_raw[:], wu_words[0].rearrange("p r i -> p (r i)").bitcast(I32))
+        for q in range(4):
+            nc.sync.dma_start(tab_s[32 * q : 32 * q + 4, :].bitcast(I32), tab_scales[0, 4 * q : 4 * q + 4, :].bitcast(I32))
 
         windows = [keep.tile([P, T], F32, name="window%d" % t) for t in range(PACK)]
-        for t in range(2):
+        for t in range(PACK):
             nc.vector.memset(windows[t][:].bitcast(I32), 0)
-        for t in range(2, PACK):
-            for c0 in range(0, T, 512):
-                nc.gpsimd.memset(windows[t][:, c0 : c0 + 512].bitcast(I32), 0)
 
         mag = keep.tile([P, HB * PACK], F32, name="mag", tag="sign0", align_bytes=64)
         magc = keep.tile([P, HB * PACK], F32, name="magc")
@@ -167,8 +164,8 @@ def tile_list_modp_relu2_res_noneP_kernel(
                 nc.scalar.activation(relu[:, t, :], acc[:], ACT.Relu, scale=factor)
             square = keep.tile([P, width * PACK], BF16, name="square", tag="square%d_%d" % (c, b), align_bytes=64)
             nc.scalar.activation(
-                square[:].rearrange("p (c i t) -> p c t i", i=4, t=PACK),
-                relu[:].rearrange("p t (c i) -> p c t i", i=4),
+                square[:].rearrange("p (c t) -> p c t", t=PACK),
+                relu[:].rearrange("p t c -> p c t"),
                 ACT.Square,
                 scale=0.5,
             )
@@ -257,8 +254,8 @@ def tile_list_modp_relu2_res_noneP_kernel(
             else:
                 copy = nc.scalar.copy if i == len(TAIL) - 1 else nc.vector.tensor_copy
                 copy(
-                    grouped[i][:].rearrange("p (c i t) -> p c t i", i=4, t=PACK),
-                    rounded[i][:].rearrange("p (t c i) -> p c t i", i=4, t=PACK),
+                    grouped[i][:].rearrange("p (c t) -> p c t", t=PACK),
+                    rounded[i][:].rearrange("p (t c) -> p c t", t=PACK),
                 )
 
         def finish(i):

@@ -20,8 +20,11 @@ P = 128
 PACK = 4
 PASS = P * PACK
 HB = R // PASS
+QUADRANTS = 4
+BANK = 512
 CHUNKS = (256, 256, 512)
-TAIL = ((256, False), (256, False), (512, True), (512, True), (256, True), (256, False))
+TAIL_VECTOR = (256, 512, 512)
+TAIL_SCALAR = (256, 256, 256)
 TINY = 2.0 ** -100
 
 
@@ -41,27 +44,33 @@ def tile_list_modp_relu2_res_noneP_kernel(
         wu_raw = keep.tile([P, R], I32, name="wu_raw", align_bytes=64)
         wus_raw = keep.tile([P, PASS], U8, name="wus_raw", align_bytes=64)
         sm_t = keep.tile([P, HB * PACK], F32, name="sm_t")
-
         wds_raw = keep.tile([P, HB * N], U8, name="wds_raw", align_bytes=64)
+
         nc.gpsimd.memset(wus_raw[:].bitcast(I32), 0)
         nc.gpsimd.memset(tab_s[:].bitcast(I32), 0)
         nc.gpsimd.memset(wds_raw[:].bitcast(I32), 0)
 
         nc.sync.dma_start(offsets[:], offs)
         nc.sync.dma_start(sm_t[:].rearrange("p (b t) -> p b t", t=PACK), sm.rearrange("(b p t) -> p b t", p=P, t=PACK))
-        for q in range(4):
+        for q in range(QUADRANTS):
             nc.sync.dma_start(
                 wus_raw[32 * q : 32 * q + 4 * HB, :].bitcast(I32),
                 wu_scales[0, 4 * q : 4 * q + 4, :].bitcast(I32).rearrange("r (b n) -> b r n", b=HB),
             )
         nc.sync.dma_start(tab_w[:], tab_words[0].rearrange("p t i -> p (t i)").bitcast(I32))
         nc.sync.dma_start(wu_raw[:], wu_words[0].rearrange("p r i -> p (r i)").bitcast(I32))
-        for q in range(4):
+        for q in range(QUADRANTS):
             nc.sync.dma_start(tab_s[32 * q : 32 * q + 4, :].bitcast(I32), tab_scales[0, 4 * q : 4 * q + 4, :].bitcast(I32))
 
-        windows = [keep.tile([P, T], F32, name="window%d" % t) for t in range(PACK)]
-        for t in range(PACK):
-            nc.vector.memset(windows[t][:].bitcast(I32), 0)
+        windows = []
+
+        def clear_window(tag):
+            window = keep.tile([P, T], F32, name="window", tag=tag, align_bytes=64)
+            nc.vector.memset(window[:].bitcast(I32), 0)
+            windows.append(window)
+
+        for t in range(PACK - 1):
+            clear_window("window%d" % t)
 
         mag = keep.tile([P, HB * PACK], F32, name="mag", tag="sign0", align_bytes=64)
         magc = keep.tile([P, HB * PACK], F32, name="magc")
@@ -75,7 +84,7 @@ def tile_list_modp_relu2_res_noneP_kernel(
         nc.vector.reciprocal(rinv[:], root0[:])
         nc.vector.tensor_tensor(quot[:], magc[:], rinv[:], ALU.mult)
         nc.vector.tensor_tensor(root[:], quot[:], root0[:], ALU.add)
-        wide = min(CHUNKS)
+        wide = max(CHUNKS) // 2
         signs = []
         for b in range(HB):
             sign_b = keep.tile([P, wide, PACK], BF16, name="sign", tag="sign%d" % b, align_bytes=64)
@@ -92,7 +101,7 @@ def tile_list_modp_relu2_res_noneP_kernel(
                 wu_w[:, part].rearrange("p (t m) -> p m t", t=PACK), wu_raw[:, part].rearrange("p (m t) -> p m t", t=PACK)
             )
         nc.vector.tensor_copy(
-            wu_s[:].rearrange("p (t m) -> p m t", t=PACK), wus_raw[:].rearrange("p (m t) -> p m t", t=PACK)
+            wu_s[:].rearrange("p (t m) -> p t m", t=PACK), wus_raw[:].rearrange("p (m t) -> p t m", t=PACK)
         )
 
         wd_raw = keep.tile([P, HB * N + HB * N // 2], I32, name="wd_raw", align_bytes=64)
@@ -106,7 +115,7 @@ def tile_list_modp_relu2_res_noneP_kernel(
             wd_raw[:, HB * N :].rearrange("p (a n) -> p a n", a=HB), wd4_words.rearrange("a p n -> p a n").bitcast(I32)
         )
         for first, planes in ((0, wd4_scales), (4, wd8_scales)):
-            for q in range(4):
+            for q in range(QUADRANTS):
                 nc.sync.dma_start(
                     wds_raw[32 * q + first : 32 * q + first + 4, :].bitcast(I32).rearrange("r (a n) -> r a n", a=HB),
                     planes[:, 4 * q : 4 * q + 4, :].bitcast(I32).rearrange("a r n -> r a n"),
@@ -135,11 +144,11 @@ def tile_list_modp_relu2_res_noneP_kernel(
             wd8_w[:].rearrange("p (a t m) -> p a m t", a=HB, t=PACK), wd8_raw.rearrange("p (a m t) -> p a m t", a=HB, t=PACK)
         )
         nc.vector.tensor_copy(
-            wd4_w[:].bitcast(U16).rearrange("p (a t m) -> p a m t", a=HB, t=PACK),
-            wd4_raw.bitcast(U16).rearrange("p (a m t) -> p a m t", a=HB, t=PACK),
+            wd4_w[:].bitcast(U16).rearrange("p (a t m) -> p a t m", a=HB, t=PACK),
+            wd4_raw.bitcast(U16).rearrange("p (a m t) -> p a t m", a=HB, t=PACK),
         )
         nc.vector.tensor_copy(
-            wd_s[:].rearrange("p (a t m) -> p a m t", a=HB, t=PACK), wds_raw[:].rearrange("p (a m t) -> p a m t", a=HB, t=PACK)
+            wd_s[:].rearrange("p (a t m) -> p a t m", a=HB, t=PACK), wds_raw[:].rearrange("p (a m t) -> p a t m", a=HB, t=PACK)
         )
 
         hidden = {}
@@ -172,20 +181,22 @@ def tile_list_modp_relu2_res_noneP_kernel(
             signed = keep.tile([P, width * PACK], BF16, name="signed", tag="signed%d_%d" % (c, b), align_bytes=64)
             h_w = keep.tile([P, width], U32, name="h_w%d_%d" % (c, b), align_bytes=64)
             h_s = keep.tile([P, width], U8, name="h_s%d_%d" % (c, b), align_bytes=64)
-            for j0 in range(0, width, wide):
-                part = slice(j0 * PACK, (j0 + wide) * PACK)
-                nc.vector.tensor_tensor(signed[:, part], square[:, part], signs[b][:].rearrange("p c t -> p (c t)"), ALU.mult)
-            for j0 in range(0, width, wide):
-                part = slice(j0 * PACK, (j0 + wide) * PACK)
+            half = width // 2
+            sign = signs[b][:].rearrange("p c t -> p (c t)")[:, : half * PACK]
+            for j0 in (0, half):
+                part = slice(j0 * PACK, (j0 + half) * PACK)
+                nc.vector.tensor_tensor(signed[:, part], square[:, part], sign, ALU.mult)
+            for j0 in (0, half):
+                part = slice(j0 * PACK, (j0 + half) * PACK)
                 nc.vector.quantize_mx(
-                    out=h_w[:, j0 : j0 + wide].bitcast(FP8X4), scales=h_s[:, j0 : j0 + wide], in_=signed[:, part]
+                    out=h_w[:, j0 : j0 + half].bitcast(FP8X4), scales=h_s[:, j0 : j0 + half], in_=signed[:, part]
                 )
             hidden[(c, b)] = (h_w, h_s)
 
         def put_result(c, t):
             width = CHUNKS[c]
             acc = psum.tile([P, width], F32, name="acc_y", tag="acc_y")
-            narrow = width if width == 512 else P
+            narrow = width if width == BANK else P
             for b in range(HB):
                 h_w, h_s = hidden[(c, b)]
                 col = b * N + t * P
@@ -218,6 +229,7 @@ def tile_list_modp_relu2_res_noneP_kernel(
         make_hidden(0, 0)
         make_hidden(0, 1)
         pick(2, "signed0_0", "signed0_1")
+        clear_window("square0_1")
         for c in range(len(CHUNKS) - 1):
             put_result(c, 0)
             put_result(c, 1)
@@ -227,36 +239,26 @@ def tile_list_modp_relu2_res_noneP_kernel(
             put_result(c, 3)
 
         rows = out_0.rearrange("(p t) c -> p t c", t=PACK)
-        widths = [w for w, paired in TAIL]
-        edges = [sum(widths[:i]) for i in range(len(TAIL))]
+        widths = TAIL_VECTOR + TAIL_SCALAR
+        edges = [sum(widths[:i]) for i in range(len(widths))]
         rounded = [keep.tile([P, PACK * w], BF16, name="rounded%d" % i, align_bytes=64) for i, w in enumerate(widths)]
         for t in range(PACK):
             put_result(len(CHUNKS) - 1, t)
         for t in range(PACK):
             nc.sync.dma_start(rows[:, t, :], windows[t][:])
-            for i, (w, paired) in enumerate(TAIL):
-                if paired:
-                    place = rounded[i][:].rearrange("p (u c e) -> p u c e", u=2, e=2)[:, t // 2, :, t % 2]
-                else:
-                    place = rounded[i][:, t * w : (t + 1) * w]
-                nc.scalar.copy(place, windows[t][:, edges[i] : edges[i] + w])
+            for i, w in enumerate(widths):
+                nc.scalar.copy(rounded[i][:, t * w : (t + 1) * w], windows[t][:, edges[i] : edges[i] + w])
 
         out_s = keep.tile([P, T], U8, name="out_s", align_bytes=64)
         words_out = out_1[0].rearrange("p t i -> p (t i)").bitcast(I32)
         grouped = [keep.tile([P, w * PACK], BF16, name="grouped%d" % i, align_bytes=64) for i, w in enumerate(widths)]
 
         def group(i):
-            if TAIL[i][1]:
-                nc.vector.tensor_copy(
-                    grouped[i][:].bitcast(I32).rearrange("p (c u) -> p c u", u=2),
-                    rounded[i][:].bitcast(I32).rearrange("p (u c) -> p c u", u=2),
-                )
-            else:
-                copy = nc.scalar.copy if i == len(TAIL) - 1 else nc.vector.tensor_copy
-                copy(
-                    grouped[i][:].rearrange("p (c t) -> p c t", t=PACK),
-                    rounded[i][:].rearrange("p (t c) -> p c t", t=PACK),
-                )
+            copy = nc.vector.tensor_copy if i < len(TAIL_VECTOR) else nc.scalar.copy
+            copy(
+                grouped[i][:].rearrange("p (c t) -> p c t", t=PACK),
+                rounded[i][:].rearrange("p (t c) -> p c t", t=PACK),
+            )
 
         def finish(i):
             w = widths[i]
@@ -265,10 +267,10 @@ def tile_list_modp_relu2_res_noneP_kernel(
             nc.sync.dma_start(words_out[:, edges[i] : edges[i] + w], out_w[:])
 
         group(0)
-        for i in range(1, len(TAIL)):
+        for i in range(1, len(widths)):
             group(i)
             finish(i - 1)
-        finish(len(TAIL) - 1)
-        for q in range(4):
+        finish(len(widths) - 1)
+        for q in range(QUADRANTS):
             queue = nc.sync if q % 2 == 0 else nc.scalar
             queue.dma_start(out_2[0, 4 * q : 4 * q + 4, :].bitcast(I32), out_s[32 * q : 32 * q + 4, :].bitcast(I32))

@@ -22,9 +22,10 @@ PASS = P * PACK
 HB = R // PASS
 QUADRANTS = 4
 BANK = 512
-CHUNKS = (256, 256, 512)
-TAIL_VECTOR = (256, 512, 512)
-TAIL_SCALAR = (256, 256, 256)
+CHUNK = 256
+CHUNKS = J // CHUNK
+TAIL_VECTOR = (512, 512)
+TAIL_SCALAR = (512, 256, 256)
 TINY = 2.0 ** -100
 
 
@@ -35,32 +36,50 @@ def tile_list_modp_relu2_res_noneP_kernel(
     nc = tc.nc
     with ExitStack() as ctx:
         keep = ctx.enter_context(tc.tile_pool(name="keep", bufs=1))
-        ring = ctx.enter_context(tc.tile_pool(name="ring", bufs=2))
         psum = ctx.enter_context(tc.psum_pool(name="psum", bufs=4))
 
         offsets = keep.tile([P, J // 16], U16, name="offsets")
         tab_w = keep.tile([P, T], I32, name="tab_w", align_bytes=64)
         tab_s = keep.tile([P, T], U8, name="tab_s", align_bytes=64)
-        wu_raw = keep.tile([P, R], I32, name="wu_raw", align_bytes=64)
+        wu_raw = [keep.tile([P, PASS], I32, name="wu_raw", tag="wu_raw%d" % b, align_bytes=64) for b in range(HB)]
         wus_raw = keep.tile([P, PASS], U8, name="wus_raw", align_bytes=64)
         sm_t = keep.tile([P, HB * PACK], F32, name="sm_t")
         wds_raw = keep.tile([P, HB * N], U8, name="wds_raw", align_bytes=64)
 
         nc.gpsimd.memset(wus_raw[:].bitcast(I32), 0)
-        nc.gpsimd.memset(tab_s[:].bitcast(I32), 0)
         nc.gpsimd.memset(wds_raw[:].bitcast(I32), 0)
 
+        for q in range(QUADRANTS):
+            nc.sync.dma_start(
+                tab_s[32 * q : 32 * q + 32, :].bitcast(I32),
+                tab_scales[0, 4 * q : 4 * q + 4, :].bitcast(I32).unsqueeze(0).to_broadcast([8, 4, T // 4]),
+            )
         nc.sync.dma_start(offsets[:], offs)
         nc.sync.dma_start(sm_t[:].rearrange("p (b t) -> p b t", t=PACK), sm.rearrange("(b p t) -> p b t", p=P, t=PACK))
+        nc.sync.dma_start(tab_w[:], tab_words[0].rearrange("p t i -> p (t i)").bitcast(I32))
         for q in range(QUADRANTS):
             nc.sync.dma_start(
                 wus_raw[32 * q : 32 * q + 4 * HB, :].bitcast(I32),
                 wu_scales[0, 4 * q : 4 * q + 4, :].bitcast(I32).rearrange("r (b n) -> b r n", b=HB),
             )
-        nc.sync.dma_start(tab_w[:], tab_words[0].rearrange("p t i -> p (t i)").bitcast(I32))
-        nc.sync.dma_start(wu_raw[:], wu_words[0].rearrange("p r i -> p (r i)").bitcast(I32))
-        for q in range(QUADRANTS):
-            nc.sync.dma_start(tab_s[32 * q : 32 * q + 4, :].bitcast(I32), tab_scales[0, 4 * q : 4 * q + 4, :].bitcast(I32))
+        wu_src = wu_words[0].rearrange("p r i -> p (r i)").bitcast(I32)
+        for b in range(HB):
+            nc.sync.dma_start(wu_raw[b][:], wu_src[:, b * PASS : (b + 1) * PASS])
+
+        wd8_raw = keep.tile([P, HB * N], I32, name="wd8_raw", tag="wd8_raw", align_bytes=64)
+        wd4_raw = keep.tile([P, HB * N // 2], I32, name="wd4_raw", align_bytes=64)
+        wgo_t = keep.tile([P, J], F32, name="wgo_t")
+        nc.sync.dma_start(
+            wd8_raw[:].rearrange("p (a n) -> p a n", a=HB), wd8_words.rearrange("a p n i -> p a (n i)").bitcast(I32)
+        )
+        nc.sync.dma_start(wd4_raw[:].rearrange("p (a n) -> p a n", a=HB), wd4_words.rearrange("a p n -> p a n").bitcast(I32))
+        for first, planes in ((0, wd4_scales), (4, wd8_scales)):
+            for q in range(QUADRANTS):
+                nc.sync.dma_start(
+                    wds_raw[32 * q + first : 32 * q + first + 4, :].bitcast(I32).rearrange("r (a n) -> r a n", a=HB),
+                    planes[:, 4 * q : 4 * q + 4, :].bitcast(I32).rearrange("a r n -> r a n"),
+                )
+        nc.sync.dma_start(wgo_t[:], wgo)
 
         windows = []
 
@@ -69,8 +88,14 @@ def tile_list_modp_relu2_res_noneP_kernel(
             nc.vector.memset(window[:].bitcast(I32), 0)
             windows.append(window)
 
-        for t in range(PACK - 1):
-            clear_window("window%d" % t)
+        clear_window("window0")
+        clear_window("window1")
+
+        def entries(first, width):
+            return offsets[:, first // 16 : (first + width) // 16]
+
+        g_s = keep.tile([P, J], U8, name="g_s", align_bytes=64)
+        nc.vector.tensor_copy(g_s[:], tab_s[:].indirect(offsets[:]))
 
         mag = keep.tile([P, HB * PACK], F32, name="mag", tag="sign0", align_bytes=64)
         magc = keep.tile([P, HB * PACK], F32, name="magc")
@@ -81,131 +106,105 @@ def tile_list_modp_relu2_res_noneP_kernel(
         nc.vector.scalar_tensor_tensor(mag[:], sm_t[:], -1.0, sm_t[:], ALU.mult, ALU.max)
         nc.vector.tensor_scalar(magc[:], mag[:], TINY, None, ALU.max)
         nc.scalar.activation(root0[:], magc[:], ACT.Sqrt)
-        nc.vector.reciprocal(rinv[:], root0[:])
-        nc.vector.tensor_tensor(quot[:], magc[:], rinv[:], ALU.mult)
-        nc.vector.tensor_tensor(root[:], quot[:], root0[:], ALU.add)
-        wide = max(CHUNKS) // 2
-        signs = []
-        for b in range(HB):
-            sign_b = keep.tile([P, wide, PACK], BF16, name="sign", tag="sign%d" % b, align_bytes=64)
-            nc.scalar.activation(
-                sign_b[:], sm_t[:, b * PACK : (b + 1) * PACK].unsqueeze(1).to_broadcast([P, wide, PACK]), ACT.Sign
-            )
-            signs.append(sign_b)
 
-        wu_w = keep.tile([P, R], I32, name="wu_w", align_bytes=64)
+        g_first = keep.tile([P, CHUNK], I32, name="g_first", align_bytes=64)
+        nc.vector.tensor_copy(g_first[:].bitcast(U32), tab_w[:].bitcast(U32).indirect(entries(0, CHUNK)))
+
+        wu_w = [keep.tile([P, PASS], I32, name="wu_w%d" % b, align_bytes=64) for b in range(HB)]
         wu_s = keep.tile([P, PASS], U8, name="wu_s", align_bytes=64)
-        for b in range(HB):
-            part = slice(b * PASS, (b + 1) * PASS)
+
+        def deal_wu(b):
             nc.vector.tensor_copy(
-                wu_w[:, part].rearrange("p (t m) -> p m t", t=PACK), wu_raw[:, part].rearrange("p (m t) -> p m t", t=PACK)
+                wu_w[b][:].rearrange("p (t m) -> p m t", t=PACK), wu_raw[b][:].rearrange("p (m t) -> p m t", t=PACK)
             )
+
+        nc.vector.reciprocal(rinv[:], root0[:])
         nc.vector.tensor_copy(
             wu_s[:].rearrange("p (t m) -> p t m", t=PACK), wus_raw[:].rearrange("p (m t) -> p t m", t=PACK)
         )
+        nc.vector.tensor_tensor(quot[:], magc[:], rinv[:], ALU.mult)
+        deal_wu(0)
+        nc.vector.tensor_tensor(root[:], quot[:], root0[:], ALU.add)
+        deal_wu(1)
+        half = CHUNK // 2
+        signs = []
+        for b in range(HB):
+            sign_b = keep.tile([P, half, PACK], BF16, name="sign", tag="sign%d" % b, align_bytes=64)
+            nc.scalar.activation(
+                sign_b[:], sm_t[:, b * PACK : (b + 1) * PACK].unsqueeze(1).to_broadcast([P, half, PACK]), ACT.Sign
+            )
+            signs.append(sign_b)
 
-        wd_raw = keep.tile([P, HB * N + HB * N // 2], I32, name="wd_raw", align_bytes=64)
-        wd8_raw = wd_raw[:, : HB * N]
-        wd4_raw = wd_raw[:, HB * N :].bitcast(U8)
-        wgo_t = keep.tile([P, J], F32, name="wgo_t")
-        nc.sync.dma_start(
-            wd8_raw.rearrange("p (a n) -> p a n", a=HB), wd8_words.rearrange("a p n i -> p a (n i)").bitcast(I32)
-        )
-        nc.sync.dma_start(
-            wd_raw[:, HB * N :].rearrange("p (a n) -> p a n", a=HB), wd4_words.rearrange("a p n -> p a n").bitcast(I32)
-        )
-        for first, planes in ((0, wd4_scales), (4, wd8_scales)):
-            for q in range(QUADRANTS):
-                nc.sync.dma_start(
-                    wds_raw[32 * q + first : 32 * q + first + 4, :].bitcast(I32).rearrange("r (a n) -> r a n", a=HB),
-                    planes[:, 4 * q : 4 * q + 4, :].bitcast(I32).rearrange("a r n -> r a n"),
-                )
-        nc.sync.dma_start(wgo_t[:], wgo)
-
-        starts = [sum(CHUNKS[:c]) for c in range(len(CHUNKS))]
-        picked = []
-
-        def pick(c, tag_w, tag_s):
-            width = CHUNKS[c]
-            cols = offsets[:, starts[c] // 16 : (starts[c] + width) // 16]
-            g_w = keep.tile([P, width], I32, name="g_w%d" % c, tag=tag_w, align_bytes=64)
-            g_s = keep.tile([P, width], U8, name="g_s%d" % c, tag=tag_s, align_bytes=64)
-            nc.vector.tensor_copy(g_w[:].bitcast(U32), tab_w[:].bitcast(U32).indirect(cols))
-            nc.vector.tensor_copy(g_s[:], tab_s[:].indirect(cols))
-            picked.append((g_w, g_s))
-
-        pick(0, "g_w0", "g_s0")
-        pick(1, "g_w1", "g_s1")
+        g_rest = keep.tile([P, J - CHUNK], I32, name="g_rest", tag="wu_raw0", align_bytes=64)
+        nc.vector.tensor_copy(g_rest[:].bitcast(U32), tab_w[:].bitcast(U32).indirect(entries(CHUNK, J - CHUNK)))
+        clear_window("wu_raw1")
 
         wd8_w = keep.tile([P, HB * N], I32, name="wd8_w", align_bytes=64)
         wd4_w = keep.tile([P, HB * N * 2], U8, name="wd4_w", align_bytes=64)
         wd_s = keep.tile([P, HB * N], U8, name="wd_s", align_bytes=64)
         nc.vector.tensor_copy(
-            wd8_w[:].rearrange("p (a t m) -> p a m t", a=HB, t=PACK), wd8_raw.rearrange("p (a m t) -> p a m t", a=HB, t=PACK)
+            wd8_w[:].rearrange("p (a t m) -> p a m t", a=HB, t=PACK),
+            wd8_raw[:].rearrange("p (a m t) -> p a m t", a=HB, t=PACK),
         )
         nc.vector.tensor_copy(
             wd4_w[:].bitcast(U16).rearrange("p (a t m) -> p a t m", a=HB, t=PACK),
-            wd4_raw.bitcast(U16).rearrange("p (a m t) -> p a t m", a=HB, t=PACK),
+            wd4_raw[:].bitcast(U16).rearrange("p (a m t) -> p a t m", a=HB, t=PACK),
         )
         nc.vector.tensor_copy(
             wd_s[:].rearrange("p (a t m) -> p a t m", a=HB, t=PACK), wds_raw[:].rearrange("p (a m t) -> p a t m", a=HB, t=PACK)
         )
 
-        hidden = {}
+        h_w = [keep.tile([P, J], U32, name="h_w%d" % b, align_bytes=64) for b in range(HB)]
+        h_s = [keep.tile([P, J], U8, name="h_s%d" % b, align_bytes=64) for b in range(HB)]
+        relus = {}
 
-        def make_hidden(c, b):
-            width = CHUNKS[c]
-            g_w, g_s = picked[c]
-            relu = ring.tile([P, PACK, width], F32, name="relu", tag="relu")
+        def rectify(c, b):
+            words = g_first[:] if c == 0 else g_rest[:, (c - 1) * CHUNK : c * CHUNK]
+            relu = keep.tile([P, PACK, CHUNK], F32, name="relu", tag="relu%d_%d" % (c, b), align_bytes=64)
             for t in range(PACK):
-                acc = psum.tile([P, width], F32, name="acc_a", tag="acc_a")
-                col = b * PASS + t * P
+                acc = psum.tile([P, CHUNK], F32, name="acc_a", tag="acc_a")
                 nc.tensor.matmul_mx(
                     out=acc[:],
-                    lhsT=wu_w[:, col : col + P].bitcast(FP8X4),
+                    lhsT=wu_w[b][:, t * P : (t + 1) * P].bitcast(FP8X4),
                     lhsT_scale=wu_s[4 * b :, t * P : (t + 1) * P],
-                    rhs=g_w[:].bitcast(FP8X4),
-                    rhs_scale=g_s[:],
+                    rhs=words.bitcast(FP8X4),
+                    rhs_scale=g_s[:, c * CHUNK : (c + 1) * CHUNK],
                     start=True,
                     stop=True,
                 )
                 factor = root[:, b * PACK + t : b * PACK + t + 1]
                 nc.scalar.activation(relu[:, t, :], acc[:], ACT.Relu, scale=factor)
-            square = keep.tile([P, width * PACK], BF16, name="square", tag="square%d_%d" % (c, b), align_bytes=64)
+            relus[(c, b)] = relu
+
+        def quantise(c, b):
+            square = keep.tile([P, CHUNK * PACK], BF16, name="square", tag="square%d_%d" % (c, b), align_bytes=64)
             nc.scalar.activation(
                 square[:].rearrange("p (c t) -> p c t", t=PACK),
-                relu[:].rearrange("p t c -> p c t"),
+                relus[(c, b)][:].rearrange("p t c -> p c t"),
                 ACT.Square,
                 scale=0.5,
             )
-            signed = keep.tile([P, width * PACK], BF16, name="signed", tag="signed%d_%d" % (c, b), align_bytes=64)
-            h_w = keep.tile([P, width], U32, name="h_w%d_%d" % (c, b), align_bytes=64)
-            h_s = keep.tile([P, width], U8, name="h_s%d_%d" % (c, b), align_bytes=64)
-            half = width // 2
-            sign = signs[b][:].rearrange("p c t -> p (c t)")[:, : half * PACK]
+            signed = keep.tile([P, CHUNK * PACK], BF16, name="signed", tag="signed%d_%d" % (c, b), align_bytes=64)
+            sign = signs[b][:].rearrange("p c t -> p (c t)")
             for j0 in (0, half):
                 part = slice(j0 * PACK, (j0 + half) * PACK)
                 nc.vector.tensor_tensor(signed[:, part], square[:, part], sign, ALU.mult)
             for j0 in (0, half):
                 part = slice(j0 * PACK, (j0 + half) * PACK)
-                nc.vector.quantize_mx(
-                    out=h_w[:, j0 : j0 + half].bitcast(FP8X4), scales=h_s[:, j0 : j0 + half], in_=signed[:, part]
-                )
-            hidden[(c, b)] = (h_w, h_s)
+                cols = slice(c * CHUNK + j0, c * CHUNK + j0 + half)
+                nc.vector.quantize_mx(out=h_w[b][:, cols].bitcast(FP8X4), scales=h_s[b][:, cols], in_=signed[:, part])
 
-        def put_result(c, t):
-            width = CHUNKS[c]
+        def project(y, t, first, width):
             acc = psum.tile([P, width], F32, name="acc_y", tag="acc_y")
             narrow = width if width == BANK else P
             for b in range(HB):
-                h_w, h_s = hidden[(c, b)]
                 col = b * N + t * P
                 nc.tensor.matmul_mx(
                     out=acc[:],
                     lhsT=wd8_w[:, col : col + P].bitcast(FP8X4),
                     lhsT_scale=wd_s[4:, col : col + P],
-                    rhs=h_w[:].bitcast(FP8X4),
-                    rhs_scale=h_s[:],
+                    rhs=h_w[b][:, first : first + width].bitcast(FP8X4),
+                    rhs_scale=h_s[b][:, first : first + width],
                     start=(b == 0),
                     stop=False,
                 )
@@ -214,50 +213,73 @@ def tile_list_modp_relu2_res_noneP_kernel(
                         out=acc[:, j0 : j0 + narrow],
                         lhsT=wd4_w[:, 2 * col : 2 * (col + P)].bitcast(FP4X4),
                         lhsT_scale=wd_s[:, col : col + P],
-                        rhs=h_w[:, j0 : j0 + narrow].bitcast(FP8X4),
-                        rhs_scale=h_s[:, j0 : j0 + narrow],
+                        rhs=h_w[b][:, first + j0 : first + j0 + narrow].bitcast(FP8X4),
+                        rhs_scale=h_s[b][:, first + j0 : first + j0 + narrow],
                         start=False,
                         stop=(b == HB - 1 and j0 + narrow == width),
                     )
-            held = t == PACK - 1 and c + 1 < len(CHUNKS)
-            tag = "square%d_%d" % (c + 1, HB - 1) if held else "y%d_%d" % (c, t)
-            y = keep.tile([P, width], F32, name="y", tag=tag, align_bytes=64)
-            nc.scalar.copy(y[:], acc[:])
-            cols = offsets[:, starts[c] // 16 : (starts[c] + width) // 16]
-            nc.vector.tensor_tensor(windows[t][:].indirect(cols), y[:], wgo_t[:, starts[c] : starts[c] + width], ALU.mult)
+            nc.scalar.copy(y, acc[:])
 
-        make_hidden(0, 0)
-        make_hidden(0, 1)
-        pick(2, "signed0_0", "signed0_1")
-        clear_window("square0_1")
-        for c in range(len(CHUNKS) - 1):
-            put_result(c, 0)
-            put_result(c, 1)
-            make_hidden(c + 1, 0)
-            put_result(c, 2)
-            make_hidden(c + 1, 1)
-            put_result(c, 3)
+        def scatter(y, t, first, width):
+            nc.vector.tensor_tensor(windows[t][:].indirect(entries(first, width)), y, wgo_t[:, first : first + width], ALU.mult)
+
+        def put(c, t, tag):
+            y = keep.tile([P, CHUNK], F32, name="y", tag=tag, align_bytes=64)
+            project(y[:], t, c * CHUNK, CHUNK)
+            scatter(y[:], t, c * CHUNK, CHUNK)
+
+        rectify(0, 0)
+        quantise(0, 0)
+        rectify(0, 1)
+        quantise(0, 1)
+        clear_window("wd8_raw")
+        rectify(1, 0)
+        put(0, 0, "y0_0")
+        quantise(1, 0)
+        rectify(1, 1)
+        put(0, 1, "relu1_0")
+        put(0, 2, "y0_2")
+        quantise(1, 1)
+        rectify(2, 0)
+        put(0, 3, "relu1_1")
+        quantise(2, 0)
+        rectify(2, 1)
+        put(1, 0, "relu2_0")
+        quantise(2, 1)
+        rectify(3, 0)
+        put(1, 1, "relu2_1")
+        quantise(3, 0)
+        rectify(3, 1)
+        put(2, 0, "relu3_0")
+        quantise(3, 1)
+        put(2, 1, "relu3_1")
+        rest = J - CHUNK
+        y2 = keep.tile([P, rest], F32, name="y2", tag="relu3_0", align_bytes=64)
+        project(y2[:, :BANK], 2, CHUNK, BANK)
+        put(3, 0, "y3_0")
+        put(3, 1, "y3_1")
+        project(y2[:, BANK:], 2, CHUNK + BANK, CHUNK)
+        scatter(y2[:], 2, CHUNK, rest)
+        y3 = keep.tile([P, rest], F32, name="y3", tag="relu3_1", align_bytes=64)
+        project(y3[:, :BANK], 3, CHUNK, BANK)
+        project(y3[:, BANK:], 3, CHUNK + BANK, CHUNK)
+        scatter(y3[:], 3, CHUNK, rest)
 
         rows = out_0.rearrange("(p t) c -> p t c", t=PACK)
         widths = TAIL_VECTOR + TAIL_SCALAR
         edges = [sum(widths[:i]) for i in range(len(widths))]
-        rounded = [keep.tile([P, PACK * w], BF16, name="rounded%d" % i, align_bytes=64) for i, w in enumerate(widths)]
-        for t in range(PACK):
-            put_result(len(CHUNKS) - 1, t)
-        for t in range(PACK):
-            nc.sync.dma_start(rows[:, t, :], windows[t][:])
-            for i, w in enumerate(widths):
-                nc.scalar.copy(rounded[i][:, t * w : (t + 1) * w], windows[t][:, edges[i] : edges[i] + w])
-
+        pairs = [keep.tile([P, 2, w, 2], BF16, name="pairs%d" % i, align_bytes=64) for i, w in enumerate(widths)]
+        grouped = [keep.tile([P, w * PACK], BF16, name="grouped%d" % i, align_bytes=64) for i, w in enumerate(widths)]
         out_s = keep.tile([P, T], U8, name="out_s", align_bytes=64)
         words_out = out_1[0].rearrange("p t i -> p (t i)").bitcast(I32)
-        grouped = [keep.tile([P, w * PACK], BF16, name="grouped%d" % i, align_bytes=64) for i, w in enumerate(widths)]
 
-        def group(i):
-            copy = nc.vector.tensor_copy if i < len(TAIL_VECTOR) else nc.scalar.copy
+        def round_rows(copy, t, i):
+            copy(pairs[i][:, t // 2, :, t % 2], windows[t][:, edges[i] : edges[i] + widths[i]])
+
+        def group(copy, word, i):
             copy(
-                grouped[i][:].rearrange("p (c t) -> p c t", t=PACK),
-                rounded[i][:].rearrange("p (t c) -> p c t", t=PACK),
+                grouped[i][:].bitcast(word).rearrange("p (c u) -> p c u", u=2),
+                pairs[i][:].rearrange("p u c e -> p (u c e)").bitcast(word).rearrange("p (u c) -> p c u", u=2),
             )
 
         def finish(i):
@@ -266,11 +288,25 @@ def tile_list_modp_relu2_res_noneP_kernel(
             nc.vector.quantize_mx(out=out_w[:].bitcast(FP8X4), scales=out_s[:, edges[i] : edges[i] + w], in_=grouped[i][:])
             nc.sync.dma_start(words_out[:, edges[i] : edges[i] + w], out_w[:])
 
-        group(0)
-        for i in range(1, len(widths)):
-            group(i)
-            finish(i - 1)
-        finish(len(widths) - 1)
+        for t in range(PACK):
+            nc.sync.dma_start(rows[:, t, :], windows[t][:])
+            if t < PACK - 1:
+                for i in range(len(widths)):
+                    if t == PACK - 2 and i < len(TAIL_VECTOR):
+                        source = windows[t][:, edges[i] : edges[i] + widths[i]]
+                        nc.scalar.copy(pairs[i][:, 1, :, :], source.unsqueeze(2).to_broadcast([P, widths[i], 2]))
+                    else:
+                        round_rows(nc.scalar.copy, t, i)
+        mine = range(len(TAIL_VECTOR))
+        for i in mine:
+            round_rows(nc.vector.tensor_copy, PACK - 1, i)
+        for i in mine:
+            group(nc.vector.tensor_copy, I32, i)
+        for i in range(len(TAIL_VECTOR), len(widths)):
+            round_rows(nc.scalar.copy, PACK - 1, i)
+            group(nc.scalar.copy, U32, i)
+        for i in range(len(widths)):
+            finish(i)
         for q in range(QUADRANTS):
             queue = nc.sync if q % 2 == 0 else nc.scalar
             queue.dma_start(out_2[0, 4 * q : 4 * q + 4, :].bitcast(I32), out_s[32 * q : 32 * q + 4, :].bitcast(I32))

@@ -44,7 +44,7 @@ def tile_list_modp_relu2_res_noneP_kernel(
         wu_raw = [keep.tile([P, PASS], I32, name="wu_raw", tag="wu_raw%d" % b, align_bytes=64) for b in range(HB)]
         wus_raw = keep.tile([P, PASS], U8, name="wus_raw", align_bytes=64)
         sm_t = keep.tile([P, HB * PACK], F32, name="sm_t")
-        wds_raw = keep.tile([P, HB * N], U8, name="wds_raw", align_bytes=64)
+        wds_raw = keep.tile([P, HB * N], U8, name="wds_raw", tag="wds_raw", align_bytes=64)
 
         nc.gpsimd.memset(wus_raw[:].bitcast(I32), 0)
         nc.gpsimd.memset(wds_raw[:].bitcast(I32), 0)
@@ -57,14 +57,14 @@ def tile_list_modp_relu2_res_noneP_kernel(
         nc.sync.dma_start(offsets[:], offs)
         nc.sync.dma_start(sm_t[:].rearrange("p (b t) -> p b t", t=PACK), sm.rearrange("(b p t) -> p b t", p=P, t=PACK))
         nc.sync.dma_start(tab_w[:], tab_words[0].rearrange("p t i -> p (t i)").bitcast(I32))
+        wu_src = wu_words[0].rearrange("p r i -> p (r i)").bitcast(I32)
+        nc.sync.dma_start(wu_raw[0][:], wu_src[:, :PASS])
         for q in range(QUADRANTS):
             nc.sync.dma_start(
                 wus_raw[32 * q : 32 * q + 4 * HB, :].bitcast(I32),
                 wu_scales[0, 4 * q : 4 * q + 4, :].bitcast(I32).rearrange("r (b n) -> b r n", b=HB),
             )
-        wu_src = wu_words[0].rearrange("p r i -> p (r i)").bitcast(I32)
-        for b in range(HB):
-            nc.sync.dma_start(wu_raw[b][:], wu_src[:, b * PASS : (b + 1) * PASS])
+        nc.sync.dma_start(wu_raw[1][:], wu_src[:, PASS:])
 
         wd8_raw = keep.tile([P, HB * N], I32, name="wd8_raw", tag="wd8_raw", align_bytes=64)
         wd4_raw = keep.tile([P, HB * N // 2], I32, name="wd4_raw", align_bytes=64)
@@ -83,13 +83,12 @@ def tile_list_modp_relu2_res_noneP_kernel(
 
         windows = []
 
-        def clear_window(tag):
+        def clear_window(tag, engine=nc.gpsimd):
             window = keep.tile([P, T], F32, name="window", tag=tag, align_bytes=64)
-            nc.vector.memset(window[:].bitcast(I32), 0)
+            engine.memset(window[:].bitcast(I32), 0)
             windows.append(window)
 
-        clear_window("window0")
-        clear_window("window1")
+        clear_window("window0", nc.vector)
 
         def entries(first, width):
             return offsets[:, first // 16 : (first + width) // 16]
@@ -135,31 +134,34 @@ def tile_list_modp_relu2_res_noneP_kernel(
             )
             signs.append(sign_b)
 
-        g_rest = keep.tile([P, J - CHUNK], I32, name="g_rest", tag="wu_raw0", align_bytes=64)
-        nc.vector.tensor_copy(g_rest[:].bitcast(U32), tab_w[:].bitcast(U32).indirect(entries(CHUNK, J - CHUNK)))
+        g_second = keep.tile([P, CHUNK], I32, name="g_second", tag="wu_raw0", align_bytes=64)
+        nc.vector.tensor_copy(g_second[:].bitcast(U32), tab_w[:].bitcast(U32).indirect(entries(CHUNK, CHUNK)))
+        picked = [g_first[:], g_second[:]]
         clear_window("wu_raw1")
 
-        wd8_w = keep.tile([P, HB * N], I32, name="wd8_w", align_bytes=64)
-        wd4_w = keep.tile([P, HB * N * 2], U8, name="wd4_w", align_bytes=64)
-        wd_s = keep.tile([P, HB * N], U8, name="wd_s", align_bytes=64)
-        nc.vector.tensor_copy(
-            wd8_w[:].rearrange("p (a t m) -> p a m t", a=HB, t=PACK),
-            wd8_raw[:].rearrange("p (a m t) -> p a m t", a=HB, t=PACK),
-        )
-        nc.vector.tensor_copy(
-            wd4_w[:].bitcast(U16).rearrange("p (a t m) -> p a t m", a=HB, t=PACK),
-            wd4_raw[:].bitcast(U16).rearrange("p (a m t) -> p a t m", a=HB, t=PACK),
-        )
-        nc.vector.tensor_copy(
-            wd_s[:].rearrange("p (a t m) -> p a t m", a=HB, t=PACK), wds_raw[:].rearrange("p (a m t) -> p a t m", a=HB, t=PACK)
-        )
+        def deal_wd():
+            wd8_w = keep.tile([P, HB * N], I32, name="wd8_w", tag="square0_0", align_bytes=64)
+            wd4_w = keep.tile([P, HB * N * 2], U8, name="wd4_w", tag="relu0_0", align_bytes=64)
+            wd_s = keep.tile([P, HB * N], U8, name="wd_s", tag="signed0_0", align_bytes=64)
+            nc.vector.tensor_copy(
+                wd8_w[:].rearrange("p (a t m) -> p a m t", a=HB, t=PACK),
+                wd8_raw[:].rearrange("p (a m t) -> p a m t", a=HB, t=PACK),
+            )
+            nc.vector.tensor_copy(
+                wd4_w[:].bitcast(U16).rearrange("p (a t m) -> p a t m", a=HB, t=PACK),
+                wd4_raw[:].bitcast(U16).rearrange("p (a m t) -> p a t m", a=HB, t=PACK),
+            )
+            nc.vector.tensor_copy(
+                wd_s[:].rearrange("p (a t m) -> p a t m", a=HB, t=PACK), wds_raw[:].rearrange("p (a m t) -> p a t m", a=HB, t=PACK)
+            )
+            return wd8_w, wd4_w, wd_s
 
         h_w = [keep.tile([P, J], U32, name="h_w%d" % b, align_bytes=64) for b in range(HB)]
         h_s = [keep.tile([P, J], U8, name="h_s%d" % b, align_bytes=64) for b in range(HB)]
         relus = {}
 
         def rectify(c, b):
-            words = g_first[:] if c == 0 else g_rest[:, (c - 1) * CHUNK : c * CHUNK]
+            words = picked[c]
             relu = keep.tile([P, PACK, CHUNK], F32, name="relu", tag="relu%d_%d" % (c, b), align_bytes=64)
             for t in range(PACK):
                 acc = psum.tile([P, CHUNK], F32, name="acc_a", tag="acc_a")
@@ -223,47 +225,81 @@ def tile_list_modp_relu2_res_noneP_kernel(
         def scatter(y, t, first, width):
             nc.vector.tensor_tensor(windows[t][:].indirect(entries(first, width)), y, wgo_t[:, first : first + width], ALU.mult)
 
-        def put(c, t, tag):
-            y = keep.tile([P, CHUNK], F32, name="y", tag=tag, align_bytes=64)
-            project(y[:], t, c * CHUNK, CHUNK)
-            scatter(y[:], t, c * CHUNK, CHUNK)
+        def put(y, t, first, width):
+            for j0 in range(0, width, BANK):
+                part = min(BANK, width - j0)
+                project(y[:, j0 : j0 + part], t, first + j0, part)
+            scatter(y, t, first, width)
+
+        def staging(width, tag):
+            return keep.tile([P, width], F32, name="y", tag=tag, align_bytes=64)
+
+        def make_hidden(c, b):
+            rectify(c, b)
+            quantise(c, b)
+
+        def make_hidden_on_vector(c, b):
+            scaled = keep.tile([P, CHUNK * PACK], F32, name="scaled", align_bytes=64)
+            rounded_h = keep.tile([P, CHUNK * PACK], BF16, name="rounded_h", align_bytes=64)
+            factor = sm_t[:, b * PACK : (b + 1) * PACK].unsqueeze(1).to_broadcast([P, half, PACK])
+            sums = []
+            for j0 in (0, half):
+                acc = psum.tile([P, PACK, half], F32, name="acc_v", tag="acc_a")
+                for t in range(PACK):
+                    nc.tensor.matmul_mx(
+                        out=acc[:, t, :],
+                        lhsT=wu_w[b][:, t * P : (t + 1) * P].bitcast(FP8X4),
+                        lhsT_scale=wu_s[4 * b :, t * P : (t + 1) * P],
+                        rhs=picked[c][:, j0 : j0 + half].bitcast(FP8X4),
+                        rhs_scale=g_s[:, c * CHUNK + j0 : c * CHUNK + j0 + half],
+                        start=True,
+                        stop=True,
+                    )
+                sums.append(acc[:].rearrange("p t c -> p c t"))
+            parts = [slice(j0 * PACK, (j0 + half) * PACK) for j0 in (0, half)]
+            for a, part in zip(sums, parts):
+                nc.vector.tensor_tensor(scaled[:, part].rearrange("p (c t) -> p c t", t=PACK), a, factor, ALU.mult)
+            for a, part in zip(sums, parts):
+                nc.vector.scalar_tensor_tensor(
+                    rounded_h[:, part].rearrange("p (c t) -> p c t", t=PACK),
+                    a,
+                    0.0,
+                    scaled[:, part].rearrange("p (c t) -> p c t", t=PACK),
+                    ALU.max,
+                    ALU.mult,
+                )
+            for j0, part in zip((0, half), parts):
+                cols = slice(c * CHUNK + j0, c * CHUNK + j0 + half)
+                nc.vector.quantize_mx(out=h_w[b][:, cols].bitcast(FP8X4), scales=h_s[b][:, cols], in_=rounded_h[:, part])
 
         rectify(0, 0)
+        make_hidden_on_vector(0, 1)
         quantise(0, 0)
-        rectify(0, 1)
-        quantise(0, 1)
-        clear_window("wd8_raw")
-        rectify(1, 0)
-        put(0, 0, "y0_0")
-        quantise(1, 0)
+        wd8_w, wd4_w, wd_s = deal_wd()
+        g_rest = keep.tile([P, 2 * CHUNK], I32, name="g_rest", tag="wds_raw", align_bytes=64)
+        nc.vector.tensor_copy(g_rest[:].bitcast(U32), tab_w[:].bitcast(U32).indirect(entries(2 * CHUNK, 2 * CHUNK)))
+        picked.extend([g_rest[:, :CHUNK], g_rest[:, CHUNK:]])
+        make_hidden(1, 0)
+        clear_window("signed1_0")
         rectify(1, 1)
-        put(0, 1, "relu1_0")
-        put(0, 2, "y0_2")
+        put(staging(CHUNK, "y_first")[:], 0, 0, CHUNK)
         quantise(1, 1)
-        rectify(2, 0)
-        put(0, 3, "relu1_1")
-        quantise(2, 0)
-        rectify(2, 1)
-        put(1, 0, "relu2_0")
-        quantise(2, 1)
-        rectify(3, 0)
-        put(1, 1, "relu2_1")
-        quantise(3, 0)
-        rectify(3, 1)
-        put(2, 0, "relu3_0")
-        quantise(3, 1)
-        put(2, 1, "relu3_1")
-        rest = J - CHUNK
-        y2 = keep.tile([P, rest], F32, name="y2", tag="relu3_0", align_bytes=64)
-        project(y2[:, :BANK], 2, CHUNK, BANK)
-        put(3, 0, "y3_0")
-        put(3, 1, "y3_1")
-        project(y2[:, BANK:], 2, CHUNK + BANK, CHUNK)
-        scatter(y2[:], 2, CHUNK, rest)
-        y3 = keep.tile([P, rest], F32, name="y3", tag="relu3_1", align_bytes=64)
-        project(y3[:, :BANK], 3, CHUNK, BANK)
-        project(y3[:, BANK:], 3, CHUNK + BANK, CHUNK)
-        scatter(y3[:], 3, CHUNK, rest)
+        clear_window("signed1_1")
+        y = staging(2 * CHUNK, "relu1_1")
+        put(y[:, :CHUNK], 1, 0, CHUNK)
+        put(y[:, CHUNK:], 2, 0, CHUNK)
+        make_hidden(2, 0)
+        make_hidden(2, 1)
+        put(staging(CHUNK, "relu2_1")[:], 3, 0, CHUNK)
+        make_hidden(3, 0)
+        put(staging(2 * CHUNK, "relu3_0")[:], 0, CHUNK, 2 * CHUNK)
+        make_hidden(3, 1)
+        y = staging(J, "relu3_1")
+        put(y[:, :CHUNK], 1, CHUNK, CHUNK)
+        put(staging(CHUNK, "y_first")[:], 0, 3 * CHUNK, CHUNK)
+        put(staging(2 * CHUNK, "relu1_1")[:], 1, 2 * CHUNK, 2 * CHUNK)
+        put(y[:, CHUNK:], 2, CHUNK, 3 * CHUNK)
+        put(staging(3 * CHUNK, "relu3_0")[:], 3, CHUNK, 3 * CHUNK)
 
         rows = out_0.rearrange("(p t) c -> p t c", t=PACK)
         widths = TAIL_VECTOR + TAIL_SCALAR

@@ -26,7 +26,6 @@ CHUNK = 256
 CHUNKS = J // CHUNK
 TAIL_VECTOR = (512, 512)
 TAIL_SCALAR = (512, 256, 256)
-TINY = 2.0 ** -100
 
 
 def tile_list_modp_relu2_res_noneP_kernel(
@@ -36,23 +35,23 @@ def tile_list_modp_relu2_res_noneP_kernel(
     nc = tc.nc
     with ExitStack() as ctx:
         keep = ctx.enter_context(tc.tile_pool(name="keep", bufs=1))
-        psum = ctx.enter_context(tc.psum_pool(name="psum", bufs=4))
+        psum = ctx.enter_context(tc.psum_pool(name="psum", bufs=1))
 
         offsets = keep.tile([P, J // 16], U16, name="offsets")
         tab_w = keep.tile([P, T], I32, name="tab_w", align_bytes=64)
         tab_s = keep.tile([P, T], U8, name="tab_s", align_bytes=64)
         wu_raw = [keep.tile([P, PASS], I32, name="wu_raw", tag="wu_raw%d" % b, align_bytes=64) for b in range(HB)]
-        wus_raw = keep.tile([P, PASS], U8, name="wus_raw", align_bytes=64)
+        wus_raw = keep.tile([P, PASS], U8, name="wus_raw", tag="wus_raw", align_bytes=64)
         sm_t = keep.tile([P, HB * PACK], F32, name="sm_t")
         wds_raw = keep.tile([P, HB * N], U8, name="wds_raw", tag="wds_raw", align_bytes=64)
 
+        nc.gpsimd.memset(tab_s[:].bitcast(I32), 0)
         nc.gpsimd.memset(wus_raw[:].bitcast(I32), 0)
         nc.gpsimd.memset(wds_raw[:].bitcast(I32), 0)
 
         for q in range(QUADRANTS):
             nc.sync.dma_start(
-                tab_s[32 * q : 32 * q + 32, :].bitcast(I32),
-                tab_scales[0, 4 * q : 4 * q + 4, :].bitcast(I32).unsqueeze(0).to_broadcast([8, 4, T // 4]),
+                tab_s[32 * q : 32 * q + 4, :].bitcast(I32), tab_scales[0, 4 * q : 4 * q + 4, :].bitcast(I32)
             )
         nc.sync.dma_start(offsets[:], offs)
         nc.sync.dma_start(sm_t[:].rearrange("p (b t) -> p b t", t=PACK), sm.rearrange("(b p t) -> p b t", p=P, t=PACK))
@@ -89,22 +88,21 @@ def tile_list_modp_relu2_res_noneP_kernel(
             windows.append(window)
 
         clear_window("window0", nc.vector)
+        clear_window("window1", nc.vector)
 
         def entries(first, width):
             return offsets[:, first // 16 : (first + width) // 16]
 
-        g_s = keep.tile([P, J], U8, name="g_s", align_bytes=64)
-        nc.vector.tensor_copy(g_s[:], tab_s[:].indirect(offsets[:]))
+        gs_first = keep.tile([P, CHUNK], U8, name="gs_first", align_bytes=64)
+        nc.vector.tensor_copy(gs_first[:], tab_s[:].indirect(entries(0, CHUNK)))
+        picked_s = [gs_first[:]]
 
-        mag = keep.tile([P, HB * PACK], F32, name="mag", tag="sign0", align_bytes=64)
-        magc = keep.tile([P, HB * PACK], F32, name="magc")
-        root0 = keep.tile([P, HB * PACK], F32, name="root0", tag="sign1", align_bytes=64)
-        rinv = keep.tile([P, HB * PACK], F32, name="rinv")
-        quot = keep.tile([P, HB * PACK], F32, name="quot")
+        mag = keep.tile([P, HB * PACK], F32, name="mag")
+        power = keep.tile([P, HB * PACK], F32, name="power")
         root = keep.tile([P, HB * PACK], F32, name="root")
-        nc.vector.scalar_tensor_tensor(mag[:], sm_t[:], -1.0, sm_t[:], ALU.mult, ALU.max)
-        nc.vector.tensor_scalar(magc[:], mag[:], TINY, None, ALU.max)
-        nc.scalar.activation(root0[:], magc[:], ACT.Sqrt)
+        nc.gpsimd.memset(power[:], 0.5)
+        nc.scalar.activation(mag[:], sm_t[:], ACT.Abs)
+        nc.gpsimd.tensor_tensor(root[:], mag[:], power[:], ALU.pow)
 
         g_first = keep.tile([P, CHUNK], I32, name="g_first", align_bytes=64)
         nc.vector.tensor_copy(g_first[:].bitcast(U32), tab_w[:].bitcast(U32).indirect(entries(0, CHUNK)))
@@ -117,13 +115,10 @@ def tile_list_modp_relu2_res_noneP_kernel(
                 wu_w[b][:].rearrange("p (t m) -> p m t", t=PACK), wu_raw[b][:].rearrange("p (m t) -> p m t", t=PACK)
             )
 
-        nc.vector.reciprocal(rinv[:], root0[:])
         nc.vector.tensor_copy(
             wu_s[:].rearrange("p (t m) -> p t m", t=PACK), wus_raw[:].rearrange("p (m t) -> p t m", t=PACK)
         )
-        nc.vector.tensor_tensor(quot[:], magc[:], rinv[:], ALU.mult)
         deal_wu(0)
-        nc.vector.tensor_tensor(root[:], quot[:], root0[:], ALU.add)
         deal_wu(1)
         half = CHUNK // 2
         signs = []
@@ -134,10 +129,12 @@ def tile_list_modp_relu2_res_noneP_kernel(
             )
             signs.append(sign_b)
 
-        g_second = keep.tile([P, CHUNK], I32, name="g_second", tag="wu_raw0", align_bytes=64)
+        g_second = keep.tile([P, CHUNK], I32, name="g_second", tag="wus_raw", align_bytes=64)
         nc.vector.tensor_copy(g_second[:].bitcast(U32), tab_w[:].bitcast(U32).indirect(entries(CHUNK, CHUNK)))
         picked = [g_first[:], g_second[:]]
-        clear_window("wu_raw1")
+        gs_rest = keep.tile([P, J - CHUNK], U8, name="gs_rest", tag="wu_raw1", align_bytes=64)
+        nc.vector.tensor_copy(gs_rest[:], tab_s[:].indirect(entries(CHUNK, J - CHUNK)))
+        picked_s.extend([gs_rest[:, c * CHUNK : (c + 1) * CHUNK] for c in range(CHUNKS - 1)])
 
         def deal_wd():
             wd8_w = keep.tile([P, HB * N], I32, name="wd8_w", tag="square0_0", align_bytes=64)
@@ -159,18 +156,19 @@ def tile_list_modp_relu2_res_noneP_kernel(
         h_w = [keep.tile([P, J], U32, name="h_w%d" % b, align_bytes=64) for b in range(HB)]
         h_s = [keep.tile([P, J], U8, name="h_s%d" % b, align_bytes=64) for b in range(HB)]
         relus = {}
+        projected = []
 
-        def rectify(c, b):
+        def rectify(c, b, first_bank=0):
             words = picked[c]
             relu = keep.tile([P, PACK, CHUNK], F32, name="relu", tag="relu%d_%d" % (c, b), align_bytes=64)
             for t in range(PACK):
-                acc = psum.tile([P, CHUNK], F32, name="acc_a", tag="acc_a")
+                acc = psum.tile([P, CHUNK], F32, name="acc_a", tag="bank%d" % (first_bank + t))
                 nc.tensor.matmul_mx(
                     out=acc[:],
                     lhsT=wu_w[b][:, t * P : (t + 1) * P].bitcast(FP8X4),
                     lhsT_scale=wu_s[4 * b :, t * P : (t + 1) * P],
                     rhs=words.bitcast(FP8X4),
-                    rhs_scale=g_s[:, c * CHUNK : (c + 1) * CHUNK],
+                    rhs_scale=picked_s[c],
                     start=True,
                     stop=True,
                 )
@@ -184,7 +182,6 @@ def tile_list_modp_relu2_res_noneP_kernel(
                 square[:].rearrange("p (c t) -> p c t", t=PACK),
                 relus[(c, b)][:].rearrange("p t c -> p c t"),
                 ACT.Square,
-                scale=0.5,
             )
             signed = keep.tile([P, CHUNK * PACK], BF16, name="signed", tag="signed%d_%d" % (c, b), align_bytes=64)
             sign = signs[b][:].rearrange("p c t -> p (c t)")
@@ -197,7 +194,8 @@ def tile_list_modp_relu2_res_noneP_kernel(
                 nc.vector.quantize_mx(out=h_w[b][:, cols].bitcast(FP8X4), scales=h_s[b][:, cols], in_=signed[:, part])
 
         def project(y, t, first, width):
-            acc = psum.tile([P, width], F32, name="acc_y", tag="acc_y")
+            acc = psum.tile([P, width], F32, name="acc_y", tag="bank%d" % (PACK + len(projected) % PACK))
+            projected.append(t)
             narrow = width if width == BANK else P
             for b in range(HB):
                 col = b * N + t * P
@@ -244,14 +242,14 @@ def tile_list_modp_relu2_res_noneP_kernel(
             factor = sm_t[:, b * PACK : (b + 1) * PACK].unsqueeze(1).to_broadcast([P, half, PACK])
             sums = []
             for j0 in (0, half):
-                acc = psum.tile([P, PACK, half], F32, name="acc_v", tag="acc_a")
+                acc = psum.tile([P, PACK, half], F32, name="acc_v", tag="bank%d" % (PACK + len(sums)))
                 for t in range(PACK):
                     nc.tensor.matmul_mx(
                         out=acc[:, t, :],
                         lhsT=wu_w[b][:, t * P : (t + 1) * P].bitcast(FP8X4),
                         lhsT_scale=wu_s[4 * b :, t * P : (t + 1) * P],
                         rhs=picked[c][:, j0 : j0 + half].bitcast(FP8X4),
-                        rhs_scale=g_s[:, c * CHUNK + j0 : c * CHUNK + j0 + half],
+                        rhs_scale=picked_s[c][:, j0 : j0 + half],
                         start=True,
                         stop=True,
                     )
@@ -280,24 +278,26 @@ def tile_list_modp_relu2_res_noneP_kernel(
         nc.vector.tensor_copy(g_rest[:].bitcast(U32), tab_w[:].bitcast(U32).indirect(entries(2 * CHUNK, 2 * CHUNK)))
         picked.extend([g_rest[:, :CHUNK], g_rest[:, CHUNK:]])
         make_hidden(1, 0)
-        clear_window("signed1_0")
-        rectify(1, 1)
-        put(staging(CHUNK, "y_first")[:], 0, 0, CHUNK)
+        rectify(1, 1, PACK)
         quantise(1, 1)
         clear_window("signed1_1")
         y = staging(2 * CHUNK, "relu1_1")
-        put(y[:, :CHUNK], 1, 0, CHUNK)
-        put(y[:, CHUNK:], 2, 0, CHUNK)
+        put(y[:, :CHUNK], 0, 0, CHUNK)
+        put(y[:, CHUNK:], 1, 0, CHUNK)
         make_hidden(2, 0)
+        clear_window("signed2_0")
+        put(staging(CHUNK, "relu2_0")[:], 2, 0, CHUNK)
         make_hidden(2, 1)
-        put(staging(CHUNK, "relu2_1")[:], 3, 0, CHUNK)
+        y = staging(2 * CHUNK, "relu2_1")
+        put(y[:, :CHUNK], 3, 0, CHUNK)
+        put(y[:, CHUNK:], 0, CHUNK, CHUNK)
         make_hidden(3, 0)
-        put(staging(2 * CHUNK, "relu3_0")[:], 0, CHUNK, 2 * CHUNK)
+        put(staging(CHUNK, "relu3_0")[:], 0, 2 * CHUNK, CHUNK)
         make_hidden(3, 1)
         y = staging(J, "relu3_1")
         put(y[:, :CHUNK], 1, CHUNK, CHUNK)
-        put(staging(CHUNK, "y_first")[:], 0, 3 * CHUNK, CHUNK)
-        put(staging(2 * CHUNK, "relu1_1")[:], 1, 2 * CHUNK, 2 * CHUNK)
+        put(staging(CHUNK, "relu1_1")[:], 0, 3 * CHUNK, CHUNK)
+        put(staging(2 * CHUNK, "relu2_0")[:], 1, 2 * CHUNK, 2 * CHUNK)
         put(y[:, CHUNK:], 2, CHUNK, 3 * CHUNK)
         put(staging(3 * CHUNK, "relu3_0")[:], 3, CHUNK, 3 * CHUNK)
 

@@ -24,8 +24,9 @@ QUADRANTS = 4
 BANK = 512
 CHUNK = 256
 CHUNKS = J // CHUNK
-TAIL_VECTOR = (512, 512)
-TAIL_SCALAR = (512, 256, 256)
+TAIL_VECTOR = (384, 512)
+TAIL_SCALAR = (512, 384, 256)
+TINY = 2.0 ** -100
 
 
 def tile_list_modp_relu2_res_noneP_kernel(
@@ -38,7 +39,7 @@ def tile_list_modp_relu2_res_noneP_kernel(
         psum = ctx.enter_context(tc.psum_pool(name="psum", bufs=1))
 
         offsets = keep.tile([P, J // 16], U16, name="offsets")
-        tab_w = keep.tile([P, T], I32, name="tab_w", align_bytes=64)
+        tab_w = keep.tile([P, T], I32, name="tab_w", tag="tab_w", align_bytes=64)
         tab_s = keep.tile([P, T], U8, name="tab_s", align_bytes=64)
         wu_raw = [keep.tile([P, PASS], I32, name="wu_raw", tag="wu_raw%d" % b, align_bytes=64) for b in range(HB)]
         wus_raw = keep.tile([P, PASS], U8, name="wus_raw", tag="wus_raw", align_bytes=64)
@@ -88,21 +89,23 @@ def tile_list_modp_relu2_res_noneP_kernel(
             windows.append(window)
 
         clear_window("window0", nc.vector)
-        clear_window("window1", nc.vector)
 
         def entries(first, width):
             return offsets[:, first // 16 : (first + width) // 16]
 
-        gs_first = keep.tile([P, CHUNK], U8, name="gs_first", align_bytes=64)
-        nc.vector.tensor_copy(gs_first[:], tab_s[:].indirect(entries(0, CHUNK)))
-        picked_s = [gs_first[:]]
+        g_s = keep.tile([P, J], U8, name="g_s", align_bytes=64)
+        nc.vector.tensor_copy(g_s[:], tab_s[:].indirect(offsets[:]))
+        picked_s = [g_s[:, c * CHUNK : (c + 1) * CHUNK] for c in range(CHUNKS)]
 
-        mag = keep.tile([P, HB * PACK], F32, name="mag")
-        power = keep.tile([P, HB * PACK], F32, name="power")
+        mag = keep.tile([P, HB * PACK], F32, name="mag", tag="sign0", align_bytes=64)
+        magc = keep.tile([P, HB * PACK], F32, name="magc")
+        root0 = keep.tile([P, HB * PACK], F32, name="root0", tag="sign1", align_bytes=64)
+        rinv = keep.tile([P, HB * PACK], F32, name="rinv")
+        quot = keep.tile([P, HB * PACK], F32, name="quot")
         root = keep.tile([P, HB * PACK], F32, name="root")
-        nc.gpsimd.memset(power[:], 0.5)
-        nc.scalar.activation(mag[:], sm_t[:], ACT.Abs)
-        nc.gpsimd.tensor_tensor(root[:], mag[:], power[:], ALU.pow)
+        nc.vector.scalar_tensor_tensor(mag[:], sm_t[:], -1.0, sm_t[:], ALU.mult, ALU.max)
+        nc.vector.tensor_scalar(magc[:], mag[:], TINY, None, ALU.max)
+        nc.scalar.activation(root0[:], magc[:], ACT.Sqrt)
 
         g_first = keep.tile([P, CHUNK], I32, name="g_first", align_bytes=64)
         nc.vector.tensor_copy(g_first[:].bitcast(U32), tab_w[:].bitcast(U32).indirect(entries(0, CHUNK)))
@@ -115,10 +118,13 @@ def tile_list_modp_relu2_res_noneP_kernel(
                 wu_w[b][:].rearrange("p (t m) -> p m t", t=PACK), wu_raw[b][:].rearrange("p (m t) -> p m t", t=PACK)
             )
 
+        nc.vector.reciprocal(rinv[:], root0[:])
+        deal_wu(0)
+        nc.vector.tensor_tensor(quot[:], magc[:], rinv[:], ALU.mult)
         nc.vector.tensor_copy(
             wu_s[:].rearrange("p (t m) -> p t m", t=PACK), wus_raw[:].rearrange("p (m t) -> p t m", t=PACK)
         )
-        deal_wu(0)
+        nc.vector.tensor_tensor(root[:], quot[:], root0[:], ALU.add)
         deal_wu(1)
         half = CHUNK // 2
         signs = []
@@ -129,29 +135,27 @@ def tile_list_modp_relu2_res_noneP_kernel(
             )
             signs.append(sign_b)
 
-        g_second = keep.tile([P, CHUNK], I32, name="g_second", tag="wus_raw", align_bytes=64)
-        nc.vector.tensor_copy(g_second[:].bitcast(U32), tab_w[:].bitcast(U32).indirect(entries(CHUNK, CHUNK)))
-        picked = [g_first[:], g_second[:]]
-        gs_rest = keep.tile([P, J - CHUNK], U8, name="gs_rest", tag="wu_raw1", align_bytes=64)
-        nc.vector.tensor_copy(gs_rest[:], tab_s[:].indirect(entries(CHUNK, J - CHUNK)))
-        picked_s.extend([gs_rest[:, c * CHUNK : (c + 1) * CHUNK] for c in range(CHUNKS - 1)])
+        g_rest = keep.tile([P, J - CHUNK], I32, name="g_rest", tag="wus_raw", align_bytes=64)
+        nc.vector.tensor_copy(g_rest[:].bitcast(U32), tab_w[:].bitcast(U32).indirect(entries(CHUNK, J - CHUNK)))
+        picked = [g_first[:]] + [g_rest[:, c * CHUNK : (c + 1) * CHUNK] for c in range(CHUNKS - 1)]
+        clear_window("tab_w")
 
-        def deal_wd():
-            wd8_w = keep.tile([P, HB * N], I32, name="wd8_w", tag="square0_0", align_bytes=64)
-            wd4_w = keep.tile([P, HB * N * 2], U8, name="wd4_w", tag="relu0_0", align_bytes=64)
-            wd_s = keep.tile([P, HB * N], U8, name="wd_s", tag="signed0_0", align_bytes=64)
-            nc.vector.tensor_copy(
-                wd8_w[:].rearrange("p (a t m) -> p a m t", a=HB, t=PACK),
-                wd8_raw[:].rearrange("p (a m t) -> p a m t", a=HB, t=PACK),
-            )
-            nc.vector.tensor_copy(
-                wd4_w[:].bitcast(U16).rearrange("p (a t m) -> p a t m", a=HB, t=PACK),
-                wd4_raw[:].bitcast(U16).rearrange("p (a m t) -> p a t m", a=HB, t=PACK),
-            )
-            nc.vector.tensor_copy(
-                wd_s[:].rearrange("p (a t m) -> p a t m", a=HB, t=PACK), wds_raw[:].rearrange("p (a m t) -> p a t m", a=HB, t=PACK)
-            )
-            return wd8_w, wd4_w, wd_s
+        dealt = {}
+
+        def deal_wd(first, count, tags):
+            w8 = keep.tile([P, HB, count, P], I32, name="wd8_w", tag=tags[0], align_bytes=64)
+            w4 = keep.tile([P, HB * count * P * 2], U8, name="wd4_w", tag=tags[1], align_bytes=64)
+            ws = keep.tile([P, HB, count, P], U8, name="wd_s", tag=tags[2], align_bytes=64)
+            for raw, out in (
+                (wd8_raw[:], w8[:]),
+                (wd4_raw[:].bitcast(U16), w4[:].bitcast(U16).rearrange("p (a t m) -> p a t m", a=HB, t=count)),
+                (wds_raw[:], ws[:]),
+            ):
+                nc.vector.tensor_copy(out, raw.rearrange("p (a m t) -> p a t m", a=HB, t=PACK)[:, :, first : first + count, :])
+            for i in range(count):
+                for b in range(HB):
+                    col = (b * count + i) * P
+                    dealt[(b, first + i)] = (w8[:, b, i, :], w4[:, 2 * col : 2 * (col + P)], ws[:, b, i, :], ws[4:, b, i, :])
 
         h_w = [keep.tile([P, J], U32, name="h_w%d" % b, align_bytes=64) for b in range(HB)]
         h_s = [keep.tile([P, J], U8, name="h_s%d" % b, align_bytes=64) for b in range(HB)]
@@ -182,6 +186,7 @@ def tile_list_modp_relu2_res_noneP_kernel(
                 square[:].rearrange("p (c t) -> p c t", t=PACK),
                 relus[(c, b)][:].rearrange("p t c -> p c t"),
                 ACT.Square,
+                scale=0.5,
             )
             signed = keep.tile([P, CHUNK * PACK], BF16, name="signed", tag="signed%d_%d" % (c, b), align_bytes=64)
             sign = signs[b][:].rearrange("p c t -> p (c t)")
@@ -198,11 +203,11 @@ def tile_list_modp_relu2_res_noneP_kernel(
             projected.append(t)
             narrow = width if width == BANK else P
             for b in range(HB):
-                col = b * N + t * P
+                w8, w4, scale4, scale8 = dealt[(b, t)]
                 nc.tensor.matmul_mx(
                     out=acc[:],
-                    lhsT=wd8_w[:, col : col + P].bitcast(FP8X4),
-                    lhsT_scale=wd_s[4:, col : col + P],
+                    lhsT=w8.bitcast(FP8X4),
+                    lhsT_scale=scale8,
                     rhs=h_w[b][:, first : first + width].bitcast(FP8X4),
                     rhs_scale=h_s[b][:, first : first + width],
                     start=(b == 0),
@@ -211,8 +216,8 @@ def tile_list_modp_relu2_res_noneP_kernel(
                 for j0 in range(0, width, narrow):
                     nc.tensor.matmul_mx(
                         out=acc[:, j0 : j0 + narrow],
-                        lhsT=wd4_w[:, 2 * col : 2 * (col + P)].bitcast(FP4X4),
-                        lhsT_scale=wd_s[:, col : col + P],
+                        lhsT=w4.bitcast(FP4X4),
+                        lhsT_scale=scale4,
                         rhs=h_w[b][:, first + j0 : first + j0 + narrow].bitcast(FP8X4),
                         rhs_scale=h_s[b][:, first + j0 : first + j0 + narrow],
                         start=False,
@@ -237,8 +242,8 @@ def tile_list_modp_relu2_res_noneP_kernel(
             quantise(c, b)
 
         def make_hidden_on_vector(c, b):
-            scaled = keep.tile([P, CHUNK * PACK], F32, name="scaled", align_bytes=64)
-            rounded_h = keep.tile([P, CHUNK * PACK], BF16, name="rounded_h", align_bytes=64)
+            scaled = keep.tile([P, CHUNK * PACK], F32, name="scaled", tag="scaled", align_bytes=64)
+            rounded_h = keep.tile([P, CHUNK * PACK], BF16, name="rounded_h", tag="rounded_h", align_bytes=64)
             factor = sm_t[:, b * PACK : (b + 1) * PACK].unsqueeze(1).to_broadcast([P, half, PACK])
             sums = []
             for j0 in (0, half):
@@ -273,74 +278,87 @@ def tile_list_modp_relu2_res_noneP_kernel(
         rectify(0, 0)
         make_hidden_on_vector(0, 1)
         quantise(0, 0)
-        wd8_w, wd4_w, wd_s = deal_wd()
-        g_rest = keep.tile([P, 2 * CHUNK], I32, name="g_rest", tag="wds_raw", align_bytes=64)
-        nc.vector.tensor_copy(g_rest[:].bitcast(U32), tab_w[:].bitcast(U32).indirect(entries(2 * CHUNK, 2 * CHUNK)))
-        picked.extend([g_rest[:, :CHUNK], g_rest[:, CHUNK:]])
+        deal_wd(0, 1, ("square0_0", "relu0_0", "signed0_0"))
+        deal_wd(1, PACK - 1, ("rounded_h", "scaled", "wd_s_rest"))
+        def put_two(first, second, tag):
+            y = staging(2 * CHUNK, tag)
+            for i, (c, t) in enumerate((first, second)):
+                put(y[:, i * CHUNK : (i + 1) * CHUNK], t, c * CHUNK, CHUNK)
+
         make_hidden(1, 0)
         rectify(1, 1, PACK)
+        put(staging(CHUNK, "y_first")[:], 0, 0, CHUNK)
         quantise(1, 1)
         clear_window("signed1_1")
-        y = staging(2 * CHUNK, "relu1_1")
-        put(y[:, :CHUNK], 0, 0, CHUNK)
-        put(y[:, CHUNK:], 1, 0, CHUNK)
-        make_hidden(2, 0)
+        rectify(2, 0)
+        put_two((0, 1), (1, 0), "relu1_1")
+        quantise(2, 0)
         clear_window("signed2_0")
-        put(staging(CHUNK, "relu2_0")[:], 2, 0, CHUNK)
-        make_hidden(2, 1)
-        y = staging(2 * CHUNK, "relu2_1")
-        put(y[:, :CHUNK], 3, 0, CHUNK)
-        put(y[:, CHUNK:], 0, CHUNK, CHUNK)
-        make_hidden(3, 0)
+        rectify(2, 1)
+        put_two((0, 2), (1, 1), "relu2_0")
+        quantise(2, 1)
+        rectify(3, 0)
+        put_two((0, 3), (1, 2), "relu2_1")
+        quantise(3, 0)
+        rectify(3, 1)
         put(staging(CHUNK, "relu3_0")[:], 0, 2 * CHUNK, CHUNK)
-        make_hidden(3, 1)
-        y = staging(J, "relu3_1")
-        put(y[:, :CHUNK], 1, CHUNK, CHUNK)
-        put(staging(CHUNK, "relu1_1")[:], 0, 3 * CHUNK, CHUNK)
-        put(staging(2 * CHUNK, "relu2_0")[:], 1, 2 * CHUNK, 2 * CHUNK)
-        put(y[:, CHUNK:], 2, CHUNK, 3 * CHUNK)
+        quantise(3, 1)
+        put(staging(CHUNK, "relu3_1")[:], 1, 2 * CHUNK, CHUNK)
+        put_two((3, 0), (3, 1), "relu1_1")
+        put(staging(2 * CHUNK, "relu2_0")[:], 2, 2 * CHUNK, 2 * CHUNK)
         put(staging(3 * CHUNK, "relu3_0")[:], 3, CHUNK, 3 * CHUNK)
 
         rows = out_0.rearrange("(p t) c -> p t c", t=PACK)
         widths = TAIL_VECTOR + TAIL_SCALAR
         edges = [sum(widths[:i]) for i in range(len(widths))]
-        pairs = [keep.tile([P, 2, w, 2], BF16, name="pairs%d" % i, align_bytes=64) for i, w in enumerate(widths)]
+        by_vector = range(len(TAIL_VECTOR))
+        by_scalar = range(len(TAIL_VECTOR), len(widths))
+        rounded = [keep.tile([P, PACK * w], BF16, name="rounded%d" % i, align_bytes=64) for i, w in enumerate(widths)]
         grouped = [keep.tile([P, w * PACK], BF16, name="grouped%d" % i, align_bytes=64) for i, w in enumerate(widths)]
         out_s = keep.tile([P, T], U8, name="out_s", align_bytes=64)
         words_out = out_1[0].rearrange("p t i -> p (t i)").bitcast(I32)
 
-        def round_rows(copy, t, i):
-            copy(pairs[i][:, t // 2, :, t % 2], windows[t][:, edges[i] : edges[i] + widths[i]])
+        def round_plane(copy, t, i):
+            w = widths[i]
+            copy(rounded[i][:, t * w : (t + 1) * w], windows[t][:, edges[i] : edges[i] + w])
 
-        def group(copy, word, i):
-            copy(
-                grouped[i][:].bitcast(word).rearrange("p (c u) -> p c u", u=2),
-                pairs[i][:].rearrange("p u c e -> p (u c e)").bitcast(word).rearrange("p (u c) -> p c u", u=2),
-            )
+        def round_pair(t, i):
+            pairs = rounded[i][:].rearrange("p (u c e) -> p u c e", u=2, e=2)
+            nc.scalar.copy(pairs[:, t // 2, :, t % 2], windows[t][:, edges[i] : edges[i] + widths[i]])
 
         def finish(i):
             w = widths[i]
             out_w = keep.tile([P, w], I32, name="out_w%d" % i, align_bytes=64)
-            nc.vector.quantize_mx(out=out_w[:].bitcast(FP8X4), scales=out_s[:, edges[i] : edges[i] + w], in_=grouped[i][:])
+            done = 0
+            while done < w:
+                part = max(n for n in (128, 256, 512) if n <= w - done)
+                nc.vector.quantize_mx(
+                    out=out_w[:, done : done + part].bitcast(FP8X4),
+                    scales=out_s[:, edges[i] + done : edges[i] + done + part],
+                    in_=grouped[i][:, done * PACK : (done + part) * PACK],
+                )
+                done = done + part
             nc.sync.dma_start(words_out[:, edges[i] : edges[i] + w], out_w[:])
 
         for t in range(PACK):
             nc.sync.dma_start(rows[:, t, :], windows[t][:])
             if t < PACK - 1:
-                for i in range(len(widths)):
-                    if t == PACK - 2 and i < len(TAIL_VECTOR):
-                        source = windows[t][:, edges[i] : edges[i] + widths[i]]
-                        nc.scalar.copy(pairs[i][:, 1, :, :], source.unsqueeze(2).to_broadcast([P, widths[i], 2]))
-                    else:
-                        round_rows(nc.scalar.copy, t, i)
-        mine = range(len(TAIL_VECTOR))
-        for i in mine:
-            round_rows(nc.vector.tensor_copy, PACK - 1, i)
-        for i in mine:
-            group(nc.vector.tensor_copy, I32, i)
-        for i in range(len(TAIL_VECTOR), len(widths)):
-            round_rows(nc.scalar.copy, PACK - 1, i)
-            group(nc.scalar.copy, U32, i)
+                for i in by_vector:
+                    round_plane(nc.scalar.copy, t, i)
+                for i in by_scalar:
+                    round_pair(t, i)
+        for i in by_vector:
+            round_plane(nc.vector.tensor_copy, PACK - 1, i)
+        for i in by_vector:
+            nc.vector.tensor_copy(
+                grouped[i][:].rearrange("p (c t) -> p c t", t=PACK), rounded[i][:].rearrange("p (t c) -> p c t", t=PACK)
+            )
+        for i in by_scalar:
+            round_pair(PACK - 1, i)
+            nc.scalar.copy(
+                grouped[i][:].bitcast(U32).rearrange("p (c u) -> p c u", u=2),
+                rounded[i][:].bitcast(U32).rearrange("p (u c) -> p c u", u=2),
+            )
         for i in range(len(widths)):
             finish(i)
         for q in range(QUADRANTS):

@@ -21,9 +21,12 @@ PACK = 4
 PASS = P * PACK
 HB = R // PASS
 QUADRANTS = 4
+LINE = 4
 BANK = 512
 CHUNK = 256
 CHUNKS = J // CHUNK
+HALF = CHUNK // 2
+QUANTISE_WIDTHS = (128, 256, 512)
 TAIL_VECTOR = (384, 512)
 TAIL_SCALAR = (512, 384, 256)
 TINY = 2.0 ** -100
@@ -42,9 +45,9 @@ def tile_list_modp_relu2_res_noneP_kernel(
         tab_w = keep.tile([P, T], I32, name="tab_w", tag="tab_w", align_bytes=64)
         tab_s = keep.tile([P, T], U8, name="tab_s", align_bytes=64)
         wu_raw = [keep.tile([P, PASS], I32, name="wu_raw", tag="wu_raw%d" % b, align_bytes=64) for b in range(HB)]
-        wus_raw = keep.tile([P, PASS], U8, name="wus_raw", tag="wus_raw", align_bytes=64)
+        wus_raw = keep.tile([P, PASS], U8, name="wus_raw", align_bytes=64)
         sm_t = keep.tile([P, HB * PACK], F32, name="sm_t")
-        wds_raw = keep.tile([P, HB * N], U8, name="wds_raw", tag="wds_raw", align_bytes=64)
+        wds_raw = keep.tile([P, HB * N], U8, name="wds_raw", align_bytes=64)
 
         nc.gpsimd.memset(tab_s[:].bitcast(I32), 0)
         nc.gpsimd.memset(wus_raw[:].bitcast(I32), 0)
@@ -66,29 +69,29 @@ def tile_list_modp_relu2_res_noneP_kernel(
             )
         nc.sync.dma_start(wu_raw[1][:], wu_src[:, PASS:])
 
-        wd8_raw = keep.tile([P, HB * N], I32, name="wd8_raw", tag="wd8_raw", align_bytes=64)
+        wd8_raw = keep.tile([P, HB * N], I32, name="wd8_raw", align_bytes=64)
         wd4_raw = keep.tile([P, HB * N // 2], I32, name="wd4_raw", align_bytes=64)
         wgo_t = keep.tile([P, J], F32, name="wgo_t")
         nc.sync.dma_start(
             wd8_raw[:].rearrange("p (a n) -> p a n", a=HB), wd8_words.rearrange("a p n i -> p a (n i)").bitcast(I32)
         )
         nc.sync.dma_start(wd4_raw[:].rearrange("p (a n) -> p a n", a=HB), wd4_words.rearrange("a p n -> p a n").bitcast(I32))
-        for first, planes in ((0, wd4_scales), (4, wd8_scales)):
+        for base, scale_rows in ((0, wd4_scales), (4, wd8_scales)):
             for q in range(QUADRANTS):
                 nc.sync.dma_start(
-                    wds_raw[32 * q + first : 32 * q + first + 4, :].bitcast(I32).rearrange("r (a n) -> r a n", a=HB),
-                    planes[:, 4 * q : 4 * q + 4, :].bitcast(I32).rearrange("a r n -> r a n"),
+                    wds_raw[32 * q + base : 32 * q + base + 4, :].bitcast(I32).rearrange("r (a n) -> r a n", a=HB),
+                    scale_rows[:, 4 * q : 4 * q + 4, :].bitcast(I32).rearrange("a r n -> r a n"),
                 )
         nc.sync.dma_start(wgo_t[:], wgo)
 
         windows = []
 
-        def clear_window(tag, engine=nc.gpsimd):
+        def clear_window(engine, tag):
             window = keep.tile([P, T], F32, name="window", tag=tag, align_bytes=64)
             engine.memset(window[:].bitcast(I32), 0)
             windows.append(window)
 
-        clear_window("window0", nc.vector)
+        clear_window(nc.vector, "window0")
 
         def entries(first, width):
             return offsets[:, first // 16 : (first + width) // 16]
@@ -100,14 +103,14 @@ def tile_list_modp_relu2_res_noneP_kernel(
         mag = keep.tile([P, HB * PACK], F32, name="mag", tag="sign0", align_bytes=64)
         magc = keep.tile([P, HB * PACK], F32, name="magc")
         root0 = keep.tile([P, HB * PACK], F32, name="root0", tag="sign1", align_bytes=64)
-        rinv = keep.tile([P, HB * PACK], F32, name="rinv")
+        rinv = keep.tile([P, HB * PACK], F32, name="rinv", tag="rinv")
         quot = keep.tile([P, HB * PACK], F32, name="quot")
         root = keep.tile([P, HB * PACK], F32, name="root")
         nc.vector.scalar_tensor_tensor(mag[:], sm_t[:], -1.0, sm_t[:], ALU.mult, ALU.max)
         nc.vector.tensor_scalar(magc[:], mag[:], TINY, None, ALU.max)
         nc.scalar.activation(root0[:], magc[:], ACT.Sqrt)
 
-        g_first = keep.tile([P, CHUNK], I32, name="g_first", align_bytes=64)
+        g_first = keep.tile([P, CHUNK], I32, name="g_first", tag="g_first", align_bytes=64)
         nc.vector.tensor_copy(g_first[:].bitcast(U32), tab_w[:].bitcast(U32).indirect(entries(0, CHUNK)))
 
         wu_w = [keep.tile([P, PASS], I32, name="wu_w%d" % b, align_bytes=64) for b in range(HB)]
@@ -126,36 +129,41 @@ def tile_list_modp_relu2_res_noneP_kernel(
         )
         nc.vector.tensor_tensor(root[:], quot[:], root0[:], ALU.add)
         deal_wu(1)
-        half = CHUNK // 2
+
         signs = []
         for b in range(HB):
-            sign_b = keep.tile([P, half, PACK], BF16, name="sign", tag="sign%d" % b, align_bytes=64)
+            sign_b = keep.tile([P, HALF, PACK], BF16, name="sign", tag="sign%d" % b, align_bytes=64)
             nc.scalar.activation(
-                sign_b[:], sm_t[:, b * PACK : (b + 1) * PACK].unsqueeze(1).to_broadcast([P, half, PACK]), ACT.Sign
+                sign_b[:], sm_t[:, b * PACK : (b + 1) * PACK].unsqueeze(1).to_broadcast([P, HALF, PACK]), ACT.Sign
             )
             signs.append(sign_b)
+        sign_last = keep.tile([P, PACK], F32, name="sign_last", tag="rinv")
+        nc.scalar.activation(sign_last[:], sm_t[:, PACK:], ACT.Sign)
 
-        g_rest = keep.tile([P, J - CHUNK], I32, name="g_rest", tag="wus_raw", align_bytes=64)
+        g_rest = keep.tile([P, J - CHUNK], I32, name="g_rest", tag="wu_raw1", align_bytes=64)
         nc.vector.tensor_copy(g_rest[:].bitcast(U32), tab_w[:].bitcast(U32).indirect(entries(CHUNK, J - CHUNK)))
         picked = [g_first[:]] + [g_rest[:, c * CHUNK : (c + 1) * CHUNK] for c in range(CHUNKS - 1)]
-        clear_window("tab_w")
+        clear_window(nc.gpsimd, "tab_w")
 
         dealt = {}
 
-        def deal_wd(first, count, tags):
+        def deal_wd(t0, count, tags):
             w8 = keep.tile([P, HB, count, P], I32, name="wd8_w", tag=tags[0], align_bytes=64)
             w4 = keep.tile([P, HB * count * P * 2], U8, name="wd4_w", tag=tags[1], align_bytes=64)
             ws = keep.tile([P, HB, count, P], U8, name="wd_s", tag=tags[2], align_bytes=64)
+            nc.vector.tensor_copy(
+                w8[:].rearrange("p a t (g i) -> p a g t i", i=LINE),
+                wd8_raw[:].rearrange("p (a g i t) -> p a g t i", a=HB, i=LINE, t=PACK)[:, :, :, t0 : t0 + count, :],
+            )
             for raw, out in (
-                (wd8_raw[:], w8[:]),
                 (wd4_raw[:].bitcast(U16), w4[:].bitcast(U16).rearrange("p (a t m) -> p a t m", a=HB, t=count)),
                 (wds_raw[:], ws[:]),
             ):
-                nc.vector.tensor_copy(out, raw.rearrange("p (a m t) -> p a t m", a=HB, t=PACK)[:, :, first : first + count, :])
+                nc.vector.tensor_copy(out, raw.rearrange("p (a m t) -> p a t m", a=HB, t=PACK)[:, :, t0 : t0 + count, :])
             for i in range(count):
                 for b in range(HB):
                     col = (b * count + i) * P
-                    dealt[(b, first + i)] = (w8[:, b, i, :], w4[:, 2 * col : 2 * (col + P)], ws[:, b, i, :], ws[4:, b, i, :])
+                    dealt[(b, t0 + i)] = (w8[:, b, i, :], w4[:, 2 * col : 2 * (col + P)], ws[:, b, i, :], ws[4:, b, i, :])
 
         h_w = [keep.tile([P, J], U32, name="h_w%d" % b, align_bytes=64) for b in range(HB)]
         h_s = [keep.tile([P, J], U8, name="h_s%d" % b, align_bytes=64) for b in range(HB)]
@@ -163,7 +171,6 @@ def tile_list_modp_relu2_res_noneP_kernel(
         projected = []
 
         def rectify(c, b, first_bank=0):
-            words = picked[c]
             relu = keep.tile([P, PACK, CHUNK], F32, name="relu", tag="relu%d_%d" % (c, b), align_bytes=64)
             for t in range(PACK):
                 acc = psum.tile([P, CHUNK], F32, name="acc_a", tag="bank%d" % (first_bank + t))
@@ -171,7 +178,7 @@ def tile_list_modp_relu2_res_noneP_kernel(
                     out=acc[:],
                     lhsT=wu_w[b][:, t * P : (t + 1) * P].bitcast(FP8X4),
                     lhsT_scale=wu_s[4 * b :, t * P : (t + 1) * P],
-                    rhs=words.bitcast(FP8X4),
+                    rhs=picked[c].bitcast(FP8X4),
                     rhs_scale=picked_s[c],
                     start=True,
                     stop=True,
@@ -183,20 +190,32 @@ def tile_list_modp_relu2_res_noneP_kernel(
         def quantise(c, b):
             square = keep.tile([P, CHUNK * PACK], BF16, name="square", tag="square%d_%d" % (c, b), align_bytes=64)
             nc.scalar.activation(
-                square[:].rearrange("p (c t) -> p c t", t=PACK),
-                relus[(c, b)][:].rearrange("p t c -> p c t"),
+                square[:].rearrange("p (g i t) -> p g t i", t=PACK, i=LINE),
+                relus[(c, b)][:].rearrange("p t (g i) -> p g t i", i=LINE),
                 ACT.Square,
                 scale=0.5,
             )
             signed = keep.tile([P, CHUNK * PACK], BF16, name="signed", tag="signed%d_%d" % (c, b), align_bytes=64)
             sign = signs[b][:].rearrange("p c t -> p (c t)")
-            for j0 in (0, half):
-                part = slice(j0 * PACK, (j0 + half) * PACK)
+            for j0 in (0, HALF):
+                part = slice(j0 * PACK, (j0 + HALF) * PACK)
                 nc.vector.tensor_tensor(signed[:, part], square[:, part], sign, ALU.mult)
-            for j0 in (0, half):
-                part = slice(j0 * PACK, (j0 + half) * PACK)
-                cols = slice(c * CHUNK + j0, c * CHUNK + j0 + half)
+            for j0 in (0, HALF):
+                part = slice(j0 * PACK, (j0 + HALF) * PACK)
+                cols = slice(c * CHUNK + j0, c * CHUNK + j0 + HALF)
                 nc.vector.quantize_mx(out=h_w[b][:, cols].bitcast(FP8X4), scales=h_s[b][:, cols], in_=signed[:, part])
+
+        def quantise_last():
+            c, b = CHUNKS - 1, HB - 1
+            square = keep.tile([P, PACK, CHUNK], F32, name="square_f32", align_bytes=64)
+            nc.scalar.activation(square[:], relus[(c, b)][:], ACT.Square, scale=0.5)
+            signed = keep.tile([P, CHUNK, PACK], BF16, name="signed", tag="signed%d_%d" % (c, b), align_bytes=64)
+            for t in range(PACK):
+                nc.scalar.activation(signed[:, :, t], square[:, t, :], ACT.Copy, scale=sign_last[:, t : t + 1])
+            cols = slice(c * CHUNK, (c + 1) * CHUNK)
+            nc.vector.quantize_mx(
+                out=h_w[b][:, cols].bitcast(FP8X4), scales=h_s[b][:, cols], in_=signed[:].rearrange("p c t -> p (c t)")
+            )
 
         def project(y, t, first, width):
             acc = psum.tile([P, width], F32, name="acc_y", tag="bank%d" % (PACK + len(projected) % PACK))
@@ -225,41 +244,39 @@ def tile_list_modp_relu2_res_noneP_kernel(
                     )
             nc.scalar.copy(y, acc[:])
 
-        def scatter(y, t, first, width):
-            nc.vector.tensor_tensor(windows[t][:].indirect(entries(first, width)), y, wgo_t[:, first : first + width], ALU.mult)
+        def put(tag, *pieces):
+            staged = keep.tile([P, sum(piece[2] for piece in pieces) * CHUNK], F32, name="y", tag=tag, align_bytes=64)
+            used = 0
+            for t, c, count in pieces:
+                first, width = c * CHUNK, count * CHUNK
+                y = staged[:, used : used + width]
+                for j0 in range(0, width, BANK):
+                    columns = min(BANK, width - j0)
+                    project(y[:, j0 : j0 + columns], t, first + j0, columns)
+                nc.vector.tensor_tensor(
+                    windows[t][:].indirect(entries(first, width)), y, wgo_t[:, first : first + width], ALU.mult
+                )
+                used = used + width
 
-        def put(y, t, first, width):
-            for j0 in range(0, width, BANK):
-                part = min(BANK, width - j0)
-                project(y[:, j0 : j0 + part], t, first + j0, part)
-            scatter(y, t, first, width)
-
-        def staging(width, tag):
-            return keep.tile([P, width], F32, name="y", tag=tag, align_bytes=64)
-
-        def make_hidden(c, b):
-            rectify(c, b)
-            quantise(c, b)
-
-        def make_hidden_on_vector(c, b):
+        def make_half_on_vector(c, b):
             scaled = keep.tile([P, CHUNK * PACK], F32, name="scaled", tag="scaled", align_bytes=64)
             rounded_h = keep.tile([P, CHUNK * PACK], BF16, name="rounded_h", tag="rounded_h", align_bytes=64)
-            factor = sm_t[:, b * PACK : (b + 1) * PACK].unsqueeze(1).to_broadcast([P, half, PACK])
+            factor = sm_t[:, b * PACK : (b + 1) * PACK].unsqueeze(1).to_broadcast([P, HALF, PACK])
             sums = []
-            for j0 in (0, half):
-                acc = psum.tile([P, PACK, half], F32, name="acc_v", tag="bank%d" % (PACK + len(sums)))
+            for j0 in (0, HALF):
+                acc = psum.tile([P, PACK, HALF], F32, name="acc_v", tag="bank%d" % (PACK + len(sums)))
                 for t in range(PACK):
                     nc.tensor.matmul_mx(
                         out=acc[:, t, :],
                         lhsT=wu_w[b][:, t * P : (t + 1) * P].bitcast(FP8X4),
                         lhsT_scale=wu_s[4 * b :, t * P : (t + 1) * P],
-                        rhs=picked[c][:, j0 : j0 + half].bitcast(FP8X4),
-                        rhs_scale=picked_s[c][:, j0 : j0 + half],
+                        rhs=picked[c][:, j0 : j0 + HALF].bitcast(FP8X4),
+                        rhs_scale=picked_s[c][:, j0 : j0 + HALF],
                         start=True,
                         stop=True,
                     )
                 sums.append(acc[:].rearrange("p t c -> p c t"))
-            parts = [slice(j0 * PACK, (j0 + half) * PACK) for j0 in (0, half)]
+            parts = [slice(j0 * PACK, (j0 + HALF) * PACK) for j0 in (0, HALF)]
             for a, part in zip(sums, parts):
                 nc.vector.tensor_tensor(scaled[:, part].rearrange("p (c t) -> p c t", t=PACK), a, factor, ALU.mult)
             for a, part in zip(sums, parts):
@@ -271,42 +288,38 @@ def tile_list_modp_relu2_res_noneP_kernel(
                     ALU.max,
                     ALU.mult,
                 )
-            for j0, part in zip((0, half), parts):
-                cols = slice(c * CHUNK + j0, c * CHUNK + j0 + half)
+            for j0, part in zip((0, HALF), parts):
+                cols = slice(c * CHUNK + j0, c * CHUNK + j0 + HALF)
                 nc.vector.quantize_mx(out=h_w[b][:, cols].bitcast(FP8X4), scales=h_s[b][:, cols], in_=rounded_h[:, part])
 
         rectify(0, 0)
-        make_hidden_on_vector(0, 1)
+        make_half_on_vector(0, 1)
         quantise(0, 0)
         deal_wd(0, 1, ("square0_0", "relu0_0", "signed0_0"))
-        deal_wd(1, PACK - 1, ("rounded_h", "scaled", "wd_s_rest"))
-        def put_two(first, second, tag):
-            y = staging(2 * CHUNK, tag)
-            for i, (c, t) in enumerate((first, second)):
-                put(y[:, i * CHUNK : (i + 1) * CHUNK], t, c * CHUNK, CHUNK)
-
-        make_hidden(1, 0)
+        deal_wd(1, PACK - 1, ("rounded_h", "scaled", "g_first"))
+        rectify(1, 0)
+        quantise(1, 0)
         rectify(1, 1, PACK)
-        put(staging(CHUNK, "y_first")[:], 0, 0, CHUNK)
+        put("y_first", (0, 0, 1))
         quantise(1, 1)
-        clear_window("signed1_1")
+        clear_window(nc.gpsimd, "signed1_1")
         rectify(2, 0)
-        put_two((0, 1), (1, 0), "relu1_1")
+        put("relu1_1", (1, 0, 1), (0, 1, 1))
         quantise(2, 0)
-        clear_window("signed2_0")
+        clear_window(nc.gpsimd, "signed2_0")
         rectify(2, 1)
-        put_two((0, 2), (1, 1), "relu2_0")
+        put("relu2_0", (2, 0, 1), (1, 1, 1))
         quantise(2, 1)
         rectify(3, 0)
-        put_two((0, 3), (1, 2), "relu2_1")
+        put("relu2_1", (3, 0, 1), (2, 1, 1))
         quantise(3, 0)
         rectify(3, 1)
-        put(staging(CHUNK, "relu3_0")[:], 0, 2 * CHUNK, CHUNK)
-        quantise(3, 1)
-        put(staging(CHUNK, "relu3_1")[:], 1, 2 * CHUNK, CHUNK)
-        put_two((3, 0), (3, 1), "relu1_1")
-        put(staging(2 * CHUNK, "relu2_0")[:], 2, 2 * CHUNK, 2 * CHUNK)
-        put(staging(3 * CHUNK, "relu3_0")[:], 3, CHUNK, 3 * CHUNK)
+        put("relu3_0", (0, 2, 1))
+        quantise_last()
+        put("relu3_1", (1, 2, 1))
+        put("relu1_1", (0, 3, 1), (1, 3, 1))
+        put("relu2_0", (2, 2, 2))
+        put("relu3_0", (3, 1, 3))
 
         rows = out_0.rearrange("(p t) c -> p t c", t=PACK)
         widths = TAIL_VECTOR + TAIL_SCALAR
@@ -331,13 +344,13 @@ def tile_list_modp_relu2_res_noneP_kernel(
             out_w = keep.tile([P, w], I32, name="out_w%d" % i, align_bytes=64)
             done = 0
             while done < w:
-                part = max(n for n in (128, 256, 512) if n <= w - done)
+                columns = max(n for n in QUANTISE_WIDTHS if n <= w - done)
                 nc.vector.quantize_mx(
-                    out=out_w[:, done : done + part].bitcast(FP8X4),
-                    scales=out_s[:, edges[i] + done : edges[i] + done + part],
-                    in_=grouped[i][:, done * PACK : (done + part) * PACK],
+                    out=out_w[:, done : done + columns].bitcast(FP8X4),
+                    scales=out_s[:, edges[i] + done : edges[i] + done + columns],
+                    in_=grouped[i][:, done * PACK : (done + columns) * PACK],
                 )
-                done = done + part
+                done = done + columns
             nc.sync.dma_start(words_out[:, edges[i] : edges[i] + w], out_w[:])
 
         for t in range(PACK):
@@ -351,7 +364,8 @@ def tile_list_modp_relu2_res_noneP_kernel(
             round_plane(nc.vector.tensor_copy, PACK - 1, i)
         for i in by_vector:
             nc.vector.tensor_copy(
-                grouped[i][:].rearrange("p (c t) -> p c t", t=PACK), rounded[i][:].rearrange("p (t c) -> p c t", t=PACK)
+                grouped[i][:].rearrange("p (g i t) -> p g t i", t=PACK, i=LINE),
+                rounded[i][:].rearrange("p (t g i) -> p g t i", t=PACK, i=LINE),
             )
         for i in by_scalar:
             round_pair(PACK - 1, i)

@@ -101,14 +101,11 @@ def tile_list_modp_relu2_res_noneP_kernel(
         picked_s = [g_s[:, c * CHUNK : (c + 1) * CHUNK] for c in range(CHUNKS)]
 
         mag = keep.tile([P, HB * PACK], F32, name="mag", tag="sign0", align_bytes=64)
-        magc = keep.tile([P, HB * PACK], F32, name="magc")
         root0 = keep.tile([P, HB * PACK], F32, name="root0", tag="sign1", align_bytes=64)
         rinv = keep.tile([P, HB * PACK], F32, name="rinv", tag="rinv")
-        quot = keep.tile([P, HB * PACK], F32, name="quot")
         root = keep.tile([P, HB * PACK], F32, name="root")
         nc.vector.scalar_tensor_tensor(mag[:], sm_t[:], -1.0, sm_t[:], ALU.mult, ALU.max)
-        nc.vector.tensor_scalar(magc[:], mag[:], TINY, None, ALU.max)
-        nc.scalar.activation(root0[:], magc[:], ACT.Sqrt)
+        nc.scalar.activation(root0[:], mag[:], ACT.Sqrt, bias=TINY)
 
         g_first = keep.tile([P, CHUNK], I32, name="g_first", tag="g_first", align_bytes=64)
         nc.vector.tensor_copy(g_first[:].bitcast(U32), tab_w[:].bitcast(U32).indirect(entries(0, CHUNK)))
@@ -123,11 +120,14 @@ def tile_list_modp_relu2_res_noneP_kernel(
 
         nc.vector.reciprocal(rinv[:], root0[:])
         deal_wu(0)
-        nc.vector.tensor_tensor(quot[:], magc[:], rinv[:], ALU.mult)
         nc.vector.tensor_copy(
             wu_s[:].rearrange("p (t m) -> p t m", t=PACK), wus_raw[:].rearrange("p (m t) -> p t m", t=PACK)
         )
-        nc.vector.tensor_tensor(root[:], quot[:], root0[:], ALU.add)
+        for j in range(HB * PACK):
+            column = slice(j, j + 1)
+            nc.scalar.activation(
+                root[:, column], mag[:, column], ACT.Identity, scale=rinv[:, column], bias=root0[:, column]
+            )
         deal_wu(1)
 
         signs = []
@@ -137,8 +137,8 @@ def tile_list_modp_relu2_res_noneP_kernel(
                 sign_b[:], sm_t[:, b * PACK : (b + 1) * PACK].unsqueeze(1).to_broadcast([P, HALF, PACK]), ACT.Sign
             )
             signs.append(sign_b)
-        sign_last = keep.tile([P, PACK], F32, name="sign_last", tag="rinv")
-        nc.scalar.activation(sign_last[:], sm_t[:, PACK:], ACT.Sign)
+        sign_column = keep.tile([P, HB * PACK], F32, name="sign_column", tag="rinv")
+        nc.scalar.activation(sign_column[:], sm_t[:], ACT.Sign)
 
         g_rest = keep.tile([P, J - CHUNK], I32, name="g_rest", tag="wu_raw1", align_bytes=64)
         nc.vector.tensor_copy(g_rest[:].bitcast(U32), tab_w[:].bitcast(U32).indirect(entries(CHUNK, J - CHUNK)))
@@ -205,17 +205,20 @@ def tile_list_modp_relu2_res_noneP_kernel(
                 cols = slice(c * CHUNK + j0, c * CHUNK + j0 + HALF)
                 nc.vector.quantize_mx(out=h_w[b][:, cols].bitcast(FP8X4), scales=h_s[b][:, cols], in_=signed[:, part])
 
-        def quantise_last():
-            c, b = CHUNKS - 1, HB - 1
-            square = keep.tile([P, PACK, CHUNK], F32, name="square_f32", align_bytes=64)
+        def quantise_signed_on_scalar(c, b):
+            square = keep.tile([P, PACK, CHUNK], BF16, name="square", tag="square%d_%d" % (c, b), align_bytes=64)
             nc.scalar.activation(square[:], relus[(c, b)][:], ACT.Square, scale=0.5)
-            signed = keep.tile([P, CHUNK, PACK], BF16, name="signed", tag="signed%d_%d" % (c, b), align_bytes=64)
+            rows = keep.tile([P, PACK, CHUNK], BF16, name="rows", tag="rows%d_%d" % (c, b), align_bytes=64)
             for t in range(PACK):
-                nc.scalar.activation(signed[:, :, t], square[:, t, :], ACT.Copy, scale=sign_last[:, t : t + 1])
-            cols = slice(c * CHUNK, (c + 1) * CHUNK)
-            nc.vector.quantize_mx(
-                out=h_w[b][:, cols].bitcast(FP8X4), scales=h_s[b][:, cols], in_=signed[:].rearrange("p c t -> p (c t)")
+                column = b * PACK + t
+                nc.scalar.activation(rows[:, t, :], square[:, t, :], ACT.Copy, scale=sign_column[:, column : column + 1])
+            signed = keep.tile([P, CHUNK * PACK], BF16, name="signed", tag="signed%d_%d" % (c, b), align_bytes=64)
+            nc.scalar.copy(
+                signed[:].rearrange("p (g i t) -> p g t i", t=PACK, i=LINE),
+                rows[:].rearrange("p t (g i) -> p g t i", i=LINE),
             )
+            cols = slice(c * CHUNK, (c + 1) * CHUNK)
+            nc.vector.quantize_mx(out=h_w[b][:, cols].bitcast(FP8X4), scales=h_s[b][:, cols], in_=signed[:])
 
         def project(y, t, first, width):
             acc = psum.tile([P, width], F32, name="acc_y", tag="bank%d" % (PACK + len(projected) % PACK))
@@ -312,10 +315,10 @@ def tile_list_modp_relu2_res_noneP_kernel(
         quantise(2, 1)
         rectify(3, 0)
         put("relu2_1", (3, 0, 1), (2, 1, 1))
-        quantise(3, 0)
+        quantise_signed_on_scalar(3, 0)
         rectify(3, 1)
         put("relu3_0", (0, 2, 1))
-        quantise_last()
+        quantise_signed_on_scalar(3, 1)
         put("relu3_1", (1, 2, 1))
         put("relu1_1", (0, 3, 1), (1, 3, 1))
         put("relu2_0", (2, 2, 2))

@@ -91,7 +91,12 @@ def tile_list_modp_relu2_res_noneP_kernel(
             engine.memset(window[:].bitcast(I32), 0)
             windows.append(window)
 
-        clear_window(nc.vector, "window0")
+        window = keep.tile([P, T], F32, name="window", tag="window0", align_bytes=64)
+        nc.vector.memset(window[:, : T - 1].bitcast(I32), 0)
+        nc.vector.memset(window[:, T - 1 :].bitcast(I32), 0)
+        windows.append(window)
+        clear_window(nc.gpsimd, "window1")
+        clear_window(nc.gpsimd, "window2")
 
         def entries(first, width):
             return offsets[:, first // 16 : (first + width) // 16]
@@ -305,11 +310,9 @@ def tile_list_modp_relu2_res_noneP_kernel(
         rectify(1, 1, PACK)
         put("y_first", (0, 0, 1))
         quantise(1, 1)
-        clear_window(nc.gpsimd, "signed1_1")
         rectify(2, 0)
         put("relu1_1", (1, 0, 1), (0, 1, 1))
         quantise(2, 0)
-        clear_window(nc.gpsimd, "signed2_0")
         rectify(2, 1)
         put("relu2_0", (2, 0, 1), (1, 1, 1))
         quantise(2, 1)

@@ -27,8 +27,9 @@ CHUNK = 256
 CHUNKS = J // CHUNK
 HALF = CHUNK // 2
 QUANTISE_WIDTHS = (128, 256, 512)
-TAIL_VECTOR = (384, 512)
-TAIL_SCALAR = (512, 384, 256)
+TAIL_VECTOR = (512, 512)
+TAIL_SCALAR = (512, 256, 256)
+SIGN_RUN = 64
 TINY = 2.0 ** -100
 
 
@@ -41,41 +42,43 @@ def tile_list_modp_relu2_res_noneP_kernel(
         keep = ctx.enter_context(tc.tile_pool(name="keep", bufs=1))
         psum = ctx.enter_context(tc.psum_pool(name="psum", bufs=1))
 
+        def tile(shape, dtype, name, tag=None):
+            return keep.tile(shape, dtype, name=name, tag=tag or name, align_bytes=64)
+
         offsets = keep.tile([P, J // 16], U16, name="offsets")
-        tab_w = keep.tile([P, T], I32, name="tab_w", tag="tab_w", align_bytes=64)
-        tab_s = keep.tile([P, T], U8, name="tab_s", align_bytes=64)
-        wu_raw = [keep.tile([P, PASS], I32, name="wu_raw", tag="wu_raw%d" % b, align_bytes=64) for b in range(HB)]
-        wus_raw = keep.tile([P, PASS], U8, name="wus_raw", align_bytes=64)
-        sm_t = keep.tile([P, HB * PACK], F32, name="sm_t")
-        wds_raw = keep.tile([P, HB * N], U8, name="wds_raw", align_bytes=64)
+        sm_t = tile([P, HB * PACK], F32, "sm_t")
+        tab_w = tile([P, T], I32, "tab_w")
+        tab_s = tile([P, T], U8, "tab_s")
+        wu_raw = [tile([P, PASS], I32, "wu_raw%d" % b) for b in range(HB)]
+        wus_raw = tile([P, PASS], U8, "wus_raw")
+        wds_raw = tile([P, HB * N], U8, "wds_raw")
+        wd8_raw = tile([P, HB * N], I32, "wd8_raw")
+        wd4_raw = tile([P, HB * N // 2], I32, "wd4_raw")
+        wgo_t = tile([P, J], F32, "wgo_t")
 
         nc.gpsimd.memset(tab_s[:].bitcast(I32), 0)
         nc.gpsimd.memset(wus_raw[:].bitcast(I32), 0)
         nc.gpsimd.memset(wds_raw[:].bitcast(I32), 0)
 
+        nc.sync.dma_start(sm_t[:].rearrange("p (b t) -> p b t", t=PACK), sm.rearrange("(b p t) -> p b t", p=P, t=PACK))
+        nc.sync.dma_start(offsets[:], offs)
         for q in range(QUADRANTS):
             nc.sync.dma_start(
                 tab_s[32 * q : 32 * q + 4, :].bitcast(I32), tab_scales[0, 4 * q : 4 * q + 4, :].bitcast(I32)
             )
-        nc.sync.dma_start(offsets[:], offs)
-        nc.sync.dma_start(sm_t[:].rearrange("p (b t) -> p b t", t=PACK), sm.rearrange("(b p t) -> p b t", p=P, t=PACK))
-        nc.sync.dma_start(tab_w[:], tab_words[0].rearrange("p t i -> p (t i)").bitcast(I32))
         wu_src = wu_words[0].rearrange("p r i -> p (r i)").bitcast(I32)
         nc.sync.dma_start(wu_raw[0][:], wu_src[:, :PASS])
+        nc.sync.dma_start(tab_w[:], tab_words[0].rearrange("p t i -> p (t i)").bitcast(I32))
         for q in range(QUADRANTS):
             nc.sync.dma_start(
                 wus_raw[32 * q : 32 * q + 4 * HB, :].bitcast(I32),
                 wu_scales[0, 4 * q : 4 * q + 4, :].bitcast(I32).rearrange("r (b n) -> b r n", b=HB),
             )
         nc.sync.dma_start(wu_raw[1][:], wu_src[:, PASS:])
-
-        wd8_raw = keep.tile([P, HB * N], I32, name="wd8_raw", align_bytes=64)
-        wd4_raw = keep.tile([P, HB * N // 2], I32, name="wd4_raw", align_bytes=64)
-        wgo_t = keep.tile([P, J], F32, name="wgo_t")
+        nc.sync.dma_start(wd4_raw[:].rearrange("p (a n) -> p a n", a=HB), wd4_words.rearrange("a p n -> p a n").bitcast(I32))
         nc.sync.dma_start(
             wd8_raw[:].rearrange("p (a n) -> p a n", a=HB), wd8_words.rearrange("a p n i -> p a (n i)").bitcast(I32)
         )
-        nc.sync.dma_start(wd4_raw[:].rearrange("p (a n) -> p a n", a=HB), wd4_words.rearrange("a p n -> p a n").bitcast(I32))
         for base, scale_rows in ((0, wd4_scales), (4, wd8_scales)):
             for q in range(QUADRANTS):
                 nc.sync.dma_start(
@@ -84,205 +87,181 @@ def tile_list_modp_relu2_res_noneP_kernel(
                 )
         nc.sync.dma_start(wgo_t[:], wgo)
 
-        windows = []
-
-        def clear_window(engine, tag):
-            window = keep.tile([P, T], F32, name="window", tag=tag, align_bytes=64)
-            engine.memset(window[:].bitcast(I32), 0)
-            windows.append(window)
-
-        window = keep.tile([P, T], F32, name="window", tag="window0", align_bytes=64)
-        nc.vector.memset(window[:, : T - 1].bitcast(I32), 0)
-        nc.vector.memset(window[:, T - 1 :].bitcast(I32), 0)
-        windows.append(window)
-        clear_window(nc.gpsimd, "window1")
-        clear_window(nc.gpsimd, "window2")
+        windows = [tile([P, T], F32, "window%d" % t) for t in range(PACK - 1)]
+        nc.vector.memset(windows[0][:, : T - 1].bitcast(I32), 0)
+        nc.vector.memset(windows[0][:, T - 1 :].bitcast(I32), 0)
+        nc.gpsimd.memset(windows[1][:].bitcast(I32), 0)
+        nc.gpsimd.memset(windows[2][:].bitcast(I32), 0)
 
         def entries(first, width):
             return offsets[:, first // 16 : (first + width) // 16]
 
-        g_s = keep.tile([P, J], U8, name="g_s", align_bytes=64)
-        nc.vector.tensor_copy(g_s[:], tab_s[:].indirect(offsets[:]))
-        picked_s = [g_s[:, c * CHUNK : (c + 1) * CHUNK] for c in range(CHUNKS)]
-
-        mag = keep.tile([P, HB * PACK], F32, name="mag", tag="sign0", align_bytes=64)
-        root0 = keep.tile([P, HB * PACK], F32, name="root0", tag="sign1", align_bytes=64)
-        rinv = keep.tile([P, HB * PACK], F32, name="rinv", tag="rinv")
-        root = keep.tile([P, HB * PACK], F32, name="root")
+        mag = tile([P, HB * PACK], F32, "mag", "sign0")
+        root0 = tile([P, HB * PACK], F32, "root0", "sign1")
+        rinv = tile([P, HB * PACK], F32, "rinv")
+        root = tile([P, HB * PACK], F32, "root")
         nc.vector.scalar_tensor_tensor(mag[:], sm_t[:], -1.0, sm_t[:], ALU.mult, ALU.max)
         nc.scalar.activation(root0[:], mag[:], ACT.Sqrt, bias=TINY)
+        nc.vector.reciprocal(rinv[:], root0[:])
 
-        g_first = keep.tile([P, CHUNK], I32, name="g_first", tag="g_first", align_bytes=64)
-        nc.vector.tensor_copy(g_first[:].bitcast(U32), tab_w[:].bitcast(U32).indirect(entries(0, CHUNK)))
+        g_s = tile([P, J], U8, "g_s")
+        nc.vector.tensor_copy(g_s[:], tab_s[:].indirect(offsets[:]))
+        picked_s = [g_s[:, c * CHUNK : (c + 1) * CHUNK] for c in range(CHUNKS)]
+        picked = []
 
-        wu_w = [keep.tile([P, PASS], I32, name="wu_w%d" % b, align_bytes=64) for b in range(HB)]
-        wu_s = keep.tile([P, PASS], U8, name="wu_s", align_bytes=64)
+        def gather_words(first, count, tag):
+            g = tile([P, count * CHUNK], I32, "picked", tag)
+            nc.vector.tensor_copy(g[:].bitcast(U32), tab_w[:].bitcast(U32).indirect(entries(first * CHUNK, count * CHUNK)))
+            picked.extend(g[:, c * CHUNK : (c + 1) * CHUNK] for c in range(count))
+
+        gather_words(0, 1, "picked0")
+
+        wu_w = [tile([P, PASS], U32, "wu_w%d" % b) for b in range(HB)]
+        wu_s = tile([P, PASS], U8, "wu_s")
 
         def deal_wu(b):
-            nc.vector.tensor_copy(
-                wu_w[b][:].rearrange("p (t m) -> p m t", t=PACK), wu_raw[b][:].rearrange("p (m t) -> p m t", t=PACK)
+            nc.scalar.copy(
+                wu_w[b][:].rearrange("p (t g i) -> p g t i", t=PACK, i=LINE),
+                wu_raw[b][:].bitcast(U32).rearrange("p (g i t) -> p g t i", t=PACK, i=LINE),
             )
 
-        nc.vector.reciprocal(rinv[:], root0[:])
-        deal_wu(0)
-        nc.vector.tensor_copy(
-            wu_s[:].rearrange("p (t m) -> p t m", t=PACK), wus_raw[:].rearrange("p (m t) -> p t m", t=PACK)
-        )
         for j in range(HB * PACK):
             column = slice(j, j + 1)
             nc.scalar.activation(
                 root[:, column], mag[:, column], ACT.Identity, scale=rinv[:, column], bias=root0[:, column]
             )
-        deal_wu(1)
-
+        deal_wu(0)
+        nc.vector.tensor_copy(
+            wu_s[:].rearrange("p (t m) -> p t m", t=PACK), wus_raw[:].rearrange("p (m t) -> p t m", t=PACK)
+        )
         signs = []
         for b in range(HB):
-            sign_b = keep.tile([P, HALF, PACK], BF16, name="sign", tag="sign%d" % b, align_bytes=64)
+            sign_b = tile([P, SIGN_RUN, PACK], BF16, "sign", "sign%d" % b)
             nc.scalar.activation(
-                sign_b[:], sm_t[:, b * PACK : (b + 1) * PACK].unsqueeze(1).to_broadcast([P, HALF, PACK]), ACT.Sign
+                sign_b[:], sm_t[:, b * PACK : (b + 1) * PACK].unsqueeze(1).to_broadcast([P, SIGN_RUN, PACK]), ACT.Sign
             )
             signs.append(sign_b)
-        sign_column = keep.tile([P, HB * PACK], F32, name="sign_column", tag="rinv")
-        nc.scalar.activation(sign_column[:], sm_t[:], ACT.Sign)
+        deal_wu(1)
+        gather_words(1, CHUNKS - 1, "wus_raw")
 
-        g_rest = keep.tile([P, J - CHUNK], I32, name="g_rest", tag="wu_raw1", align_bytes=64)
-        nc.vector.tensor_copy(g_rest[:].bitcast(U32), tab_w[:].bitcast(U32).indirect(entries(CHUNK, J - CHUNK)))
-        picked = [g_first[:]] + [g_rest[:, c * CHUNK : (c + 1) * CHUNK] for c in range(CHUNKS - 1)]
-        clear_window(nc.gpsimd, "tab_w")
-
-        dealt = {}
-
-        def deal_wd(t0, count, tags):
-            w8 = keep.tile([P, HB, count, P], I32, name="wd8_w", tag=tags[0], align_bytes=64)
-            w4 = keep.tile([P, HB * count * P * 2], U8, name="wd4_w", tag=tags[1], align_bytes=64)
-            ws = keep.tile([P, HB, count, P], U8, name="wd_s", tag=tags[2], align_bytes=64)
-            nc.vector.tensor_copy(
-                w8[:].rearrange("p a t (g i) -> p a g t i", i=LINE),
-                wd8_raw[:].rearrange("p (a g i t) -> p a g t i", a=HB, i=LINE, t=PACK)[:, :, :, t0 : t0 + count, :],
+        wd8_w = tile([P, HB, PACK, P], I32, "wd8_w")
+        for b in range(HB):
+            nc.gpsimd.tensor_copy(
+                wd8_w[:, b, :, :].rearrange("p t (g i) -> p g t i", i=LINE),
+                wd8_raw[:, b * N : (b + 1) * N].rearrange("p (g i t) -> p g t i", i=LINE, t=PACK),
             )
-            for raw, out in (
-                (wd4_raw[:].bitcast(U16), w4[:].bitcast(U16).rearrange("p (a t m) -> p a t m", a=HB, t=count)),
-                (wds_raw[:], ws[:]),
-            ):
-                nc.vector.tensor_copy(out, raw.rearrange("p (a m t) -> p a t m", a=HB, t=PACK)[:, :, t0 : t0 + count, :])
+        wd4_w, wd_s = {}, {}
+
+        def deal_wd4(t0, count, tag):
+            w4 = tile([P, HB * count * P * 2], U8, "wd4_w", tag)
+            nc.scalar.copy(
+                w4[:].bitcast(U16).rearrange("p (a t m) -> p a t m", a=HB, t=count),
+                wd4_raw[:].bitcast(U16).rearrange("p (a m t) -> p a t m", a=HB, t=PACK)[:, :, t0 : t0 + count, :],
+            )
             for i in range(count):
                 for b in range(HB):
                     col = (b * count + i) * P
-                    dealt[(b, t0 + i)] = (w8[:, b, i, :], w4[:, 2 * col : 2 * (col + P)], ws[:, b, i, :], ws[4:, b, i, :])
+                    wd4_w[(b, t0 + i)] = w4[:, 2 * col : 2 * (col + P)]
 
-        h_w = [keep.tile([P, J], U32, name="h_w%d" % b, align_bytes=64) for b in range(HB)]
-        h_s = [keep.tile([P, J], U8, name="h_s%d" % b, align_bytes=64) for b in range(HB)]
+        def deal_wd_scales(t0, count, tag):
+            ws = tile([P, HB, count, P], U8, "wd_s", tag)
+            nc.vector.tensor_copy(
+                ws[:], wds_raw[:].rearrange("p (a m t) -> p a t m", a=HB, t=PACK)[:, :, t0 : t0 + count, :]
+            )
+            for i in range(count):
+                for b in range(HB):
+                    wd_s[(b, t0 + i)] = (ws[:, b, i, :], ws[4:, b, i, :])
+
+        h_w = [tile([P, J], U32, "h_w%d" % b) for b in range(HB)]
+        h_s = [tile([P, J], U8, "h_s%d" % b) for b in range(HB)]
         relus = {}
         projected = []
 
-        def rectify(c, b, first_bank=0):
-            relu = keep.tile([P, PACK, CHUNK], F32, name="relu", tag="relu%d_%d" % (c, b), align_bytes=64)
+        def first_product(acc, c, b, t, columns):
+            nc.tensor.matmul_mx(
+                out=acc,
+                lhsT=wu_w[b][:, t * P : (t + 1) * P].bitcast(FP8X4),
+                lhsT_scale=wu_s[4 * b :, t * P : (t + 1) * P],
+                rhs=picked[c][:, columns].bitcast(FP8X4),
+                rhs_scale=picked_s[c][:, columns],
+                start=True,
+                stop=True,
+            )
+
+        def rectify(c, b):
+            relu = tile([P, PACK, CHUNK], F32, "relu%d_%d" % (c, b))
             for t in range(PACK):
-                acc = psum.tile([P, CHUNK], F32, name="acc_a", tag="bank%d" % (first_bank + t))
-                nc.tensor.matmul_mx(
-                    out=acc[:],
-                    lhsT=wu_w[b][:, t * P : (t + 1) * P].bitcast(FP8X4),
-                    lhsT_scale=wu_s[4 * b :, t * P : (t + 1) * P],
-                    rhs=picked[c].bitcast(FP8X4),
-                    rhs_scale=picked_s[c],
-                    start=True,
-                    stop=True,
-                )
+                acc = psum.tile([P, CHUNK], F32, name="acc_a", tag="bank%d" % t)
+                first_product(acc[:], c, b, t, slice(0, CHUNK))
                 factor = root[:, b * PACK + t : b * PACK + t + 1]
                 nc.scalar.activation(relu[:, t, :], acc[:], ACT.Relu, scale=factor)
             relus[(c, b)] = relu
 
-        def quantise(c, b):
-            square = keep.tile([P, CHUNK * PACK], BF16, name="square", tag="square%d_%d" % (c, b), align_bytes=64)
+        def quantise_h(c, b, source, parts):
+            width = CHUNK // parts
+            for j0 in range(0, CHUNK, width):
+                cols = slice(c * CHUNK + j0, c * CHUNK + j0 + width)
+                nc.vector.quantize_mx(
+                    out=h_w[b][:, cols].bitcast(FP8X4),
+                    scales=h_s[b][:, cols],
+                    in_=source[:, j0 * PACK : (j0 + width) * PACK],
+                )
+
+        def square_and_sign(c, b):
+            square = tile([P, CHUNK * PACK], BF16, "square%d_%d" % (c, b))
             nc.scalar.activation(
                 square[:].rearrange("p (g i t) -> p g t i", t=PACK, i=LINE),
                 relus[(c, b)][:].rearrange("p t (g i) -> p g t i", i=LINE),
                 ACT.Square,
                 scale=0.5,
             )
-            signed = keep.tile([P, CHUNK * PACK], BF16, name="signed", tag="signed%d_%d" % (c, b), align_bytes=64)
-            sign = signs[b][:].rearrange("p c t -> p (c t)")
-            for j0 in (0, HALF):
-                part = slice(j0 * PACK, (j0 + HALF) * PACK)
-                nc.vector.tensor_tensor(signed[:, part], square[:, part], sign, ALU.mult)
-            for j0 in (0, HALF):
-                part = slice(j0 * PACK, (j0 + HALF) * PACK)
-                cols = slice(c * CHUNK + j0, c * CHUNK + j0 + HALF)
-                nc.vector.quantize_mx(out=h_w[b][:, cols].bitcast(FP8X4), scales=h_s[b][:, cols], in_=signed[:, part])
-
-        def quantise_signed_on_scalar(c, b):
-            square = keep.tile([P, PACK, CHUNK], BF16, name="square", tag="square%d_%d" % (c, b), align_bytes=64)
-            nc.scalar.activation(square[:], relus[(c, b)][:], ACT.Square, scale=0.5)
-            rows = keep.tile([P, PACK, CHUNK], BF16, name="rows", tag="rows%d_%d" % (c, b), align_bytes=64)
-            for t in range(PACK):
-                column = b * PACK + t
-                nc.scalar.activation(rows[:, t, :], square[:, t, :], ACT.Copy, scale=sign_column[:, column : column + 1])
-            signed = keep.tile([P, CHUNK * PACK], BF16, name="signed", tag="signed%d_%d" % (c, b), align_bytes=64)
-            nc.scalar.copy(
-                signed[:].rearrange("p (g i t) -> p g t i", t=PACK, i=LINE),
-                rows[:].rearrange("p t (g i) -> p g t i", i=LINE),
+            signed = tile([P, CHUNK * PACK], BF16, "signed%d_%d" % (c, b))
+            runs = CHUNK // SIGN_RUN
+            sign = signs[b][:].rearrange("p c t -> p (c t)").unsqueeze(1).to_broadcast([P, runs, SIGN_RUN * PACK])
+            nc.vector.tensor_tensor(
+                signed[:].rearrange("p (u v) -> p u v", u=runs),
+                square[:].rearrange("p (u v) -> p u v", u=runs),
+                sign,
+                ALU.mult,
             )
-            cols = slice(c * CHUNK, (c + 1) * CHUNK)
-            nc.vector.quantize_mx(out=h_w[b][:, cols].bitcast(FP8X4), scales=h_s[b][:, cols], in_=signed[:])
+            quantise_h(c, b, signed, 1)
 
-        def project(y, t, first, width):
-            acc = psum.tile([P, width], F32, name="acc_y", tag="bank%d" % (PACK + len(projected) % PACK))
-            projected.append(t)
-            narrow = width if width == BANK else P
-            for b in range(HB):
-                w8, w4, scale4, scale8 = dealt[(b, t)]
-                nc.tensor.matmul_mx(
-                    out=acc[:],
-                    lhsT=w8.bitcast(FP8X4),
-                    lhsT_scale=scale8,
-                    rhs=h_w[b][:, first : first + width].bitcast(FP8X4),
-                    rhs_scale=h_s[b][:, first : first + width],
-                    start=(b == 0),
-                    stop=False,
-                )
-                for j0 in range(0, width, narrow):
-                    nc.tensor.matmul_mx(
-                        out=acc[:, j0 : j0 + narrow],
-                        lhsT=w4.bitcast(FP4X4),
-                        lhsT_scale=scale4,
-                        rhs=h_w[b][:, first + j0 : first + j0 + narrow].bitcast(FP8X4),
-                        rhs_scale=h_s[b][:, first + j0 : first + j0 + narrow],
-                        start=False,
-                        stop=(b == HB - 1 and j0 + narrow == width),
-                    )
-            nc.scalar.copy(y, acc[:])
-
-        def put(tag, *pieces):
-            staged = keep.tile([P, sum(piece[2] for piece in pieces) * CHUNK], F32, name="y", tag=tag, align_bytes=64)
-            used = 0
-            for t, c, count in pieces:
-                first, width = c * CHUNK, count * CHUNK
-                y = staged[:, used : used + width]
-                for j0 in range(0, width, BANK):
-                    columns = min(BANK, width - j0)
-                    project(y[:, j0 : j0 + columns], t, first + j0, columns)
-                nc.vector.tensor_tensor(
-                    windows[t][:].indirect(entries(first, width)), y, wgo_t[:, first : first + width], ALU.mult
-                )
-                used = used + width
+        def put(t, c, count, tag, bank=None):
+            first, width = c * CHUNK, count * CHUNK
+            y = tile([P, width], F32, "y", tag)
+            for j0 in range(0, width, BANK):
+                columns = min(BANK, width - j0)
+                acc = psum.tile([P, columns], F32, name="acc_y", tag="bank%d" % (bank or PACK + len(projected) % PACK))
+                projected.append(t)
+                cols = slice(first + j0, first + j0 + columns)
+                for b in range(HB):
+                    scale4, scale8 = wd_s[(b, t)]
+                    for k, (words, scale) in enumerate(
+                        ((wd8_w[:, b, t, :].bitcast(FP8X4), scale8), (wd4_w[(b, t)].bitcast(FP4X4), scale4))
+                    ):
+                        nc.tensor.matmul_mx(
+                            out=acc[:],
+                            lhsT=words,
+                            lhsT_scale=scale,
+                            rhs=h_w[b][:, cols].bitcast(FP8X4),
+                            rhs_scale=h_s[b][:, cols],
+                            start=(b == 0 and k == 0),
+                            stop=(b == HB - 1 and k == 1),
+                        )
+                nc.scalar.copy(y[:, j0 : j0 + columns], acc[:])
+            nc.vector.tensor_tensor(
+                windows[t][:].indirect(entries(first, width)), y[:], wgo_t[:, first : first + width], ALU.mult
+            )
 
         def make_half_on_vector(c, b):
-            scaled = keep.tile([P, CHUNK * PACK], F32, name="scaled", tag="scaled", align_bytes=64)
-            rounded_h = keep.tile([P, CHUNK * PACK], BF16, name="rounded_h", tag="rounded_h", align_bytes=64)
+            scaled = tile([P, CHUNK * PACK], F32, "scaled")
+            rounded_h = tile([P, CHUNK * PACK], BF16, "rounded_h")
             factor = sm_t[:, b * PACK : (b + 1) * PACK].unsqueeze(1).to_broadcast([P, HALF, PACK])
             sums = []
             for j0 in (0, HALF):
-                acc = psum.tile([P, PACK, HALF], F32, name="acc_v", tag="bank%d" % (PACK + len(sums)))
+                acc = psum.tile([P, PACK, HALF], F32, name="acc_v", tag="bank%d" % (PACK + 2 + len(sums)))
                 for t in range(PACK):
-                    nc.tensor.matmul_mx(
-                        out=acc[:, t, :],
-                        lhsT=wu_w[b][:, t * P : (t + 1) * P].bitcast(FP8X4),
-                        lhsT_scale=wu_s[4 * b :, t * P : (t + 1) * P],
-                        rhs=picked[c][:, j0 : j0 + HALF].bitcast(FP8X4),
-                        rhs_scale=picked_s[c][:, j0 : j0 + HALF],
-                        start=True,
-                        stop=True,
-                    )
+                    first_product(acc[:, t, :], c, b, t, slice(j0, j0 + HALF))
                 sums.append(acc[:].rearrange("p t c -> p c t"))
             parts = [slice(j0 * PACK, (j0 + HALF) * PACK) for j0 in (0, HALF)]
             for a, part in zip(sums, parts):
@@ -296,58 +275,66 @@ def tile_list_modp_relu2_res_noneP_kernel(
                     ALU.max,
                     ALU.mult,
                 )
-            for j0, part in zip((0, HALF), parts):
-                cols = slice(c * CHUNK + j0, c * CHUNK + j0 + HALF)
-                nc.vector.quantize_mx(out=h_w[b][:, cols].bitcast(FP8X4), scales=h_s[b][:, cols], in_=rounded_h[:, part])
+            return rounded_h
 
+        deal_wd4(0, PACK, "wd4_w")
         rectify(0, 0)
-        make_half_on_vector(0, 1)
-        quantise(0, 0)
-        deal_wd(0, 1, ("square0_0", "relu0_0", "signed0_0"))
-        deal_wd(1, PACK - 1, ("rounded_h", "scaled", "g_first"))
+        rounded_h = make_half_on_vector(0, 1)
+        deal_wd_scales(0, 1, "scaled")
+        square_and_sign(0, 0)
+        quantise_h(0, 1, rounded_h, 1)
+        deal_wd_scales(1, PACK - 1, "rounded_h")
         rectify(1, 0)
-        quantise(1, 0)
-        rectify(1, 1, PACK)
-        put("y_first", (0, 0, 1))
-        quantise(1, 1)
+        square_and_sign(1, 0)
+        windows.append(tile([P, T], F32, "window3", "signed1_0"))
+        nc.gpsimd.memset(windows[3][:].bitcast(I32), 0)
+        put(0, 0, 1, "y0")
+        put(1, 0, 1, "y1")
+        rectify(1, 1)
+        square_and_sign(1, 1)
+        put(2, 0, 1, "relu1_1")
         rectify(2, 0)
-        put("relu1_1", (1, 0, 1), (0, 1, 1))
-        quantise(2, 0)
+        square_and_sign(2, 0)
+        put(3, 0, 1, "relu2_0")
         rectify(2, 1)
-        put("relu2_0", (2, 0, 1), (1, 1, 1))
-        quantise(2, 1)
+        put(0, 1, 1, "y2", PACK - 1)
+        square_and_sign(2, 1)
+        put(1, 1, 1, "relu2_1")
         rectify(3, 0)
-        put("relu2_1", (3, 0, 1), (2, 1, 1))
-        quantise_signed_on_scalar(3, 0)
+        square_and_sign(3, 0)
+        put(2, 1, 1, "relu3_0")
         rectify(3, 1)
-        put("relu3_0", (0, 2, 1))
-        quantise_signed_on_scalar(3, 1)
-        put("relu3_1", (1, 2, 1))
-        put("relu1_1", (0, 3, 1), (1, 3, 1))
-        put("relu2_0", (2, 2, 2))
-        put("relu3_0", (3, 1, 3))
+        put(0, 2, 1, "y3", PACK - 1)
+        square_and_sign(3, 1)
+        put(1, 2, 1, "relu3_1")
+        put(0, 3, 1, "y4")
+        put(1, 3, 1, "y5")
+        put(2, 2, 2, "y6")
+        put(3, 1, 2, "y7")
 
         rows = out_0.rearrange("(p t) c -> p t c", t=PACK)
         widths = TAIL_VECTOR + TAIL_SCALAR
         edges = [sum(widths[:i]) for i in range(len(widths))]
         by_vector = range(len(TAIL_VECTOR))
         by_scalar = range(len(TAIL_VECTOR), len(widths))
-        rounded = [keep.tile([P, PACK * w], BF16, name="rounded%d" % i, align_bytes=64) for i, w in enumerate(widths)]
-        grouped = [keep.tile([P, w * PACK], BF16, name="grouped%d" % i, align_bytes=64) for i, w in enumerate(widths)]
-        out_s = keep.tile([P, T], U8, name="out_s", align_bytes=64)
+        paired = [tile([P, PACK * w], BF16, "paired%d" % i) for i, w in enumerate(widths)]
+        grouped = [tile([P, w * PACK], BF16, "grouped%d" % i) for i, w in enumerate(widths)]
+        out_s = tile([P, T], U8, "out_s")
         words_out = out_1[0].rearrange("p t i -> p (t i)").bitcast(I32)
 
-        def round_plane(copy, t, i):
-            w = widths[i]
-            copy(rounded[i][:, t * w : (t + 1) * w], windows[t][:, edges[i] : edges[i] + w])
+        def round_pair(copy, t, i):
+            pairs = paired[i][:].rearrange("p (u c e) -> p u c e", u=2, e=2)
+            copy(pairs[:, t // 2, :, t % 2], windows[t][:, edges[i] : edges[i] + widths[i]])
 
-        def round_pair(t, i):
-            pairs = rounded[i][:].rearrange("p (u c e) -> p u c e", u=2, e=2)
-            nc.scalar.copy(pairs[:, t // 2, :, t % 2], windows[t][:, edges[i] : edges[i] + widths[i]])
+        def group(copy, dtype, i):
+            copy(
+                grouped[i][:].bitcast(dtype).rearrange("p (c u) -> p c u", u=2),
+                paired[i][:].bitcast(dtype).rearrange("p (u c) -> p c u", u=2),
+            )
 
         def finish(i):
             w = widths[i]
-            out_w = keep.tile([P, w], I32, name="out_w%d" % i, align_bytes=64)
+            out_w = tile([P, w], I32, "out_w%d" % i)
             done = 0
             while done < w:
                 columns = max(n for n in QUANTISE_WIDTHS if n <= w - done)
@@ -359,26 +346,22 @@ def tile_list_modp_relu2_res_noneP_kernel(
                 done = done + columns
             nc.sync.dma_start(words_out[:, edges[i] : edges[i] + w], out_w[:])
 
-        for t in range(PACK):
+        for t in range(PACK - 1):
             nc.sync.dma_start(rows[:, t, :], windows[t][:])
-            if t < PACK - 1:
-                for i in by_vector:
-                    round_plane(nc.scalar.copy, t, i)
-                for i in by_scalar:
-                    round_pair(t, i)
+            for i in by_vector:
+                round_pair(nc.scalar.copy, t, i)
+            if t == PACK - 2:
+                put(3, 3, 1, "y6")
+            for i in by_scalar:
+                round_pair(nc.scalar.copy, t, i)
+        nc.sync.dma_start(rows[:, PACK - 1, :], windows[PACK - 1][:])
         for i in by_vector:
-            round_plane(nc.vector.tensor_copy, PACK - 1, i)
+            round_pair(nc.vector.tensor_copy, PACK - 1, i)
         for i in by_vector:
-            nc.vector.tensor_copy(
-                grouped[i][:].rearrange("p (g i t) -> p g t i", t=PACK, i=LINE),
-                rounded[i][:].rearrange("p (t g i) -> p g t i", t=PACK, i=LINE),
-            )
+            group(nc.vector.tensor_copy, I32, i)
         for i in by_scalar:
-            round_pair(PACK - 1, i)
-            nc.scalar.copy(
-                grouped[i][:].bitcast(U32).rearrange("p (c u) -> p c u", u=2),
-                rounded[i][:].bitcast(U32).rearrange("p (u c) -> p c u", u=2),
-            )
+            round_pair(nc.scalar.copy, PACK - 1, i)
+            group(nc.scalar.copy, U32, i)
         for i in range(len(widths)):
             finish(i)
         for q in range(QUADRANTS):

@@ -27,8 +27,8 @@ CHUNK = 256
 CHUNKS = J // CHUNK
 HALF = CHUNK // 2
 QUANTISE_WIDTHS = (128, 256, 512)
-TAIL_VECTOR = (512, 512)
-TAIL_SCALAR = (512, 256, 256)
+TAIL_VECTOR = (640, 512)
+TAIL_SCALAR = (512, 256, 128)
 SIGN_RUN = 64
 TINY = 2.0 ** -100
 
@@ -141,6 +141,8 @@ def tile_list_modp_relu2_res_noneP_kernel(
                 sign_b[:], sm_t[:, b * PACK : (b + 1) * PACK].unsqueeze(1).to_broadcast([P, SIGN_RUN, PACK]), ACT.Sign
             )
             signs.append(sign_b)
+        sign_column = tile([P, HB * PACK], F32, "sign_column", "rinv")
+        nc.scalar.activation(sign_column[:], sm_t[:], ACT.Sign)
         deal_wu(1)
         gather_words(1, CHUNKS - 1, "wus_raw")
 
@@ -226,6 +228,20 @@ def tile_list_modp_relu2_res_noneP_kernel(
             )
             quantise_h(c, b, signed, 1)
 
+        def square_and_sign_on_scalar(c, b):
+            square = tile([P, PACK, CHUNK], BF16, "square%d_%d" % (c, b))
+            nc.scalar.activation(square[:], relus[(c, b)][:], ACT.Square, scale=0.5)
+            rows = tile([P, PACK, CHUNK], BF16, "rows%d_%d" % (c, b))
+            for t in range(PACK):
+                column = b * PACK + t
+                nc.scalar.activation(rows[:, t, :], square[:, t, :], ACT.Copy, scale=sign_column[:, column : column + 1])
+            signed = tile([P, CHUNK * PACK], BF16, "signed%d_%d" % (c, b))
+            nc.scalar.copy(
+                signed[:].rearrange("p (g i t) -> p g t i", t=PACK, i=LINE),
+                rows[:].rearrange("p t (g i) -> p g t i", i=LINE),
+            )
+            quantise_h(c, b, signed, 1)
+
         def put(t, c, count, tag, bank=None):
             first, width = c * CHUNK, count * CHUNK
             y = tile([P, width], F32, "y", tag)
@@ -280,33 +296,32 @@ def tile_list_modp_relu2_res_noneP_kernel(
         deal_wd4(0, PACK, "wd4_w")
         rectify(0, 0)
         rounded_h = make_half_on_vector(0, 1)
-        deal_wd_scales(0, 1, "scaled")
         square_and_sign(0, 0)
         quantise_h(0, 1, rounded_h, 1)
-        deal_wd_scales(1, PACK - 1, "rounded_h")
-        rectify(1, 0)
-        square_and_sign(1, 0)
-        windows.append(tile([P, T], F32, "window3", "signed1_0"))
+        rectify(1, 1)
+        rounded_h = make_half_on_vector(1, 0)
+        deal_wd_scales(0, PACK, "scaled")
+        square_and_sign(1, 1)
+        quantise_h(1, 0, rounded_h, 1)
+        windows.append(tile([P, T], F32, "window3", "rounded_h"))
         nc.gpsimd.memset(windows[3][:].bitcast(I32), 0)
+        rectify(2, 0)
         put(0, 0, 1, "y0")
         put(1, 0, 1, "y1")
-        rectify(1, 1)
-        square_and_sign(1, 1)
-        put(2, 0, 1, "relu1_1")
-        rectify(2, 0)
         square_and_sign(2, 0)
-        put(3, 0, 1, "relu2_0")
+        put(2, 0, 1, "relu2_0")
         rectify(2, 1)
-        put(0, 1, 1, "y2", PACK - 1)
+        put(0, 1, 1, "y2")
         square_and_sign(2, 1)
-        put(1, 1, 1, "relu2_1")
+        put(3, 0, 1, "relu2_1")
         rectify(3, 0)
-        square_and_sign(3, 0)
-        put(2, 1, 1, "relu3_0")
+        put(1, 1, 1, "y8")
+        square_and_sign_on_scalar(3, 0)
+        put(2, 1, 1, "rows3_0")
         rectify(3, 1)
         put(0, 2, 1, "y3", PACK - 1)
-        square_and_sign(3, 1)
-        put(1, 2, 1, "relu3_1")
+        square_and_sign_on_scalar(3, 1)
+        put(1, 2, 1, "rows3_1")
         put(0, 3, 1, "y4")
         put(1, 3, 1, "y5")
         put(2, 2, 2, "y6")
@@ -350,8 +365,11 @@ def tile_list_modp_relu2_res_noneP_kernel(
             nc.sync.dma_start(rows[:, t, :], windows[t][:])
             for i in by_vector:
                 round_pair(nc.scalar.copy, t, i)
-            if t == PACK - 2:
-                put(3, 3, 1, "y6")
+            if t == 0:
+                for i in by_scalar:
+                    round_pair(nc.scalar.copy, t, i)
+        put(3, 3, 1, "y6")
+        for t in range(1, PACK - 1):
             for i in by_scalar:
                 round_pair(nc.scalar.copy, t, i)
         nc.sync.dma_start(rows[:, PACK - 1, :], windows[PACK - 1][:])

@@ -146,12 +146,17 @@ def tile_list_modp_relu2_res_noneP_kernel(
         deal_wu(1)
         gather_words(1, CHUNKS - 1, "wus_raw")
 
-        wd8_w = tile([P, HB, PACK, P], I32, "wd8_w")
-        for b in range(HB):
+        wd8_w = []
+
+        def deal_wd8(b, tag):
+            w8 = tile([P, PACK, P], I32, "wd8_w", tag)
             nc.gpsimd.tensor_copy(
-                wd8_w[:, b, :, :].rearrange("p t (g i) -> p g t i", i=LINE),
+                w8[:].rearrange("p t (g i) -> p g t i", i=LINE),
                 wd8_raw[:, b * N : (b + 1) * N].rearrange("p (g i t) -> p g t i", i=LINE, t=PACK),
             )
+            wd8_w.append(w8)
+
+        deal_wd8(0, "wd8_w0")
         wd4_w, wd_s = {}, {}
 
         def deal_wd4(t0, count, tag):
@@ -253,7 +258,7 @@ def tile_list_modp_relu2_res_noneP_kernel(
                 for b in range(HB):
                     scale4, scale8 = wd_s[(b, t)]
                     for k, (words, scale) in enumerate(
-                        ((wd8_w[:, b, t, :].bitcast(FP8X4), scale8), (wd4_w[(b, t)].bitcast(FP4X4), scale4))
+                        ((wd8_w[b][:, t, :].bitcast(FP8X4), scale8), (wd4_w[(b, t)].bitcast(FP4X4), scale4))
                     ):
                         nc.tensor.matmul_mx(
                             out=acc[:],
@@ -298,6 +303,7 @@ def tile_list_modp_relu2_res_noneP_kernel(
         rounded_h = make_half_on_vector(0, 1)
         square_and_sign(0, 0)
         quantise_h(0, 1, rounded_h, 1)
+        deal_wd8(1, "signed0_0")
         rectify(1, 1)
         rounded_h = make_half_on_vector(1, 0)
         deal_wd_scales(0, PACK, "scaled")
@@ -383,5 +389,4 @@ def tile_list_modp_relu2_res_noneP_kernel(
         for i in range(len(widths)):
             finish(i)
         for q in range(QUADRANTS):
-            queue = nc.sync if q % 2 == 0 else nc.scalar
-            queue.dma_start(out_2[0, 4 * q : 4 * q + 4, :].bitcast(I32), out_s[32 * q : 32 * q + 4, :].bitcast(I32))
+            nc.sync.dma_start(out_2[0, 4 * q : 4 * q + 4, :].bitcast(I32), out_s[32 * q : 32 * q + 4, :].bitcast(I32))

@@ -42,7 +42,11 @@ def tile_list_modp_relu2_res_noneP_kernel(
         keep = ctx.enter_context(tc.tile_pool(name="keep", bufs=1))
         psum = ctx.enter_context(tc.psum_pool(name="psum", bufs=1))
 
+        laid = ctx.enter_context(tc.tile_pool(name="laid", bufs=1))
+
         def tile(shape, dtype, name, tag=None):
+            if isinstance(tag, int):
+                return laid.tile(shape, dtype, name=name, offset=tag, align_bytes=64)
             return keep.tile(shape, dtype, name=name, tag=tag or name, align_bytes=64)
 
         offsets = keep.tile([P, J // 16], U16, name="offsets")
@@ -131,7 +135,7 @@ def tile_list_modp_relu2_res_noneP_kernel(
                 root[:, column], mag[:, column], ACT.Identity, scale=rinv[:, column], bias=root0[:, column]
             )
         deal_wu(0)
-        nc.vector.tensor_copy(
+        nc.gpsimd.tensor_copy(
             wu_s[:].rearrange("p (t m) -> p t m", t=PACK), wus_raw[:].rearrange("p (m t) -> p t m", t=PACK)
         )
         signs = []
@@ -144,12 +148,14 @@ def tile_list_modp_relu2_res_noneP_kernel(
         sign_column = tile([P, HB * PACK], F32, "sign_column", "rinv")
         nc.scalar.activation(sign_column[:], sm_t[:], ACT.Sign)
         deal_wu(1)
-        gather_words(1, CHUNKS - 1, "wus_raw")
+        gather_words(1, CHUNKS - 1, "picked1")
+        windows.append(tile([P, T], F32, "window3", "wus_raw"))
+        nc.gpsimd.memset(windows[3][:].bitcast(I32), 0)
 
         wd8_w = []
 
         def deal_wd8(b, tag):
-            w8 = tile([P, PACK, P], I32, "wd8_w", tag)
+            w8 = tile([P, PACK, P], I32, "wd8_w%d" % b, tag)
             nc.gpsimd.tensor_copy(
                 w8[:].rearrange("p t (g i) -> p g t i", i=LINE),
                 wd8_raw[:, b * N : (b + 1) * N].rearrange("p (g i t) -> p g t i", i=LINE, t=PACK),
@@ -172,7 +178,7 @@ def tile_list_modp_relu2_res_noneP_kernel(
 
         def deal_wd_scales(t0, count, tag):
             ws = tile([P, HB, count, P], U8, "wd_s", tag)
-            nc.vector.tensor_copy(
+            nc.gpsimd.tensor_copy(
                 ws[:], wds_raw[:].rearrange("p (a m t) -> p a t m", a=HB, t=PACK)[:, :, t0 : t0 + count, :]
             )
             for i in range(count):
@@ -214,7 +220,7 @@ def tile_list_modp_relu2_res_noneP_kernel(
                     in_=source[:, j0 * PACK : (j0 + width) * PACK],
                 )
 
-        def square_and_sign(c, b):
+        def square_and_sign(c, b, tag=None):
             square = tile([P, CHUNK * PACK], BF16, "square%d_%d" % (c, b))
             nc.scalar.activation(
                 square[:].rearrange("p (g i t) -> p g t i", t=PACK, i=LINE),
@@ -222,7 +228,7 @@ def tile_list_modp_relu2_res_noneP_kernel(
                 ACT.Square,
                 scale=0.5,
             )
-            signed = tile([P, CHUNK * PACK], BF16, "signed%d_%d" % (c, b))
+            signed = tile([P, CHUNK * PACK], BF16, "signed%d_%d" % (c, b), tag)
             runs = CHUNK // SIGN_RUN
             sign = signs[b][:].rearrange("p c t -> p (c t)").unsqueeze(1).to_broadcast([P, runs, SIGN_RUN * PACK])
             nc.vector.tensor_tensor(
@@ -274,8 +280,8 @@ def tile_list_modp_relu2_res_noneP_kernel(
                 windows[t][:].indirect(entries(first, width)), y[:], wgo_t[:, first : first + width], ALU.mult
             )
 
-        def make_half_on_vector(c, b):
-            scaled = tile([P, CHUNK * PACK], F32, "scaled")
+        def make_half_on_vector(c, b, tag=None):
+            scaled = tile([P, CHUNK * PACK], F32, "scaled%d" % c, tag)
             rounded_h = tile([P, CHUNK * PACK], BF16, "rounded_h")
             factor = sm_t[:, b * PACK : (b + 1) * PACK].unsqueeze(1).to_broadcast([P, HALF, PACK])
             sums = []
@@ -301,16 +307,14 @@ def tile_list_modp_relu2_res_noneP_kernel(
         deal_wd4(0, PACK, "wd4_w")
         rectify(0, 0)
         rounded_h = make_half_on_vector(0, 1)
-        square_and_sign(0, 0)
+        square_and_sign(0, 0, 3072)
         quantise_h(0, 1, rounded_h, 1)
-        deal_wd8(1, "signed0_0")
+        deal_wd8(1, 4096)
+        deal_wd_scales(0, PACK, "wd8_raw")
         rectify(1, 1)
-        rounded_h = make_half_on_vector(1, 0)
-        deal_wd_scales(0, PACK, "scaled")
+        rounded_h = make_half_on_vector(1, 0, 0)
         square_and_sign(1, 1)
         quantise_h(1, 0, rounded_h, 1)
-        windows.append(tile([P, T], F32, "window3", "rounded_h"))
-        nc.gpsimd.memset(windows[3][:].bitcast(I32), 0)
         rectify(2, 0)
         put(0, 0, 1, "y0")
         put(1, 0, 1, "y1")
@@ -389,4 +393,5 @@ def tile_list_modp_relu2_res_noneP_kernel(
         for i in range(len(widths)):
             finish(i)
         for q in range(QUADRANTS):
-            nc.sync.dma_start(out_2[0, 4 * q : 4 * q + 4, :].bitcast(I32), out_s[32 * q : 32 * q + 4, :].bitcast(I32))
+            queue = nc.sync if q % 2 == 0 else nc.scalar
+            queue.dma_start(out_2[0, 4 * q : 4 * q + 4, :].bitcast(I32), out_s[32 * q : 32 * q + 4, :].bitcast(I32))

@@ -154,15 +154,16 @@ def tile_list_modp_relu2_res_noneP_kernel(
 
         wd8_w = []
 
-        def deal_wd8(b, tag):
-            w8 = tile([P, PACK, P], I32, "wd8_w%d" % b, tag)
+        def deal_wd8(b):
+            w8 = tile([P, PACK, P], I32, "wd8_w%d" % b)
             nc.gpsimd.tensor_copy(
                 w8[:].rearrange("p t (g i) -> p g t i", i=LINE),
                 wd8_raw[:, b * N : (b + 1) * N].rearrange("p (g i t) -> p g t i", i=LINE, t=PACK),
             )
             wd8_w.append(w8)
 
-        deal_wd8(0, "wd8_w0")
+        for b in range(HB):
+            deal_wd8(b)
         wd4_w, wd_s = {}, {}
 
         def deal_wd4(t0, count, tag):
@@ -309,8 +310,7 @@ def tile_list_modp_relu2_res_noneP_kernel(
         rounded_h = make_half_on_vector(0, 1)
         square_and_sign(0, 0, 3072)
         quantise_h(0, 1, rounded_h, 1)
-        deal_wd8(1, 4096)
-        deal_wd_scales(0, PACK, "wd8_raw")
+        deal_wd_scales(0, PACK, 4096)
         rectify(1, 1)
         rounded_h = make_half_on_vector(1, 0, 0)
         square_and_sign(1, 1)

from contextlib import ExitStack

import concourse.mybir as mybir

K, R, N, T, J = 512, 1024, 512, 2048, 1024
FLOPS = 2 * K * R * J + 2 * 2 * R * N * J

F32 = mybir.dt.float32
BF16 = mybir.dt.bfloat16
I32 = mybir.dt.int32
U32 = mybir.dt.uint32
U16 = mybir.dt.uint16
U8 = mybir.dt.uint8
FP8X4 = mybir.dt.float8_e4m3fn_x4
FP4X4 = mybir.dt.float4_e2m1fn_x4
ALU = mybir.AluOpType
ACT = mybir.ActivationFunctionType

P = 128
PACK = 4
PASS = P * PACK
HB = R // PASS
QUADRANTS = 4
LINE = 4
BANK = 512
CHUNK = 256
CHUNKS = J // CHUNK
HALF = CHUNK // 2
QUANTISE_WIDTHS = (128, 256, 512)
TAIL_VECTOR = (640, 512)
TAIL_SCALAR = (512, 256, 128)
SIGN_RUN = 64
TINY = 2.0 ** -100


def tile_list_modp_relu2_res_noneP_kernel(
    tc, tab_words, tab_scales, wu_words, wu_scales, sm, wd4_words, wd4_scales, wd8_words, wd8_scales, wgo, offs,
    out_0, out_1, out_2,
):
    nc = tc.nc
    with ExitStack() as ctx:
        keep = ctx.enter_context(tc.tile_pool(name="keep", bufs=1))
        psum = ctx.enter_context(tc.psum_pool(name="psum", bufs=1))

        laid = ctx.enter_context(tc.tile_pool(name="laid", bufs=1))

        def tile(shape, dtype, name, tag=None):
            if isinstance(tag, int):
                return laid.tile(shape, dtype, name=name, offset=tag, align_bytes=64)
            return keep.tile(shape, dtype, name=name, tag=tag or name, align_bytes=64)

        offsets = keep.tile([P, J // 16], U16, name="offsets")
        sm_t = tile([P, HB * PACK], F32, "sm_t")
        tab_w = tile([P, T], I32, "tab_w")
        tab_s = tile([P, T], U8, "tab_s")
        wu_raw = [tile([P, PASS], I32, "wu_raw%d" % b) for b in range(HB)]
        wus_raw = tile([P, PASS], U8, "wus_raw")
        wds_raw = tile([P, HB * N], U8, "wds_raw")
        wd8_raw = tile([P, HB * N], I32, "wd8_raw")
        wd4_raw = tile([P, HB * N // 2], I32, "wd4_raw")
        wgo_t = tile([P, J], F32, "wgo_t")

        nc.gpsimd.memset(tab_s[:].bitcast(I32), 0)
        nc.gpsimd.memset(wus_raw[:].bitcast(I32), 0)
        nc.gpsimd.memset(wds_raw[:].bitcast(I32), 0)

        nc.sync.dma_start(sm_t[:].rearrange("p (b t) -> p b t", t=PACK), sm.rearrange("(b p t) -> p b t", p=P, t=PACK))
        nc.sync.dma_start(offsets[:], offs)
        for q in range(QUADRANTS):
            nc.sync.dma_start(
                tab_s[32 * q : 32 * q + 4, :].bitcast(I32), tab_scales[0, 4 * q : 4 * q + 4, :].bitcast(I32)
            )
        wu_src = wu_words[0].rearrange("p r i -> p (r i)").bitcast(I32)
        nc.sync.dma_start(wu_raw[0][:], wu_src[:, :PASS])
        nc.sync.dma_start(tab_w[:], tab_words[0].rearrange("p t i -> p (t i)").bitcast(I32))
        for q in range(QUADRANTS):
            nc.sync.dma_start(
                wus_raw[32 * q : 32 * q + 4 * HB, :].bitcast(I32),
                wu_scales[0, 4 * q : 4 * q + 4, :].bitcast(I32).rearrange("r (b n) -> b r n", b=HB),
            )
        nc.sync.dma_start(wu_raw[1][:], wu_src[:, PASS:])
        nc.sync.dma_start(wd4_raw[:].rearrange("p (a n) -> p a n", a=HB), wd4_words.rearrange("a p n -> p a n").bitcast(I32))
        nc.sync.dma_start(
            wd8_raw[:].rearrange("p (a n) -> p a n", a=HB), wd8_words.rearrange("a p n i -> p a (n i)").bitcast(I32)
        )
        for base, scale_rows in ((0, wd4_scales), (4, wd8_scales)):
            for q in range(QUADRANTS):
                nc.sync.dma_start(
                    wds_raw[32 * q + base : 32 * q + base + 4, :].bitcast(I32).rearrange("r (a n) -> r a n", a=HB),
                    scale_rows[:, 4 * q : 4 * q + 4, :].bitcast(I32).rearrange("a r n -> r a n"),
                )
        nc.sync.dma_start(wgo_t[:], wgo)

        windows = [tile([P, T], F32, "window%d" % t) for t in range(PACK - 1)]
        nc.vector.memset(windows[0][:, : T - 1].bitcast(I32), 0)
        nc.vector.memset(windows[0][:, T - 1 :].bitcast(I32), 0)
        nc.gpsimd.memset(windows[1][:].bitcast(I32), 0)
        nc.gpsimd.memset(windows[2][:].bitcast(I32), 0)

        def entries(first, width):
            return offsets[:, first // 16 : (first + width) // 16]

        mag = tile([P, HB * PACK], F32, "mag", "sign0")
        root0 = tile([P, HB * PACK], F32, "root0", "sign1")
        rinv = tile([P, HB * PACK], F32, "rinv")
        root = tile([P, HB * PACK], F32, "root")
        nc.vector.scalar_tensor_tensor(mag[:], sm_t[:], -1.0, sm_t[:], ALU.mult, ALU.max)
        nc.scalar.activation(root0[:], mag[:], ACT.Sqrt, bias=TINY)
        nc.vector.reciprocal(rinv[:], root0[:])

        g_s = tile([P, J], U8, "g_s")
        nc.vector.tensor_copy(g_s[:], tab_s[:].indirect(offsets[:]))
        picked_s = [g_s[:, c * CHUNK : (c + 1) * CHUNK] for c in range(CHUNKS)]
        picked = []

        def gather_words(first, count, tag):
            g = tile([P, count * CHUNK], I32, "picked", tag)
            nc.vector.tensor_copy(g[:].bitcast(U32), tab_w[:].bitcast(U32).indirect(entries(first * CHUNK, count * CHUNK)))
            picked.extend(g[:, c * CHUNK : (c + 1) * CHUNK] for c in range(count))

        gather_words(0, 1, "picked0")

        wu_w = [tile([P, PASS], U32, "wu_w%d" % b) for b in range(HB)]
        wu_s = tile([P, PASS], U8, "wu_s")

        def deal_wu(b):
            nc.scalar.copy(
                wu_w[b][:].rearrange("p (t g i) -> p g t i", t=PACK, i=LINE),
                wu_raw[b][:].bitcast(U32).rearrange("p (g i t) -> p g t i", t=PACK, i=LINE),
            )

        for j in range(HB * PACK):
            column = slice(j, j + 1)
            nc.scalar.activation(
                root[:, column], mag[:, column], ACT.Identity, scale=rinv[:, column], bias=root0[:, column]
            )
        deal_wu(0)
        nc.gpsimd.tensor_copy(
            wu_s[:].rearrange("p (t m) -> p t m", t=PACK), wus_raw[:].rearrange("p (m t) -> p t m", t=PACK)
        )
        signs = []
        for b in range(HB):
            sign_b = tile([P, SIGN_RUN, PACK], BF16, "sign", "sign%d" % b)
            nc.scalar.activation(
                sign_b[:], sm_t[:, b * PACK : (b + 1) * PACK].unsqueeze(1).to_broadcast([P, SIGN_RUN, PACK]), ACT.Sign
            )
            signs.append(sign_b)
        sign_column = tile([P, HB * PACK], F32, "sign_column", "rinv")
        nc.scalar.activation(sign_column[:], sm_t[:], ACT.Sign)
        deal_wu(1)
        gather_words(1, CHUNKS - 1, "picked1")
        windows.append(tile([P, T], F32, "window3", "wus_raw"))
        nc.gpsimd.memset(windows[3][:].bitcast(I32), 0)

        wd8_w = []

        def deal_wd8(b):
            w8 = tile([P, PACK, P], I32, "wd8_w%d" % b)
            nc.gpsimd.tensor_copy(
                w8[:].rearrange("p t (g i) -> p g t i", i=LINE),
                wd8_raw[:, b * N : (b + 1) * N].rearrange("p (g i t) -> p g t i", i=LINE, t=PACK),
            )
            wd8_w.append(w8)

        for b in range(HB):
            deal_wd8(b)
        wd4_w, wd_s = {}, {}

        def deal_wd4(t0, count, tag):
            w4 = tile([P, HB * count * P * 2], U8, "wd4_w", tag)
            nc.scalar.copy(
                w4[:].bitcast(U16).rearrange("p (a t m) -> p a t m", a=HB, t=count),
                wd4_raw[:].bitcast(U16).rearrange("p (a m t) -> p a t m", a=HB, t=PACK)[:, :, t0 : t0 + count, :],
            )
            for i in range(count):
                for b in range(HB):
                    col = (b * count + i) * P
                    wd4_w[(b, t0 + i)] = w4[:, 2 * col : 2 * (col + P)]

        def deal_wd_scales(t0, count, tag):
            ws = tile([P, HB, count, P], U8, "wd_s", tag)
            nc.gpsimd.tensor_copy(
                ws[:], wds_raw[:].rearrange("p (a m t) -> p a t m", a=HB, t=PACK)[:, :, t0 : t0 + count, :]
            )
            for i in range(count):
                for b in range(HB):
                    wd_s[(b, t0 + i)] = (ws[:, b, i, :], ws[4:, b, i, :])

        h_w = [tile([P, J], U32, "h_w%d" % b) for b in range(HB)]
        h_s = [tile([P, J], U8, "h_s%d" % b) for b in range(HB)]
        relus = {}
        projected = []

        def first_product(acc, c, b, t, columns):
            nc.tensor.matmul_mx(
                out=acc,
                lhsT=wu_w[b][:, t * P : (t + 1) * P].bitcast(FP8X4),
                lhsT_scale=wu_s[4 * b :, t * P : (t + 1) * P],
                rhs=picked[c][:, columns].bitcast(FP8X4),
                rhs_scale=picked_s[c][:, columns],
                start=True,
                stop=True,
            )

        def rectify(c, b):
            relu = tile([P, PACK, CHUNK], F32, "relu%d_%d" % (c, b))
            for t in range(PACK):
                acc = psum.tile([P, CHUNK], F32, name="acc_a", tag="bank%d" % t)
                first_product(acc[:], c, b, t, slice(0, CHUNK))
                factor = root[:, b * PACK + t : b * PACK + t + 1]
                nc.scalar.activation(relu[:, t, :], acc[:], ACT.Relu, scale=factor)
            relus[(c, b)] = relu

        def quantise_h(c, b, source, parts):
            width = CHUNK // parts
            for j0 in range(0, CHUNK, width):
                cols = slice(c * CHUNK + j0, c * CHUNK + j0 + width)
                nc.vector.quantize_mx(
                    out=h_w[b][:, cols].bitcast(FP8X4),
                    scales=h_s[b][:, cols],
                    in_=source[:, j0 * PACK : (j0 + width) * PACK],
                )

        def square_and_sign(c, b, tag=None):
            square = tile([P, CHUNK * PACK], BF16, "square%d_%d" % (c, b))
            nc.scalar.activation(
                square[:].rearrange("p (g i t) -> p g t i", t=PACK, i=LINE),
                relus[(c, b)][:].rearrange("p t (g i) -> p g t i", i=LINE),
                ACT.Square,
                scale=0.5,
            )
            signed = tile([P, CHUNK * PACK], BF16, "signed%d_%d" % (c, b), tag)
            runs = CHUNK // SIGN_RUN
            sign = signs[b][:].rearrange("p c t -> p (c t)").unsqueeze(1).to_broadcast([P, runs, SIGN_RUN * PACK])
            nc.vector.tensor_tensor(
                signed[:].rearrange("p (u v) -> p u v", u=runs),
                square[:].rearrange("p (u v) -> p u v", u=runs),
                sign,
                ALU.mult,
            )
            quantise_h(c, b, signed, 1)

        def square_and_sign_on_scalar(c, b):
            square = tile([P, PACK, CHUNK], BF16, "square%d_%d" % (c, b))
            nc.scalar.activation(square[:], relus[(c, b)][:], ACT.Square, scale=0.5)
            rows = tile([P, PACK, CHUNK], BF16, "rows%d_%d" % (c, b))
            for t in range(PACK):
                column = b * PACK + t
                nc.scalar.activation(rows[:, t, :], square[:, t, :], ACT.Copy, scale=sign_column[:, column : column + 1])
            signed = tile([P, CHUNK * PACK], BF16, "signed%d_%d" % (c, b))
            nc.scalar.copy(
                signed[:].rearrange("p (g i t) -> p g t i", t=PACK, i=LINE),
                rows[:].rearrange("p t (g i) -> p g t i", i=LINE),
            )
            quantise_h(c, b, signed, 1)

        def put(t, c, count, tag, bank=None):
            first, width = c * CHUNK, count * CHUNK
            y = tile([P, width], F32, "y", tag)
            for j0 in range(0, width, BANK):
                columns = min(BANK, width - j0)
                acc = psum.tile([P, columns], F32, name="acc_y", tag="bank%d" % (bank or PACK + len(projected) % PACK))
                projected.append(t)
                cols = slice(first + j0, first + j0 + columns)
                for b in range(HB):
                    scale4, scale8 = wd_s[(b, t)]
                    for k, (words, scale) in enumerate(
                        ((wd8_w[b][:, t, :].bitcast(FP8X4), scale8), (wd4_w[(b, t)].bitcast(FP4X4), scale4))
                    ):
                        nc.tensor.matmul_mx(
                            out=acc[:],
                            lhsT=words,
                            lhsT_scale=scale,
                            rhs=h_w[b][:, cols].bitcast(FP8X4),
                            rhs_scale=h_s[b][:, cols],
                            start=(b == 0 and k == 0),
                            stop=(b == HB - 1 and k == 1),
                        )
                nc.scalar.copy(y[:, j0 : j0 + columns], acc[:])
            nc.vector.tensor_tensor(
                windows[t][:].indirect(entries(first, width)), y[:], wgo_t[:, first : first + width], ALU.mult
            )

        def make_half_on_vector(c, b, tag=None):
            scaled = tile([P, CHUNK * PACK], F32, "scaled%d" % c, tag)
            rounded_h = tile([P, CHUNK * PACK], BF16, "rounded_h")
            factor = sm_t[:, b * PACK : (b + 1) * PACK].unsqueeze(1).to_broadcast([P, HALF, PACK])
            sums = []
            for j0 in (0, HALF):
                acc = psum.tile([P, PACK, HALF], F32, name="acc_v", tag="bank%d" % (PACK + 2 + len(sums)))
                for t in range(PACK):
                    first_product(acc[:, t, :], c, b, t, slice(j0, j0 + HALF))
                sums.append(acc[:].rearrange("p t c -> p c t"))
            parts = [slice(j0 * PACK, (j0 + HALF) * PACK) for j0 in (0, HALF)]
            for a, part in zip(sums, parts):
                nc.vector.tensor_tensor(scaled[:, part].rearrange("p (c t) -> p c t", t=PACK), a, factor, ALU.mult)
            for a, part in zip(sums, parts):
                nc.vector.scalar_tensor_tensor(
                    rounded_h[:, part].rearrange("p (c t) -> p c t", t=PACK),
                    a,
                    0.0,
                    scaled[:, part].rearrange("p (c t) -> p c t", t=PACK),
                    ALU.max,
                    ALU.mult,
                )
            return rounded_h

        deal_wd4(0, PACK, "wd4_w")
        rectify(0, 0)
        rounded_h = make_half_on_vector(0, 1)
        square_and_sign(0, 0, 3072)
        quantise_h(0, 1, rounded_h, 1)
        deal_wd_scales(0, PACK, 4096)
        rectify(1, 1)
        rounded_h = make_half_on_vector(1, 0, 0)
        square_and_sign(1, 1)
        quantise_h(1, 0, rounded_h, 1)
        rectify(2, 0)
        put(0, 0, 1, "y0")
        put(1, 0, 1, "y1")
        square_and_sign(2, 0)
        put(2, 0, 1, "relu2_0")
        rectify(2, 1)
        put(0, 1, 1, "y2")
        square_and_sign(2, 1)
        put(3, 0, 1, "relu2_1")
        rectify(3, 0)
        put(1, 1, 1, "y8")
        square_and_sign_on_scalar(3, 0)
        put(2, 1, 1, "rows3_0")
        rectify(3, 1)
        put(0, 2, 1, "y3", PACK - 1)
        square_and_sign_on_scalar(3, 1)
        put(1, 2, 1, "rows3_1")
        put(0, 3, 1, "y4")
        put(1, 3, 1, "y5")
        put(2, 2, 2, "y6")
        put(3, 1, 2, "y7")

        rows = out_0.rearrange("(p t) c -> p t c", t=PACK)
        widths = TAIL_VECTOR + TAIL_SCALAR
        edges = [sum(widths[:i]) for i in range(len(widths))]
        by_vector = range(len(TAIL_VECTOR))
        by_scalar = range(len(TAIL_VECTOR), len(widths))
        paired = [tile([P, PACK * w], BF16, "paired%d" % i) for i, w in enumerate(widths)]
        grouped = [tile([P, w * PACK], BF16, "grouped%d" % i) for i, w in enumerate(widths)]
        out_s = tile([P, T], U8, "out_s")
        words_out = out_1[0].rearrange("p t i -> p (t i)").bitcast(I32)

        def round_pair(copy, t, i):
            pairs = paired[i][:].rearrange("p (u c e) -> p u c e", u=2, e=2)
            copy(pairs[:, t // 2, :, t % 2], windows[t][:, edges[i] : edges[i] + widths[i]])

        def group(copy, dtype, i):
            copy(
                grouped[i][:].bitcast(dtype).rearrange("p (c u) -> p c u", u=2),
                paired[i][:].bitcast(dtype).rearrange("p (u c) -> p c u", u=2),
            )

        def finish(i):
            w = widths[i]
            out_w = tile([P, w], I32, "out_w%d" % i)
            done = 0
            while done < w:
                columns = max(n for n in QUANTISE_WIDTHS if n <= w - done)
                nc.vector.quantize_mx(
                    out=out_w[:, done : done + columns].bitcast(FP8X4),
                    scales=out_s[:, edges[i] + done : edges[i] + done + columns],
                    in_=grouped[i][:, done * PACK : (done + columns) * PACK],
                )
                done = done + columns
            nc.sync.dma_start(words_out[:, edges[i] : edges[i] + w], out_w[:])

        for t in range(PACK - 1):
            nc.sync.dma_start(rows[:, t, :], windows[t][:])
            for i in by_vector:
                round_pair(nc.scalar.copy, t, i)
            if t == 0:
                for i in by_scalar:
                    round_pair(nc.scalar.copy, t, i)
        put(3, 3, 1, "y6")
        for t in range(1, PACK - 1):
            for i in by_scalar:
                round_pair(nc.scalar.copy, t, i)
        nc.sync.dma_start(rows[:, PACK - 1, :], windows[PACK - 1][:])
        for i in by_vector:
            round_pair(nc.vector.tensor_copy, PACK - 1, i)
        for i in by_vector:
            group(nc.vector.tensor_copy, I32, i)
        for i in by_scalar:
            round_pair(nc.scalar.copy, PACK - 1, i)
            group(nc.scalar.copy, U32, i)
        for i in range(len(widths)):
            finish(i)
        for q in range(QUADRANTS):
            queue = nc.sync if q % 2 == 0 else nc.scalar
            queue.dma_start(out_2[0, 4 * q : 4 * q + 4, :].bitcast(I32), out_s[32 * q : 32 * q + 4, :].bitcast(I32))
